import numpy as np, ml_dtypes
CORES = [242,247,114,119]
N = 4
BF = ml_dtypes.bfloat16
def gentries(a):
    return np.ascontiguousarray(a.reshape(8, 16, -1).transpose(0, 2, 1)).reshape(8, -1)
def gtable(e):
    e = np.asarray(e); return np.ascontiguousarray(e.reshape(8, -1, 16).transpose(0, 2, 1)).reshape(128, -1).astype(np.int32)
S, M, NA, RO = 128, 512, 1024, 4
W0 = M + (N - 1) * S; W = W0 + RO * S
def parts(rng):
    amp = rng.choice(np.array([255, 160, 96]), (1, 8, 1, 1))
    y = (rng.random((N, 8, 16, W0)) * (amp + 1)).astype(np.int64)
    l = rng.integers(0, W0, (N, 8, 16, NA)); c = rng.integers(0, NA, (N, 8, 16, M))
    f = np.where(rng.random((N, 8, W0)) < 0.3, rng.integers(0, W0, (N, 8, W0)), np.arange(W0))
    th = (amp[..., 0] * (4.6 + 2.2 * rng.random((N, 8, S)))).astype(np.int64)
    return y, l, c, f, th
def pack(y, l, c, f, th):
    return {"y0": np.ascontiguousarray(y.reshape(N, 128, W0)).astype(np.float32).astype(BF), "lk": np.ascontiguousarray(l.reshape(N, 128, NA)).astype(np.int32),
            "cl": np.ascontiguousarray(c.reshape(N, 128, M)).astype(np.int32), "fw0": np.stack([gtable(z) for z in f]), "th": np.ascontiguousarray(th).astype(np.int32)}
def uneven(rng, hi, *shape):
    z = rng.random(shape) ** 3; side = rng.random(shape[:2] + (1,) * (len(shape) - 2)) < 0.5
    return np.minimum((hi * np.where(side, z, 1 - z)).astype(np.int64), hi - 1)
def far(y, l, c, f):
    r4 = np.arange(N)[:, None, None, None]; g4 = np.arange(8)[None, :, None, None]; k4 = np.arange(16)[None, None, :, None]
    a = c[..., :S]; b = f[r4, g4, l[r4, g4, k4, a]].reshape(N, 8, 1, 16 * S); e = f[r4, g4, l[r4, g4, (k4 + 5) % 16, a]].reshape(N, 8, 1, 16 * S)
    z = ((np.take_along_axis(y, b, 3) + np.take_along_axis(y, e, 3)) >> 1).reshape(N, 8, 16, 16, S)
    return np.max(np.add.reduce(np.abs(z - y[..., :S][:, :, :, None, :]), axis=2), axis=2)
def setup_inputs(rng):
    return pack(*parts(rng))
def setup_inputs_spread(rng):
    y, l, c, f, th = parts(rng)
    y = np.minimum((np.exp2(8 * rng.random((N, 8, 1, W0))) * rng.random((N, 8, 16, W0))).astype(np.int64), 255)
    l = uneven(rng, W0, N, 8, 16, NA); c = uneven(rng, NA, N, 8, 16, M)
    f = np.where(rng.random((N, 8, W0)) < 0.5, uneven(rng, W0, N, 8, W0), f)
    th = np.minimum((4081 * rng.random((N, 8, S)) ** 3).astype(np.int64), 4080)
    return pack(y, l, c, f, th)
def setup_inputs_ends(rng):
    y, l, c, f, th = parts(rng)
    y = np.where(rng.random((N, 8, 1, W0)) < 0.6, 255 * rng.integers(0, 2, (N, 8, 1, W0)), 255 * rng.integers(0, 2, (N, 8, 16, W0)))
    y[..., 0] = 0; y[..., W0 - 1] = 255; y[..., S - 1] = 0
    l = np.where(rng.random(l.shape) < 0.72, (W0 - 1) * rng.integers(0, 2, l.shape), l)
    c = np.where(rng.random(c.shape) < 0.72, (NA - 1) * rng.integers(0, 2, c.shape), c)
    f = np.where(rng.random(f.shape) < 0.7, (W0 - 1) * rng.integers(0, 2, f.shape), rng.integers(0, W0, f.shape))
    f[..., 0] = 0; f[..., W0 - 1] = W0 - 1
    l[:, 1::2, :, 0] = 0; l[:, 1::2, :, NA - 1] = W0 - 1
    c[:, :, 0, S - 1] = 0; c[:, :, 14, S - 1] = 0; c[:, :, 2, S - 1] = NA - 1; c[:, :, 15, S - 1] = NA - 1
    th = 4080 * rng.integers(0, 2, (N, 8, S))
    near = np.maximum(far(y, l, c, f) - rng.choice(np.array([0, 0, 1, 1, 1, 2, 9, 15, 16]), th.shape), 0)
    th = np.where(rng.random(th.shape) < 0.28, near, th)
    th[..., S - 1] = 0; th[:, 1::4, S - 1] = 4079
    th[np.arange(N), 2 * rng.integers(0, 4, N)] = 4080
    return pack(y, l, c, f, th)
def setup_inputs_corners(rng):
    y, l, c, f, th = parts(rng); x = np.arange(W0)
    th = np.where(rng.random(th.shape) < 0.25, 4080 * rng.integers(0, 2, th.shape), th)
    for r in range(N):
        o = rng.permutation(8)
        for g in range(8):
            f[r, g] = (x, np.maximum(x - 1, 0), (x + 1) % W0, x ^ 1, x * 0, x * 0 + W0 - 1, rng.choice(np.array([0, M - 1, M, W0 - 1]), W0), W0 - 1 - x)[int(o[g])]
            j = int(rng.integers(0, 6)); h = int(rng.integers(0, 6))
            if o[g] == 0: j = 5; h = 1; th[r, g] = 0
            if o[g] == 2: th[r, g] = 4080
            if j == 0: l[r, g] = np.arange(NA) % M
            if j == 1: l[r, g] = rng.choice(np.array([0, M - 1, M, W0 - 1]), (16, NA))
            if j == 2: l[r, g] = rng.integers(M, W0, (16, NA))
            if j == 3: l[r, g] = rng.integers(0, M, (16, NA))
            if j == 4: l[r, g, 1::2] = W0 - 1
            if h == 0: c[r, g] = c[r, g, :1]
            if h == 1: c[r, g] = np.arange(M) % NA
            if h == 2: c[r, g] = rng.choice(np.array([0, NA - 1]), (16, M))
            if h == 3: c[r, g] = (np.arange(M)[None, :] * 7 + np.arange(16)[:, None]) % NA
    return pack(y, l, c, f, th)
def setup_inputs_crowd(rng):
    y, l, c, f, th = parts(rng); y = rng.integers(0, 8, y.shape); th = rng.integers(25, 60, th.shape); i = np.arange(S)
    for r in range(N):
        for g in range(8):
            m = (1, 1, 2, 2, 16, 16, 1, 1)[g]; o = rng.permutation(NA); a = o[:m]
            x = int(rng.integers(M - S, M)) if g % 4 < 2 else int(rng.integers(M, W0))
            if r == N - 1 and g > 5: x = W0 - 1
            y[r, g, :, x] = 255; f[r, g, x] = x; l[r, g][:, a] = x
            c[r, g][rng.integers(0, 16, S), i] = a[i % m]
            if g in (1, 3, 4, 6):
                e = int(rng.integers(0, S)); f[r, g, e] = e; l[r, g, :, o[m]] = e; c[r, g, :, e] = o[m]
    return pack(y, l, c, f, th)
def setup_inputs_ties(rng):
    y, l, c, f, th = parts(rng)
    step = rng.choice(np.array([1, 3]), (1, 8, 1)); low = np.array([0, 127, 200, 252, 0, 127, 200, 252])[rng.permutation(8)].reshape(1, 8, 1)
    o = rng.permutation(8); step[0, o[:2]] = 1
    y = low[..., None] + step[..., None] * rng.integers(0, 2, y.shape)
    th = step * rng.integers(0, 11, th.shape)
    for g in o[:2]:
        y[:, g, 0] = low[0, g, 0]; th[:, g] = 0
        for r in range(N):
            e = int(rng.integers(0, S)); b = int(rng.integers(0, NA))
            f[r, g, e] = e; l[r, g, :, b] = e; c[r, g, :, e] = b
    B = NA // RO
    for r in range(N):
        for j in (2, 3):
            g = int(o[j]); e = int(rng.integers(0, S)); h = int(rng.integers(0, 16)); x = int(rng.integers(40, 175)); d = int(rng.integers(4, 41))
            s = np.array([x, x, x + d, x - d, x + 2 * d]) if j == 2 else np.array([x, x + 1, x + 1 + d, x + 1, x + 1 + d])
            y[r, g, :, :RO * S] = rng.integers(0, 256, (16, 1)); y[r, g, h, :RO * S] = np.repeat(s[:RO], S); y[r, g, h, (RO - 1) * S + e] = s[RO]
            f[r, g, :RO * S] = np.arange(RO * S)
            for t in range(RO):
                c[r, g, :, t * S:(t + 1) * S] = rng.integers(t * B, (t + 1) * B, (16, S))
                l[r, g, :, t * B:(t + 1) * B] = (t + 1) * S + (e + rng.integers(1, S, (16, B))) % S if t < RO - 1 else t * S + e
            if j == 2: th[r, g] = (1 + r % (RO - 1)) * d - 1
            else:
                k = 1 + r % 3; th[r, g] = d - rng.integers(1, k + 1, S); th[r, g, rng.permutation(S)[:k]] = 0
    w = far(y, l, c, f); th[:, o[4:6]] = w[:, o[4:6]]; g = int(o[5])
    for r in range(N): th[r, g, np.argsort(-w[r, g])[:1 + r % 3]] -= 1
    return pack(y, l, c, f, np.maximum(th, 0))
def check_inputs(d):
    bad = []
    for k, lo, hi in (("y0", 0, 255), ("lk", 0, W0 - 1), ("cl", 0, NA - 1), ("fw0", 0, W0 - 1), ("th", 0, 4080)):
        z = np.asarray(d[k]).astype(np.float64)
        if not np.all((z >= lo) & (z <= hi)): bad.append("range of " + k)
        elif not np.all(z == np.floor(z)): bad.append("whole numbers in " + k)
    return bad
def at(z, k):
    return np.take_along_axis(z, k[:, :, None, :], 2)[:, :, 0]
def reference(y0, lk, cl, fw0, th):
    Y = np.zeros((N, 8, 16, W), np.int64); Y[..., :W0] = y0.astype(np.float32).astype(np.int64).reshape(N, 8, 16, W0)
    L = lk.astype(np.int64).reshape(N, 8, 16, NA)
    C = np.zeros((N, 8, 16, W), np.int64); C[..., :M] = cl.astype(np.int64).reshape(N, 8, 16, M)
    F = np.tile(np.arange(W), (N, 8, 1)); F[:, :, :W0] = np.stack([gentries(z) for z in fw0])
    lane = np.arange(S); v = np.tile(lane, (N, 8, 1)); A = np.zeros((N, 8), np.int64); lim = th.astype(np.int64).reshape(N, 8, S)
    rk = np.arange(N)[:, None, None]; gr = np.arange(8)[None, :, None]; row = np.arange(16)[None, None, :, None]
    rk4 = rk[..., None]; gr4 = gr[..., None]
    for t in range(RO):
        a = np.take_along_axis(C, v[:, :, None, :], 3)
        b = np.take_along_axis(L, a, 3); c = L[rk4, gr4, (row + 5) % 16, a]
        fb = F[rk4, gr4, b].reshape(N, 8, 1, 16 * S); fc = F[rk4, gr4, c].reshape(N, 8, 1, 16 * S)
        y = ((np.take_along_axis(Y, fb, 3) + np.take_along_axis(Y, fc, 3)) >> 1).reshape(N, 8, 16, 16, S)
        own = np.take_along_axis(Y, v[:, :, None, :], 3)
        D = np.add.reduce(np.abs(y - own[:, :, :, None, :]), axis=2)
        p = np.argmax(D, axis=2); q = np.argmin(D, axis=2)
        big = at(D, p) > lim + (A % 16)[:, :, None]
        ap = at(a, p); bp = at(b, p); bq = at(b, q)
        yp = np.take_along_axis(y, p[:, :, None, None, :], 3)[:, :, :, 0]; yq = np.take_along_axis(y, q[:, :, None, None, :], 3)[:, :, :, 0]
        n = W0 + t * S + lane; new = own + np.sign(yq - own); u = np.add.reduce(own, axis=2)
        Y[..., W0 + t * S:W0 + (t + 1) * S] = yp
        C[..., W0 + t * S:W0 + (t + 1) * S] = a
        C[rk, gr, p, v] = (ap + u + t + 1) % NA
        Y[rk4, gr4, row, v[:, :, None, :]] = new
        for r in range(N):
            for s in range(N - 1): Y[r, :, :, M + s * S:M + (s + 1) * S] = new[(r + 1 + s) % N]
        for i in range(S - 1, -1, -1):
            i0, i1 = np.nonzero(big[:, :, i])
            L[i0, i1, 1::2, ap[i0, i1, i]] = n[i]
        F[rk, gr, v] = np.where(big, F[rk, gr, v], F[rk, gr, bq])
        F = np.take_along_axis(F, F, 2)
        w = F[rk, gr, bp]
        v = np.where((w < M) | (w >= W0), w - w % S + lane, np.where(big, n, (v + S) % M))
        A = np.add.reduce(big.astype(np.int64), axis=2)
    return {"yo": Y.reshape(N, 128, W).astype(np.float32).astype(BF), "lo": L.reshape(N, 128, NA).astype(np.float32), "fo": np.stack([gtable(z) for z in F]).astype(np.float32)}

@@ -1,0 +1,551 @@
+from concourse.bass import DstId, RemoteDMATransfer
+from concourse.mybir import AluOpType, AxisListType, ActivationFunctionType
+
+RO = 4
+BIG = 262144.0
+MAG = 402653184.0
+F32, BF, I32, U16, F16 = "float32", "bfloat16", "int32", "uint16", "float16"
+
+SCRATCH = {}
+for _n, _c, _d in (
+        ("Y", 1408, BF), ("C", 1024, I32), ("LI", 1024, I32), ("L", 1152, F32), ("LO", 1152, F32),
+        ("FW", 56, I32), ("FL", 88, U16), ("FR0", 1536, F32), ("FR1", 1536, F32), ("W", 1408, BF), ("TH8", 128, I32),
+        ("THF", 128, F32), ("BT8", 128, F32), ("T4", 128, I32), ("NEW", 512, BF), ("LAND", 1536, BF),
+        ("a16", 128, U16), ("af", 128, F32), ("Lg", 2048, F16), ("bc16", 256, U16), ("bt", 128, F32),
+        ("xb", 2048, F32), ("y16", 2048, F16), ("dS", 2048, BF), ("dA", [8, 256], BF),
+        ("own", 128, BF), ("nown", 128, F16), ("u1", 128, F32), ("SC", 256, F32), ("hi", 16, F32), ("pkc", 16, F32),
+        ("of", 16, F32), ("po", 16, U16), ("pr", [3, 128], F16), ("nrm", 128, F16), ("sg", 128, BF),
+        ("l16", 16, U16), ("er", 128, F32), ("em", 128, F32), ("es", 128, F32), ("e16", 8, U16), ("fx", 128, F32),
+        ("wm", 128, F32), ("ws", 128, F32), ("w16", 8, U16),
+        ("lamA", 8, F32), ("ap16", 8, U16), ("DD", 1024, BF), ("DS", 1024, BF), ("LE", 128, F32), ("ODDN", 128, F32),
+        ("ODDO", 128, F32), ("um", 128, F32), ("cn", 128, I32), ("cm", 128, I32),
+        ("REF", 8, F32), ("NREF", 8, F32), ("thr", 8, F32), ("thr0", 8, F32), ("ar", 1, F32), ("arh", 1, F16), ("ai", 1, I32),
+        ("aj", 1, I32), ("ak", 1, F32), ("vB", 8, F32), ("v16", 8, U16), ("vf", 8, F32), ("vo", 8, F32), ("vq", 8, F32),
+        ("vp", 8, F32), ("vo16", 8, U16), ("t0", 8, F32), ("t1", 8, F32), ("t2", 8, F32), ("t3", 8, F32), ("t4", 8, F32),
+        ("lo16", 8, U16), ("al0", 8, F32), ("al1", 8, I32), ("al2", 8, I32), ("al3", 8, F32), ("al4", 8, F32), ("alt", 8, F32),
+        ("aln", 8, F32), ("wi", 8, I32), ("wB", 8, I32), ("gh", 8, F32), ("ng", 8, F32), ("x1", 8, F32), ("ga", 8, F32),
+        ("gb", 8, F32), ("FO", 88, F32), ("FOt", 88, F32), ("FOu", 88, F32),
+        ("T1", 128, I32), ("T1a", 128, I32), ("T2", 128, I32), ("T2a", 128, I32), ("M1", 2048, BF), ("I16", 128, F16),
+        ("If", 128, F32), ("BO", 128, F16), ("I5", 128, F16), ("E", 2048, F16), ("E5", 2048, F16), ("EF", 2048, F32),
+        ("OHf", 16, F32), ("Z32", 144, BF), ("Z1", 144, F16), ("zb", 512, BF), ("MK", 128, F32), ("MKH", 128, F32),
+        ("d0P", 128, F32), ("d0Q", 128, F32), ("d0S", 128, F32), ("d0D", 1024, BF), ("JR", 128, F32),
+        ("SMI", 64, I32), ("SMF", 64, F32), ("CL", 8, U16)):
+    SCRATCH[_n] = ("sbuf", [128] + (_c if isinstance(_c, list) else [_c]), _d)
+for _n in ("psb0", "psb1", "psd0", "psd1", "psd2", "psd3", "psk", "psm"):
+    SCRATCH[_n] = ("psum", [128, 512], F32)
+
+SEMAPHORES = ["dv", "ac", "pe", "gp"] + ["in%d" % i for i in range(6)] + ["out%d" % i for i in range(6)] + \
+             ["arr%d" % t for t in range(RO)] + ["snt%d" % t for t in range(RO)]
+
+
+def rank_program(g, core, T, topo):
+    rank = T.rank_of(core)
+    if rank is None:
+        return
+    cores = T.cores
+    add, sub, mul, mx, mn = AluOpType.add, AluOpType.subtract, AluOpType.mult, AluOpType.max, AluOpType.min
+    ge, gt, le, lt, eq, ne = (AluOpType.is_ge, AluOpType.is_gt, AluOpType.is_le, AluOpType.is_lt, AluOpType.is_equal,
+                              AluOpType.not_equal)
+    band, shr = AluOpType.bitwise_and, AluOpType.arith_shift_right
+    AF = ActivationFunctionType
+    queues = {"v": g.vector, "a": g.scalar, "p": g.tensor, "g": g, "s": g.sync}
+    semof = {"v": "dv", "a": "ac", "p": "pe", "g": "gp"}
+    count = {"dv": 0, "ac": 0, "pe": 0, "gp": 0}
+    known = {"v": {}, "a": {}, "p": {}, "g": {}, "s": {}}
+    log = {}
+    total = {}
+
+    def waits(e, reads, writes):
+        need = {}
+        for toks, wr in ((reads, False), (writes, True)):
+            for nm, lo, hi in toks:
+                ps = nm[:2] == "ps"
+                for ent in log.get(nm, []):
+                    if ps:
+                        if ent[3] == e:
+                            continue
+                    elif ent[1] <= lo or ent[0] >= hi or not (wr or ent[2]):
+                        continue
+                    if ent[4] not in need or need[ent[4]][0] < ent[5]:
+                        need[ent[4]] = (ent[5], ent[6])
+        for sem in sorted(need, key=lambda s: -len(need[s][1])):
+            val, clk = need[sem]
+            k = known[e]
+            if k.get(sem, 0) >= val:
+                continue
+            queues[e].wait_ge(T.sem[sem], val)
+            k[sem] = val
+            for s2 in clk:
+                if k.get(s2, 0) < clk[s2]:
+                    k[s2] = clk[s2]
+
+    def note(e, clk, reads, writes, sem, val):
+        for toks, wr in ((reads, False), (writes, True)):
+            for nm, lo, hi in toks:
+                ents = log.setdefault(nm, [])
+                if nm[:2] == "ps":
+                    ents[:] = []
+                elif wr:
+                    ents[:] = [x for x in ents if not (x[0] >= lo and x[1] <= hi)]
+                ents.append((lo, hi, wr, e, sem, val, clk))
+
+    def do(e, fn, reads, writes):
+        waits(e, reads, writes)
+        sem = semof[e]
+        count[sem] += 1
+        fn().then_inc(T.sem[sem], 1)
+        note(e, dict(known[e]), reads, writes, sem, count[sem])
+
+    def dma(e, out, in_, reads, writes, sem):
+        waits(e, reads, writes)
+        queues[e].dma_start(out=out, in_=in_).then_inc(T.sem[sem], 16)
+        total[sem] = 16
+        note("d", dict(known[e]), reads, writes, sem, 16)
+
+    def A(nm, lo=0, hi=None, st=1):
+        if hi is None:
+            hi = SCRATCH[nm][1][1]
+        ap = T[nm][:, lo:hi] if st == 1 else T[nm][:, lo:hi:st]
+        return (ap, [(nm, lo, hi)], [])
+
+    def A8(nm):
+        return (T[nm][0:8, :], [(nm, 0, 128)], [])
+
+    def PR(q):
+        return (T.pr[:, q, :], [("pr", q, q + 1)], [])
+
+    def ind(win, off):
+        return (win[0].indirect(off[0]), win[1], off[1])
+
+    def vcopy(o, x):
+        do("v", lambda: g.vector.tensor_copy(out=o[0], in_=x[0]), x[1] + x[2] + o[2], o[1])
+
+    def vtt(o, x, y, op):
+        do("v", lambda: g.vector.tensor_tensor(out=o[0], in0=x[0], in1=y[0], op=op), x[1] + x[2] + y[1] + o[2], o[1])
+
+    def vts(o, x, s1, op0, s2=None, op1=None):
+        rd = x[1] + x[2] + o[2]
+        a1, a2 = s1, s2
+        if isinstance(s1, tuple):
+            rd = rd + s1[1]
+            a1 = s1[0]
+        if isinstance(s2, tuple):
+            rd = rd + s2[1]
+            a2 = s2[0]
+        if op1 is None:
+            do("v", lambda: g.vector.tensor_scalar(out=o[0], in0=x[0], scalar1=a1, scalar2=None, op0=op0), rd, o[1])
+        else:
+            do("v", lambda: g.vector.tensor_scalar(out=o[0], in0=x[0], scalar1=a1, scalar2=a2, op0=op0, op1=op1), rd, o[1])
+
+    def vscan(o, d0, d1, op0, op1):
+        do("v", lambda: g.vector.tensor_tensor_scan(out=o[0], data0=d0[0], data1=d1[0], initial=0.0, op0=op0, op1=op1),
+           d0[1] + d1[1], o[1])
+
+    def vset(o, c):
+        do("v", lambda: g.vector.memset(o[0], c), [], o[1])
+
+    def act(o, x, f, bias=None, scale=None):
+        rd = x[1] + x[2]
+        kw = {}
+        for key, z in (("bias", bias), ("scale", scale)):
+            if isinstance(z, tuple):
+                rd = rd + z[1]
+                kw[key] = z[0]
+            elif z is not None:
+                kw[key] = z
+        do("a", lambda: g.scalar.activation(out=o[0], in_=x[0], func=f, **kw), rd, o[1])
+
+    def mms(bank, reads, jobs):
+        def fn():
+            last = None
+            for o, l, r, st, sp in jobs:
+                last = g.tensor.matmul(out=o, lhsT=l, rhs=r, start=st, stop=sp)
+            return last
+        do("p", fn, reads, [(bank, 0, 512)])
+
+    def iota(o, pattern, base, cmul, flag=False):
+        if flag:
+            do("g", lambda: g.iota(o[0], pattern=pattern, base=base, channel_multiplier=cmul,
+                                   allow_small_or_imprecise_dtypes=True), [], o[1])
+        else:
+            do("g", lambda: g.iota(o[0], pattern=pattern, base=base, channel_multiplier=cmul), [], o[1])
+
+    def fill(o, c, flag=True):
+        iota(o, [[0, o[1][0][2] - o[1][0][1]]], c, 0, flag)
+
+    def SF(j, n=1):
+        return A("SMF", j, j + n)
+
+    RC, EV, OD, LIc, K15, TRc, TD = SF(0), SF(1), SF(2), SF(8, 8), SF(16, 8), SF(24, 8), SF(32, 8)
+
+    dma("s", T.LI[:, :], T.lk[:, :], [], [("LI", 0, 1024)], "in0")
+    dma("a", T.C[:, 512:640], T.cl[:, 0:128], [], [("C", 512, 640)], "in1")
+    dma("a", T.FW[:, :], T.fw0[:, :], [], [("FW", 0, 56)], "in2")
+    dma("a", T.TH8[0:8, :], T.th[:, :], [], [("TH8", 0, 128)], "in5")
+    dma("s", T.Y[:, 512:1408], T.y0[:, :], [], [("Y", 512, 1408)], "in3")
+    dma("s", T.C[:, 640:1024], T.cl[:, 128:512], [], [("C", 640, 1024)], "in4")
+
+    iota(A("T1"), [[1, 128]], 128, -1)
+    iota(A("SMI", 0, 1), [[0, 1]], 0, 1)
+    iota(A("T2"), [[16, 8], [0, 16]], 15, -1)
+    iota(A("SMI", 32, 64), [[16, 32]], 0, 0)
+    iota(A("SMI", 16, 24), [[1, 8]], 0, 0)
+    iota(A8("T4"), [[1, 128]], 0, -16)
+    fill(A("zb"), 0)
+    iota(A("JR"), [[1, 128]], 0, 0, True)
+    fill(A("Y", 0, 512), 0)
+    fill(A("Z32"), 0)
+    fill(A("d0P"), 1)
+    fill(A("d0Q"), -1)
+    fill(A("W", 0, 512), 0)
+    fill(A("d0S"), 1)
+    fill(A("vB"), 512)
+    iota(A("FR1", 128, 1536), [[1, 1408]], 0, 0, True)
+    iota(A("FR0", 128, 640), [[1, 512]], 0, 0, True)
+    fill(A("C", 0, 512), 0, False)
+
+    vts(A("T1a"), A("T1"), 15, band)
+    vts(A("If"), A("T1"), 128, eq)
+    vts(A("M1", 0, 128), A("T1a"), 0, eq)
+    vts(A("I16"), A("T1"), 128, eq)
+    vcopy(A("OHf"), A("M1", 0, 16))
+    vcopy(A("M1", 128, 256), A("M1", 0, 128))
+    vts(A("SMI", 1, 2), A("SMI", 0, 1), 15, band)
+    vts(A("SMI", 2, 3), A("SMI", 0, 1), 1, band)
+    vts(A("T2a"), A("T2"), 4, shr)
+    vcopy(RC, A("SMI", 1, 2))
+    vcopy(OD, A("SMI", 2, 3))
+    vts(A("BO"), A("T2a"), 0, eq)
+    vts(A("FL", 0, 32), A("SMI", 32, 64), RC, add)
+    vts(LIc, A("SMI", 32, 40), RC, add)
+    for k in range(16):
+        vts(A("E", 128 * k, 128 * k + 128), A("I16"), A("M1", k, k + 1), mul)
+    vtt(A("I5"), A("M1", 5, 133), A("BO"), mul)
+    vts(A("FL", 32, 88), A("FW"), 512, add)
+    vts(A("v16"), A("SMI", 32, 40), RC, add, 512, add)
+    vcopy(A("a16"), A("C", 512, 640))
+    for k in range(16):
+        z = (k + 5) % 16
+        vts(A("E5", 128 * k, 128 * k + 128), A("I5"), A("M1", z, z + 1), mul)
+
+    act(A("MK"), A("M1", 0, 128), AF.Copy)
+    act(A("MKH"), A("M1", 0, 128), AF.Copy, scale=0.5)
+    for j in (256, 512, 1024):
+        act(A("M1", j, 2 * j), A("M1", 0, j), AF.Copy)
+    for k in range(16):
+        act(A("EF", 128 * k, 128 * k + 128), A("If"), AF.Copy, scale=A("OHf", k, k + 1))
+    for j in (0, 512):
+        act(A("d0D", j, j + 512), A("zb"), AF.Copy, bias=-1.0 / 256)
+    act(TRc, LIc, AF.Copy, bias=1024.0)
+    act(TD, LIc, AF.Copy, scale=1.0 / 256, bias=-127.0 / 256)
+    for o, z in ((SF(3), -512.0), (SF(4), 896.0), (SF(5), 128.0)):
+        act(o, OD, AF.Copy, scale=z)
+    act(EV, OD, AF.Copy, scale=-1.0, bias=1.0)
+    act(A("ODDN"), A("JR"), AF.Identity, scale=OD, bias=SF(3))
+    act(A("ODDO"), A("JR"), AF.Identity, scale=OD, bias=SF(4))
+    act(A("own"), ind(A("Y", 0, 1024), A("v16")), AF.Copy)
+    act(A("W", 512, 1408), ind(A("Y"), A("FL", 32, 88)), AF.Copy, scale=0.5)
+
+    vcopy(A("Z32", 16, 144, 16), A("BO", 0, 128, 16))
+    vcopy(A("Z1"), A("Z32"))
+    vts(A("Z32", 16, 144, 16), A("BO", 0, 128, 16), 32.0, mul)
+    vset(A("d0P", 0, 128, 16), -BIG)
+    vset(A("d0Q", 0, 128, 16), BIG)
+    vts(K15, LIc, 16.0, mul, 15.0, add)
+
+    def to_list(bank, o, src, q):
+        return [(T[bank][:, o:o + 8 * q], T.Z1[:, 16 - r:144 - r], src(r), r == 0, r == 15) for r in range(16)]
+
+    FRc, FRn = "FR0", "FR1"
+    for t in range(RO):
+        last = t == RO - 1
+
+        def gather_links(q):
+            src = A("LI") if t == 0 else A("L", 0, 1024)
+            vcopy(A("Lg", 512 * q, 512 * q + 512), ind(src, A("a16", 32 * q, 32 * q + 32)))
+
+        def list_at(h, z):
+            return ("psm", 400) if h and z else ("psb%d" % h, z)
+
+        def lists(h):
+            for z, nm in ((0, "E"), (64, "E5")):
+                bank, o = list_at(h, z)
+                mms(bank, [(nm, 0, 2048), ("Lg", 1024 * h, 1024 * h + 1024)],
+                    [(T[bank][:, o:o + 64], T[nm][:, 128 * k:128 * k + 128], T.Lg[:, 1024 * h + k:1024 * h + 1024:16],
+                      k == 0, k == 15) for k in range(16)])
+
+        def lists_out(h, z):
+            bank, o = list_at(h, z)
+            vts(A("bc16", 128 * h + z, 128 * h + z + 64), A(bank, o, o + 64), 512.0, add)
+
+        def own_in(n):
+            ps = T["psd%d" % n]
+            mms("psd%d" % n, [("I16", 0, 128), ("nown", 0, 128)],
+                [(ps[:, k:512:16], T.I16[:, :], T.nown[:, 32 * n:32 * n + 32], k == 0, False) for k in range(16)])
+
+        def blend_b(n):
+            o = 128 * (n // 2) + 32 * (n % 2)
+            act(A("xb", 512 * n, 512 * n + 512), ind(A("W"), A("bc16", o, o + 32)), AF.Copy, bias=1087.75)
+
+        def blend_c(n):
+            o = 128 * (n // 2) + 64 + 32 * (n % 2)
+            vtt(A("y16", 512 * n, 512 * n + 512), ind(A("W"), A("bc16", o, o + 32)), A("xb", 512 * n, 512 * n + 512), add)
+            mms("psd%d" % n, [("I16", 0, 128), ("y16", 512 * n, 512 * n + 512)],
+                [(T["psd%d" % n][:, :], T.I16[:, :], T.y16[:, 512 * n:512 * n + 512], False, True)])
+
+        def size_d(n):
+            act((T.dA[:, 2 * n:2 * n + 2, :], [("dA", 2 * n, 2 * n + 2)], []), A("psd%d" % n), AF.Abs)
+
+        def keep_d(n):
+            vcopy(A("dS", 512 * n, 512 * n + 512), A("psd%d" % n))
+
+        def sum_d(h):
+            bank = "psb1" if h else "psk"
+            mms(bank, [("Z32", 0, 144), ("dA", 4 * h, 4 * h + 4)],
+                [(T[bank][:, 0:64], T.Z32[:, 16 - r:144 - r], T.dA[:, 4 * h:4 * h + 4, 16 * r:16 * r + 16], r == 0, r == 15)
+                 for r in range(16)])
+
+        def scans(h):
+            bank, o = ("psb1" if h else "psk"), 64 * h
+            vscan(A("SC", o, o + 64), A("d0P", o, o + 64), A(bank, 0, 64), add, mx)
+            vscan(A("SC", 128 + o, 192 + o), A("d0Q", o, o + 64), A(bank, 0, 64), add, mn)
+
+        def room():
+            vtt(A("Y", 128 * t, 128 * t + 128), ind(A("dS"), P), A("own"), add)
+
+        def fix():
+            vcopy(ind(A(FRn, 0, 1536), A("vo16")), A("fx"))
+            lo = 640 if t == 0 else 128
+            mms("psm", [("EF", 0, 2048), (FRn, 128, 1536)],
+                [(T.psm[:, 0:(1536 - lo) // 16], T.EF[:, 128 * r:128 * r + 128], T[FRn][:, lo + r:1536:16], r == 0, r == 15)
+                 for r in range(16)])
+
+        gather_links(0)
+        vts(A("nown"), A("own"), -1.0, mul, -1088.0, add)
+        gather_links(1)
+        if t == 0:
+            vts(A8("T4"), A8("T4"), 4, shr)
+            vset(A("d0S", 0, 128, 16), 0.0)
+            vcopy(A("CL"), A("SMI", 16, 24))
+            vts(A8("BT8"), A8("T4"), 0, eq)
+        else:
+            vcopy(A("FL", 32 if t == 1 else 0, 88), A("psm", 0, 56 if t == 1 else 88))
+        lists(0)
+        own_in(0)
+        gather_links(2)
+        if t > 0:
+            do("v", lambda: g.vector.tensor_reduce(out=T.ar[:, :], in_=T.REF[:, :], axis=AxisListType.X, op=add),
+               [("REF", 0, 8)], [("ar", 0, 1)])
+        vcopy(A("af"), A("a16"))
+        if t > 0:
+            vcopy(A("arh"), A("ar"))
+            act(A("Y", 1024, 1408), A("LAND", 384 * t - 384, 384 * t), AF.Copy)
+            act(A("W", 512, 1408), ind(A("Y"), A("FL", 32, 88)), AF.Copy, scale=0.5)
+            act(A("W", 0, 128 * t), ind(A("Y"), A("FL", 0, 8 * t)), AF.Copy, scale=0.5)
+        lists_out(0, 0)
+        lists_out(0, 64)
+        gather_links(3)
+        lists(1)
+        vts(A("al0"), A("vB"), 512.0, ge, 128.0, mul)
+        if t == 0:
+            vcopy(A("L", 0, 1024), A("LI"))
+            vcopy(A8("THF"), A8("TH8"))
+            mms("psk", [("BT8", 0, 128), ("THF", 0, 128)], [(T.psk[:, 128:256], T.BT8[0:8, :], T.THF[0:8, :], True, True)])
+        else:
+            vtt(ind(A("LO", 0, 1152), A("lo16")), A("LE"), A("ODDO"), add)
+        lists_out(1, 0)
+        blend_b(0)
+        own_in(1)
+        blend_b(1)
+        blend_c(0)
+        lists_out(1, 64)
+        if t == 0:
+            vtt(A("em"), A("psk", 128, 256), A("MK"), mul)
+        blend_b(2)
+        blend_b(3)
+        own_in(2)
+        blend_c(1)
+        if t == 0:
+            vscan(A("es"), A("d0S"), A("em"), mul, add)
+        size_d(0)
+        own_in(3)
+        blend_c(2)
+        if t == 0:
+            vts(A("thr0"), A("es", 15, 128, 16), 32.0, mul, 15.0, add)
+        size_d(1)
+        blend_c(3)
+        vts(A("vp"), A("vB"), 128.0, add)
+        if t == 0:
+            vcopy(A("thr"), A("thr0"))
+            vset(A("d0D", 0, 1024, 128), 2048.0)
+        mms("psm", [("BO", 0, 128), ("nown", 0, 128)], [(T.psm[:, 256:384], T.BO[:, :], T.nown[:, :], True, True)])
+        if t > 0:
+            mms("psm", [("BO", 0, 128), ("arh", 0, 1)], [(T.psm[:, 500:501], T.BO[:, :], T.arh[:, :], True, True)])
+        size_d(2)
+        sum_d(0)
+        keep_d(0)
+        keep_d(1)
+        size_d(3)
+        act(A("dS", 1536, 2048), A("psd3"), AF.Copy)
+        sum_d(1)
+        if t > 0:
+            vcopy(A("ai"), A("psm", 500, 501))
+        vcopy(A("bt", 0, 64), A("bc16", 0, 64))
+        keep_d(2)
+        if t > 0:
+            vts(A("aj"), A("ai"), 15, band)
+        scans(0)
+        if t > 0:
+            vts(A("ak"), A("aj"), 32.0, mul)
+        vcopy(A("bt", 64, 128), A("bc16", 128, 192))
+        if t > 0:
+            vts(A("thr"), A("thr0"), A("ak"), add)
+        if t == 0:
+            act(A("FR0", 640, 1536), ind(A("FR1", 128, 1536), A("FL", 32, 88)), AF.Copy)
+
+        scans(1)
+        vtt(A("al1"), A("vB"), A("al0"), add)
+        vts(A("hi"), A("SC", 15, 256, 16), MAG, add, MAG, sub)
+        vtt(A("pkc", 0, 8), K15, A("SC", 15, 128, 16), sub)
+        vtt(A("pkc", 8, 16), K15, A("SC", 143, 256, 16), add)
+        vts(A("al2"), A("al1"), 384, band)
+        vtt(A("of", 0, 8), A("pkc", 0, 8), A("hi", 0, 8), add)
+        vtt(A("of", 8, 16), A("pkc", 8, 16), A("hi", 8, 16), sub)
+        vtt(A("NREF"), A("SC", 15, 128, 16), A("thr"), le)
+        vcopy(A("po"), A("of"))
+        vtt(A("REF"), A("SC", 15, 128, 16), A("thr"), gt)
+        P, Q = A("po", 0, 8), A("po", 8, 16)
+        act(A("sg"), ind(A("dS"), Q), AF.Sign)
+        if not last:
+            act(A("u1"), A("psm", 256, 384), AF.Identity, scale=-1.0, bias=float(t + 1 - 17408))
+        if t > 0:
+            act(A("ODDN"), A("ODDN"), AF.Identity, bias=SF(5))
+            act(A("ODDO"), A("ODDO"), AF.Identity, bias=SF(5))
+        vtt(A("vo"), A("vp"), A("NREF"), mul)
+        vtt(PR(0), ind(A("M1"), Q), A("bt"), mul)
+        vtt(PR(1), ind(A("M1"), P), A("bt"), mul)
+        mms("psb0", [("Z1", 0, 144), ("pr", 0, 2)], to_list("psb0", 0, lambda r: T.pr[:, 0:2, r:128:16], 2))
+        vtt(A("vq"), A("vo"), LIc, add)
+        vtt(PR(2), ind(A("M1"), P), A("af"), mul)
+        vtt(A("nrm"), ind(A("NREF"), A("CL")), A("MKH"), mul)
+        mms("psk", [("Z1", 0, 144), ("pr", 2, 3)], to_list("psk", 256, lambda r: T.pr[:, 2, r:128:16], 1))
+        for nm in ("psd0", "psd1") if last else ("psd0",):
+            mms(nm, [("BO", 0, 128), ("pr", 2, 3), ("nrm", 0, 128)],
+                [(T[nm][:, 0:128], T.BO[:, :], T.pr[:, 2, :], True, False), (T[nm][:, 0:128], T.BO[:, :], T.nrm[:, :], False, True)])
+        vcopy(A("vo16"), A("vq"))
+        nw = A("NEW", 128 * t, 128 * t + 128)
+        vtt(nw, A("own"), A("sg"), add)
+        waits("g", nw[1], [])
+        used, transfers = set(), []
+        others = sorted([c for c in cores if c != core], key=lambda c: len(topo.engines(core, c)))
+        for c in others:
+            fewest = topo.engines(core, others[0])
+            eng = [e for e in topo.engines(core, c) if e not in used]
+            if len(topo.engines(core, c)) > len(fewest):
+                eng = [e for e in eng if e not in fewest]
+            eng = eng[:4]
+            used.update(eng)
+            s = (rank - T.rank_of(c) - 1) % len(cores)
+            rid, pid = topo.addr(c, core)
+            transfers.append(RemoteDMATransfer(dst_ids=[DstId(rid=rid, pnc=pid)], dma_engine_mask=sum(1 << e for e in eng),
+                                               remote_sem=T.sem["arr%d" % t], src=nw[0],
+                                               dst=T.LAND[:, 384 * t + 128 * s:384 * t + 128 * s + 128]))
+        g.remote_dma_fused(transfers, local_sem=T.sem["snt%d" % t])
+        total["arr%d" % t] = 12
+        total["snt%d" % t] = 12
+        note("r", {}, [], [("LAND", 384 * t, 384 * t + 384)], "arr%d" % t, 12)
+
+        vts(A("al3"), A("al2"), 512.0, add)
+        vcopy(A("l16"), A("psb0", 0, 16))
+        if not last:
+            vts(A("al4"), A("REF"), float(128 * t), mul)
+        vcopy(A("er"), ind(A(FRc, 128, 1536), A("l16", 0, 8)))
+        if not last:
+            vcopy(A("C", 128 * t, 128 * t + 128), A("a16"))
+            vtt(A("alt"), A("al3"), A("NREF"), mul)
+        act(A("lamA"), A("psk", 256, 264), AF.Copy)
+        vcopy(ind(A(FRc, 0, 1536), A("vo16")), A("er"))
+        if not last:
+            mms("psb1", [("EF", 0, 2048), ("er", 0, 128)],
+                [(T.psb1[:, 384:392], T.EF[:, 128 * r:128 * r + 128], T.er[:, r:128:16], r == 0, r == 15) for r in range(16)])
+        vcopy(A("ap16"), A("psk", 256, 264))
+        if not last:
+            vtt(A("aln"), A("alt"), A("al4"), add)
+        for c in range(4 if last else 8):
+            act(A("DD", 128 * c, 128 * c + 128), A("psd0", 0, 128), AF.Abs, scale=-1.0, bias=A("lamA", c, c + 1))
+        act(A("LE"), ind(A("L", 0, 1024), A("ap16")), AF.Copy, scale=EV)
+        act(A(FRn, 640, 1536), ind(A(FRc, 128, 1536), A("FL", 32, 88)), AF.Copy)
+        if t > 0:
+            act(A(FRn, 128, 128 + 128 * t), ind(A(FRc, 128, 1536), A("FL", 0, 8 * t)), AF.Copy)
+        if not last:
+            vtt(A("wm"), ind(A(FRc, 128, 1536), A("l16", 8, 16)), A("MK"), mul)
+            vtt(A("t0"), A("lamA"), TRc, sub)
+            vscan(A("ws"), A("d0S"), A("wm"), mul, add)
+            vtt(A("t1"), A("t0"), A("REF"), mul)
+            vcopy(A("w16"), A("ws", 15, 128, 16))
+            vtt(A("em"), ind(A(FRc, 128, 1536), A("w16")), A("MK"), mul)
+            vscan(A("es"), A("d0S"), A("em"), mul, add)
+            vtt(A("um"), ind(A("M1"), P), A("u1"), mul)
+            vcopy(A("wi"), A("es", 15, 128, 16))
+            vts(A("gh"), A("es", 15, 128, 16), 1024.0, ge)
+            vts(A("ng"), A("es", 15, 128, 16), 1024.0, lt)
+            vts(A("wB"), A("wi"), 1920, band)
+            vtt(A("cn"), A("um"), A("af"), add)
+            vtt(A("x1"), A("wB"), A("ng"), mul)
+            vts(A("cm"), A("cn"), 1023, band)
+            vtt(A("ga"), A("gh"), A("aln"), mul)
+            vcopy(ind(A("C"), A("v16")), A("cm"))
+            vtt(A("gb"), A("ga"), LIc, add)
+            vcopy(A("e16"), A("psb1", 384, 392))
+        else:
+            vtt(A("em"), A("er"), A("MK"), mul)
+            vtt(A("t0"), A("lamA"), TRc, sub)
+            vscan(A("es"), A("d0S"), A("em"), mul, add)
+            vtt(A("t1"), A("t0"), A("REF"), mul)
+            vcopy(A("e16"), A("es", 15, 128, 16))
+            for c in range(4, 8):
+                vts(A("DD", 128 * c, 128 * c + 128), A("psd1", 0, 128), A("lamA", c, c + 1), ne)
+            room()
+        act(A("fx"), ind(A(FRc, 128, 1536), A("e16")), AF.Copy)
+        if t == 0:
+            act(A("LO", 0, 1024), A("L", 0, 1024), AF.Copy)
+            dma("s", T.lo[0:128:2, :], T.LO[0:128:2, 0:1024], [("LO", 0, 1024)], [], "out0")
+        vscan(A("DS"), A("d0D"), A("DD"), add, mn)
+        if not last:
+            vtt(A("vf"), A("x1"), A("gb"), add)
+        vtt(A("t2"), A("DS", 127, 1024, 128), TD, ge)
+        if not last:
+            vtt(A("vB"), A("x1"), A("ga"), add)
+            fix()
+        vtt(A("t3"), A("t2"), A("t1"), mul)
+        if not last:
+            room()
+        vtt(A("t4"), A("t3"), TRc, add)
+        if not last:
+            vcopy(ind(A("Y", 0, 1024), A("v16")), nw)
+        vcopy(A("lo16"), A("t4"))
+        if not last:
+            vcopy(A("v16"), A("vf"))
+            vtt(ind(A("L", 0, 1152), A("lo16")), A("LE"), A("ODDN"), add)
+            vcopy(A("a16"), ind(A("C"), A("v16")))
+            act(A("own"), ind(A("Y", 0, 1024), A("v16")), AF.Copy)
+        else:
+            vtt(ind(A("LO", 0, 1152), A("lo16")), A("LE"), A("ODDO"), add)
+            fix()
+            vcopy(ind(A("Y", 0, 1024), A("v16")), nw)
+        FRc, FRn = FRn, FRc
+
+    dma("s", T.lo[1:128:2, :], T.LO[1:128:2, 0:1024], [("LO", 0, 1024)], [], "out5")
+    dma("s", T.yo[:, 0:512], T.Y[:, 512:1024], [("Y", 512, 1024)], [], "out1")
+    dma("s", T.yo[:, 896:1408], T.Y[:, 0:512], [("Y", 0, 512)], [], "out2")
+    vts(A("FOt"), A("psm", 0, 88), 512.0, lt, 1408.0, mul)
+    vtt(A("FOu"), A("psm", 0, 88), A("FOt"), add)
+    vts(A("FO", 0, 56), A("FOu", 32, 88), -512.0, add)
+    vts(A("FO", 56, 88), A("FOu", 0, 32), -512.0, add)
+    dma("a", T.fo[:, :], T.FO[:, :], [("FO", 0, 88)], [], "out3")
+    p = 384 * (RO - 1)
+    dma("s", T.yo[:, 512:896], T.LAND[:, p:p + 384], [("LAND", p, p + 384)], [], "out4")
+    for sem in ("dv", "ac", "pe", "gp"):
+        g.wait_ge(T.sem[sem], count[sem])
+    for sem in sorted(total):
+        g.wait_ge(T.sem[sem], total[sem])

@@ -1,35 +1,32 @@
 from concourse.bass import DstId, RemoteDMATransfer
-from concourse.mybir import AluOpType, AxisListType, ActivationFunctionType
+from concourse.mybir import AluOpType, ActivationFunctionType
 
 RO = 4
 BIG = 262144.0
-MAG = 402653184.0
 F32, BF, I32, U16, F16 = "float32", "bfloat16", "int32", "uint16", "float16"
+
+
+def unit(u):
+    return 1.5 * 2.0 ** 23 * u
+
 
 SCRATCH = {}
 for _n, _c, _d in (
-        ("Y", 1408, BF), ("C", 1024, I32), ("LI", 1024, I32), ("L", 1152, F32), ("LO", 1152, F32),
-        ("FW", 56, I32), ("FL", 88, U16), ("FR0", 1536, F32), ("FR1", 1536, F32), ("W", 1408, BF), ("TH8", 128, I32),
-        ("THF", 128, F32), ("BT8", 128, F32), ("T4", 128, I32), ("NEW", 512, BF), ("LAND", 1536, BF),
-        ("a16", 128, U16), ("af", 128, F32), ("Lg", 2048, F16), ("bc16", 256, U16), ("bt", 128, F32),
-        ("xb", 2048, F32), ("y16", 2048, F16), ("dS", 2048, BF), ("dA", [8, 256], BF),
-        ("own", 128, BF), ("nown", 128, F16), ("u1", 128, F32), ("SC", 256, F32), ("hi", 16, F32), ("pkc", 16, F32),
-        ("of", 16, F32), ("po", 16, U16), ("pr", [3, 128], F16), ("nrm", 128, F16), ("sg", 128, BF),
-        ("l16", 16, U16), ("er", 128, F32), ("em", 128, F32), ("es", 128, F32), ("e16", 8, U16), ("fx", 128, F32),
-        ("wm", 128, F32), ("ws", 128, F32), ("w16", 8, U16),
-        ("lamA", 8, F32), ("ap16", 8, U16), ("DD", 1024, BF), ("DS", 1024, BF), ("LE", 128, F32), ("ODDN", 128, F32),
-        ("ODDO", 128, F32), ("um", 128, F32), ("cn", 128, I32), ("cm", 128, I32),
-        ("REF", 8, F32), ("NREF", 8, F32), ("thr", 8, F32), ("thr0", 8, F32), ("ar", 1, F32), ("arh", 1, F16), ("ai", 1, I32),
-        ("aj", 1, I32), ("ak", 1, F32), ("vB", 8, F32), ("v16", 8, U16), ("vf", 8, F32), ("vo", 8, F32), ("vq", 8, F32),
-        ("vp", 8, F32), ("vo16", 8, U16), ("t0", 8, F32), ("t1", 8, F32), ("t2", 8, F32), ("t3", 8, F32), ("t4", 8, F32),
-        ("lo16", 8, U16), ("al0", 8, F32), ("al1", 8, I32), ("al2", 8, I32), ("al3", 8, F32), ("al4", 8, F32), ("alt", 8, F32),
-        ("aln", 8, F32), ("wi", 8, I32), ("wB", 8, I32), ("gh", 8, F32), ("ng", 8, F32), ("x1", 8, F32), ("ga", 8, F32),
-        ("gb", 8, F32), ("FO", 88, F32), ("FOt", 88, F32), ("FOu", 88, F32),
-        ("T1", 128, I32), ("T1a", 128, I32), ("T2", 128, I32), ("T2a", 128, I32), ("M1", 2048, BF), ("I16", 128, F16),
-        ("If", 128, F32), ("BO", 128, F16), ("I5", 128, F16), ("E", 2048, F16), ("E5", 2048, F16), ("EF", 2048, F32),
-        ("OHf", 16, F32), ("Z32", 144, BF), ("Z1", 144, F16), ("zb", 512, BF), ("MK", 128, F32), ("MKH", 128, F32),
-        ("d0P", 128, F32), ("d0Q", 128, F32), ("d0S", 128, F32), ("d0D", 1024, BF), ("JR", 128, F32),
-        ("SMI", 64, I32), ("SMF", 64, F32), ("CL", 8, U16)):
+        ("Y", 1408, BF), ("C", 1408, I32), ("LI", 1024, I32), ("L", 1152, F32), ("FW", 56, I32), ("FL", 88, U16),
+        ("FR0", 1536, BF), ("FR1", 1536, BF), ("W", 1408, BF), ("TH8", 128, I32), ("THF", 128, F32), ("NEW", 512, BF),
+        ("LAND", 1536, BF), ("FO", 88, F32), ("v16", 32, U16),
+        ("abc", 384, U16), ("Lg", 2048, F16), ("lh", 128, F32), ("xb", 2048, F32), ("y16", 2048, F16), ("yS", 2048, F32),
+        ("dA", [8, 256], BF), ("own", 128, BF), ("nT", 128, F16), ("u1", 128, F32), ("SC", 256, F32), ("hi", 16, F32),
+        ("pk", 16, F32), ("po", 16, U16), ("RN", 16, BF), ("pd", 32, F32), ("pr", 384, F16), ("dq", 128, F16), ("sg", 128, BF),
+        ("l16", 24, U16), ("vo16", 8, U16), ("er", 128, BF), ("hw", 128, BF), ("apr", 128, F16), ("EQ", 1024, BF),
+        ("DD", 128, BF), ("DS", 128, BF), ("m1", 8, F32), ("m2", 8, F32), ("lo16", 8, U16), ("LE", 128, F32), ("ODN", 128, F32), ("um", 128, F32),
+        ("cn", 128, I32), ("cm", 128, I32), ("ai", 8, I32), ("al", 8, I32), ("mx", 8, F32), ("B", 8, F32), ("s2", 8, U16),
+        ("thr", 8, F32), ("thr0", 8, F32), ("ah", 1, F32),
+        ("T1", 128, I32), ("T1a", 128, I32), ("TK", 128, I32), ("Q16", 88, I32), ("PI", 8, I32), ("JR", 128, BF),
+        ("I", 128, F16), ("M1", 2048, BF), ("M32", 32, BF), ("R", 512, F16), ("EE", [16, 144], F16), ("e1", 128, F16),
+        ("e2", 128, F16), ("BC", 16, BF), ("BO", 128, BF), ("Z", 576, BF), ("ZT", 144, F32), ("d0P", 64, F32), ("d0Q", 64, F32),
+        ("d0D", 128, BF), ("half", 128, F32), ("POW", 128, F32), ("TM", 128, F32), ("TM0", 128, F32), ("PC", 32, F32),
+        ("SF", 64, F32), ("LH", 8, F16), ("CL", 34, U16), ("RB", 12, F32), ("wt", 16, F32), ("cst", 2, BF)):
     SCRATCH[_n] = ("sbuf", [128] + (_c if isinstance(_c, list) else [_c]), _d)
 for _n in ("psb0", "psb1", "psd0", "psd1", "psd2", "psd3", "psk", "psm"):
     SCRATCH[_n] = ("psum", [128, 512], F32)
@@ -44,8 +41,7 @@ def rank_program(g, core, T, topo):
         return
     cores = T.cores
     add, sub, mul, mx, mn = AluOpType.add, AluOpType.subtract, AluOpType.mult, AluOpType.max, AluOpType.min
-    ge, gt, le, lt, eq, ne = (AluOpType.is_ge, AluOpType.is_gt, AluOpType.is_le, AluOpType.is_lt, AluOpType.is_equal,
-                              AluOpType.not_equal)
+    ge, gt, le, eq = AluOpType.is_ge, AluOpType.is_gt, AluOpType.is_le, AluOpType.is_equal
     band, shr = AluOpType.bitwise_and, AluOpType.arith_shift_right
     AF = ActivationFunctionType
     queues = {"v": g.vector, "a": g.scalar, "p": g.tensor, "g": g, "s": g.sync}
@@ -89,7 +85,9 @@ def rank_program(g, core, T, topo):
                     ents[:] = [x for x in ents if not (x[0] >= lo and x[1] <= hi)]
                 ents.append((lo, hi, wr, e, sem, val, clk))
 
-    def do(e, fn, reads, writes):
+    def do(e, fn, ins, outs):
+        reads = [tok for x in ins if isinstance(x, tuple) for tok in x[1] + x[2]] + [tok for x in outs for tok in x[2]]
+        writes = [tok for x in outs for tok in x[1]]
         waits(e, reads, writes)
         sem = semof[e]
         count[sem] += 1
@@ -102,339 +100,302 @@ def rank_program(g, core, T, topo):
         total[sem] = 16
         note("d", dict(known[e]), reads, writes, sem, 16)
 
-    def A(nm, lo=0, hi=None, st=1):
+    def A(nm, lo=0, hi=None, st=1, parts=128):
         if hi is None:
             hi = SCRATCH[nm][1][1]
-        ap = T[nm][:, lo:hi] if st == 1 else T[nm][:, lo:hi:st]
+        ap = T[nm][0:parts, lo:hi] if st == 1 else T[nm][0:parts, lo:hi:st]
         return (ap, [(nm, lo, hi)], [])
 
-    def A8(nm):
-        return (T[nm][0:8, :], [(nm, 0, 128)], [])
-
-    def PR(q):
-        return (T.pr[:, q, :], [("pr", q, q + 1)], [])
+    def A3(nm, ap):
+        return (ap, [(nm, 0, 1 << 20)], [])
 
     def ind(win, off):
         return (win[0].indirect(off[0]), win[1], off[1])
 
+    def val(z):
+        return z[0] if isinstance(z, tuple) else z
+
     def vcopy(o, x):
-        do("v", lambda: g.vector.tensor_copy(out=o[0], in_=x[0]), x[1] + x[2] + o[2], o[1])
+        do("v", lambda: g.vector.tensor_copy(out=o[0], in_=x[0]), [x], [o])
 
     def vtt(o, x, y, op):
-        do("v", lambda: g.vector.tensor_tensor(out=o[0], in0=x[0], in1=y[0], op=op), x[1] + x[2] + y[1] + o[2], o[1])
+        do("v", lambda: g.vector.tensor_tensor(out=o[0], in0=x[0], in1=y[0], op=op), [x, y], [o])
 
     def vts(o, x, s1, op0, s2=None, op1=None):
-        rd = x[1] + x[2] + o[2]
-        a1, a2 = s1, s2
-        if isinstance(s1, tuple):
-            rd = rd + s1[1]
-            a1 = s1[0]
-        if isinstance(s2, tuple):
-            rd = rd + s2[1]
-            a2 = s2[0]
         if op1 is None:
-            do("v", lambda: g.vector.tensor_scalar(out=o[0], in0=x[0], scalar1=a1, scalar2=None, op0=op0), rd, o[1])
+            do("v", lambda: g.vector.tensor_scalar(out=o[0], in0=x[0], scalar1=val(s1), scalar2=None, op0=op0), [x, s1], [o])
         else:
-            do("v", lambda: g.vector.tensor_scalar(out=o[0], in0=x[0], scalar1=a1, scalar2=a2, op0=op0, op1=op1), rd, o[1])
+            do("v", lambda: g.vector.tensor_scalar(out=o[0], in0=x[0], scalar1=val(s1), scalar2=val(s2), op0=op0, op1=op1),
+               [x, s1, s2], [o])
 
-    def vscan(o, d0, d1, op0, op1):
-        do("v", lambda: g.vector.tensor_tensor_scan(out=o[0], data0=d0[0], data1=d1[0], initial=0.0, op0=op0, op1=op1),
-           d0[1] + d1[1], o[1])
+    def vscan(o, d0, d1, op0, op1, first=0.0):
+        do("v", lambda: g.vector.tensor_tensor_scan(out=o[0], data0=d0[0], data1=d1[0], initial=first, op0=op0, op1=op1),
+           [d0, d1], [o])
 
     def vset(o, c):
-        do("v", lambda: g.vector.memset(o[0], c), [], o[1])
+        do("v", lambda: g.vector.memset(o[0], c), [], [o])
 
-    def act(o, x, f, bias=None, scale=None):
-        rd = x[1] + x[2]
+    def act(o, x, f=AF.Copy, bias=None, scale=None):
         kw = {}
         for key, z in (("bias", bias), ("scale", scale)):
-            if isinstance(z, tuple):
-                rd = rd + z[1]
-                kw[key] = z[0]
-            elif z is not None:
-                kw[key] = z
-        do("a", lambda: g.scalar.activation(out=o[0], in_=x[0], func=f, **kw), rd, o[1])
+            if z is not None:
+                kw[key] = val(z)
+        do("a", lambda: g.scalar.activation(out=o[0], in_=x[0], func=f, **kw), [x, bias, scale], [o])
 
-    def mms(bank, reads, jobs):
+    def copy(e, o, x):
+        if e == "v":
+            vcopy(o, x)
+        elif e == "a":
+            act(o, x)
+        else:
+            n = o[1][0][2] - o[1][0][1]
+            do("g", lambda: g.affine_select(out=o[0], in_=x[0], pattern=[[0, n]], compare_op=ge, fill=0.0, base=0,
+                                            channel_multiplier=0), [x], [o])
+
+    def mms(bank, jobs, first=True, last=True):
         def fn():
-            last = None
-            for o, l, r, st, sp in jobs:
-                last = g.tensor.matmul(out=o, lhsT=l, rhs=r, start=st, stop=sp)
-            return last
-        do("p", fn, reads, [(bank, 0, 512)])
+            call = None
+            for j, (o, l, r) in enumerate(jobs):
+                call = g.tensor.matmul(out=o[0], lhsT=l[0], rhs=r[0], start=first and j == 0, stop=last and j == len(jobs) - 1)
+            return call
+        do("p", fn, [x for job in jobs for x in job[1:]], [A(bank)])
 
     def iota(o, pattern, base, cmul, flag=False):
-        if flag:
-            do("g", lambda: g.iota(o[0], pattern=pattern, base=base, channel_multiplier=cmul,
-                                   allow_small_or_imprecise_dtypes=True), [], o[1])
-        else:
-            do("g", lambda: g.iota(o[0], pattern=pattern, base=base, channel_multiplier=cmul), [], o[1])
+        kw = {"allow_small_or_imprecise_dtypes": True} if flag else {}
+        do("g", lambda: g.iota(o[0], pattern=pattern, base=base, channel_multiplier=cmul, **kw), [], [o])
 
-    def fill(o, c, flag=True):
-        iota(o, [[0, o[1][0][2] - o[1][0][1]]], c, 0, flag)
+    def to_list(out, z, nm, lo, hi):
+        return [(out, A("Z", 144 * z + 16 - r, 144 * z + 144 - r), A(nm, lo + r, hi, 16)) for r in range(16)]
 
-    def SF(j, n=1):
-        return A("SMF", j, j + n)
-
-    RC, EV, OD, LIc, K15, TRc, TD = SF(0), SF(1), SF(2), SF(8, 8), SF(16, 8), SF(24, 8), SF(32, 8)
+    ONE, X32, FULL, BLOCK = range(4)
+    SF = lambda j, n=1: A("SF", j, j + n)
+    RC, EV, OD, R1, R2, RF, RO2, PW = SF(0), SF(1), SF(2), SF(3), SF(4), SF(5), SF(6), SF(7)
+    LI, K15, IK, ODB = SF(8, 8), SF(16, 8), SF(24, 8), SF(32, 4)
+    R0, RH = SF(36), SF(37)
 
     dma("s", T.LI[:, :], T.lk[:, :], [], [("LI", 0, 1024)], "in0")
-    dma("a", T.C[:, 512:640], T.cl[:, 0:128], [], [("C", 512, 640)], "in1")
+    dma("a", T.C[:, 0:128], T.cl[:, 0:128], [], [("C", 0, 128)], "in1")
     dma("a", T.FW[:, :], T.fw0[:, :], [], [("FW", 0, 56)], "in2")
+    dma("s", T.Y[:, 0:896], T.y0[:, :], [], [("Y", 0, 896)], "in3")
     dma("a", T.TH8[0:8, :], T.th[:, :], [], [("TH8", 0, 128)], "in5")
-    dma("s", T.Y[:, 512:1408], T.y0[:, :], [], [("Y", 512, 1408)], "in3")
-    dma("s", T.C[:, 640:1024], T.cl[:, 128:512], [], [("C", 640, 1024)], "in4")
+    dma("s", T.C[:, 128:512], T.cl[:, 128:512], [("LI", 0, 1024)], [("C", 128, 512)], "in4")
 
+    iota(A("TK"), [[1, 16], [16, 8]], 0, -1)
     iota(A("T1"), [[1, 128]], 128, -1)
-    iota(A("SMI", 0, 1), [[0, 1]], 0, 1)
-    iota(A("T2"), [[16, 8], [0, 16]], 15, -1)
-    iota(A("SMI", 32, 64), [[16, 32]], 0, 0)
-    iota(A("SMI", 16, 24), [[1, 8]], 0, 0)
-    iota(A8("T4"), [[1, 128]], 0, -16)
-    fill(A("zb"), 0)
+    iota(A("PI", 0, 1), [[0, 1]], 0, 1)
+    iota(A("Q16"), [[16, 88]], 0, 0)
     iota(A("JR"), [[1, 128]], 0, 0, True)
-    fill(A("Y", 0, 512), 0)
-    fill(A("Z32"), 0)
-    fill(A("d0P"), 1)
-    fill(A("d0Q"), -1)
-    fill(A("W", 0, 512), 0)
-    fill(A("d0S"), 1)
-    fill(A("vB"), 512)
-    iota(A("FR1", 128, 1536), [[1, 1408]], 0, 0, True)
-    iota(A("FR0", 128, 640), [[1, 512]], 0, 0, True)
-    fill(A("C", 0, 512), 0, False)
+    iota(A("C", 512, 896), [[0, 384]], 0, 0)
 
+    vset(A3("EE", T.EE[:, :, :]), 0.0)
+    vts(A("e1"), A("TK"), 0, eq, 4096.0, mul)
+    vts(A("e2", 0, 88), A("TK", 0, 88), -5, eq)
+    vts(A("e2", 88, 128), A("TK", 88, 128), 11, eq)
     vts(A("T1a"), A("T1"), 15, band)
-    vts(A("If"), A("T1"), 128, eq)
+    vts(A("I"), A("T1"), 128, eq)
+    vtt(A3("EE", T.EE[:, :, 15:143:16]), A("e1"), A("e2"), add)
     vts(A("M1", 0, 128), A("T1a"), 0, eq)
-    vts(A("I16"), A("T1"), 128, eq)
-    vcopy(A("OHf"), A("M1", 0, 16))
-    vcopy(A("M1", 128, 256), A("M1", 0, 128))
-    vts(A("SMI", 1, 2), A("SMI", 0, 1), 15, band)
-    vts(A("SMI", 2, 3), A("SMI", 0, 1), 1, band)
-    vts(A("T2a"), A("T2"), 4, shr)
-    vcopy(RC, A("SMI", 1, 2))
-    vcopy(OD, A("SMI", 2, 3))
-    vts(A("BO"), A("T2a"), 0, eq)
-    vts(A("FL", 0, 32), A("SMI", 32, 64), RC, add)
-    vts(LIc, A("SMI", 32, 40), RC, add)
-    for k in range(16):
-        vts(A("E", 128 * k, 128 * k + 128), A("I16"), A("M1", k, k + 1), mul)
-    vtt(A("I5"), A("M1", 5, 133), A("BO"), mul)
-    vts(A("FL", 32, 88), A("FW"), 512, add)
-    vts(A("v16"), A("SMI", 32, 40), RC, add, 512, add)
-    vcopy(A("a16"), A("C", 512, 640))
-    for k in range(16):
-        z = (k + 5) % 16
-        vts(A("E5", 128 * k, 128 * k + 128), A("I5"), A("M1", z, z + 1), mul)
+    vts(A("T1a", 0, 32), A("T1", 0, 32), 31, band)
+    vts(A("PI", 1, 2), A("PI", 0, 1), 15, band)
+    vts(A("PI", 2, 3), A("PI", 0, 1), 1, band)
+    vts(A("PI", 3, 4), A("PI", 0, 1), 7, band)
+    vts(A("ai"), A("TK", 120, 128), 4, shr)
+    vts(A("CL", 0, 32), A("Q16", 0, 32), 1.0 / 16, mul)
+    vts(A("M32"), A("T1a", 0, 32), 0, eq)
+    vcopy(RC, A("PI", 1, 2))
+    vset(A("BC", 8, 16), 0.0)
+    vts(A("BC", 0, 8), A("ai"), 0, eq)
+    act(A("R"), ind(A("M32"), A("CL", 0, 32)))
+    vts(R1, RC, 1.0, ge)
+    vts(R2, RC, 2.0, ge, -4096.0, mul)
+    vcopy(SF(36, 2), A("M1", 0, 2))
+    act(A("BO"), ind(A("BC"), A("CL", 0, 8)), scale=32.0)
+    for j in (128, 256, 512, 1024):
+        act(A("M1", j, 2 * j), A("M1", 0, j))
 
-    act(A("MK"), A("M1", 0, 128), AF.Copy)
-    act(A("MKH"), A("M1", 0, 128), AF.Copy, scale=0.5)
-    for j in (256, 512, 1024):
-        act(A("M1", j, 2 * j), A("M1", 0, j), AF.Copy)
-    for k in range(16):
-        act(A("EF", 128 * k, 128 * k + 128), A("If"), AF.Copy, scale=A("OHf", k, k + 1))
-    for j in (0, 512):
-        act(A("d0D", j, j + 512), A("zb"), AF.Copy, bias=-1.0 / 256)
-    act(TRc, LIc, AF.Copy, bias=1024.0)
-    act(TD, LIc, AF.Copy, scale=1.0 / 256, bias=-127.0 / 256)
-    for o, z in ((SF(3), -512.0), (SF(4), 896.0), (SF(5), 128.0)):
-        act(o, OD, AF.Copy, scale=z)
-    act(EV, OD, AF.Copy, scale=-1.0, bias=1.0)
-    act(A("ODDN"), A("JR"), AF.Identity, scale=OD, bias=SF(3))
-    act(A("ODDO"), A("JR"), AF.Identity, scale=OD, bias=SF(4))
-    act(A("own"), ind(A("Y", 0, 1024), A("v16")), AF.Copy)
-    act(A("W", 512, 1408), ind(A("Y"), A("FL", 32, 88)), AF.Copy, scale=0.5)
+    def later_constants(part):
+        if part == 0:
+            vts(A("RB", 0, 11), A("Q16", 0, 88, 8), R1, mul)
+            vset(A("Z"), 0.0)
+            vts(A("RB", 4, 7), A("Q16", 32, 56, 8), RH, mul, R2, add)
+            vts(LI, A("Q16", 0, 8), RC, add)
+            vts(RF, RC, 1.0, le)
+            vts(RO2, RC, 2.0, eq)
+            for b in range(11):
+                vts(A("FR1", 128 * b, 128 * b + 128), A("JR"), R0, mul, A("RB", b, b + 1), add)
+            for z, s in ((ONE, 1.0), (X32, 32.0), (FULL, RF), (BLOCK, RO2)):
+                vts(A("Z", 144 * z + 16, 144 * z + 144, 16), A("BC", 0, 8), s, mul)
+        if part == 1:
+            vset(A("ZT", parts=8), 0.0)
+            vset(A("d0P"), 1.0)
+            vset(A("d0Q"), -1.0)
+            vcopy(A("ZT", 16, 144, 16, parts=8), A("I", 0, 8, parts=8))
+            vset(A("d0P", 0, 64, 16), -BIG)
+            vset(A("d0Q", 0, 64, 16), BIG)
+            vts(K15, LI, 16.0, mul, 15.0, add)
+            vts(A("v16", 0, 8), A("Q16", 0, 8), RC, add)
+            vts(A("FL", 56, 88), A("Q16", 56, 88), RC, add)
+            vcopy(A("CL", 32, 33), A("PI", 3, 4))
+            vcopy(A("CL", 33, 34), A("PI", 1, 2))
+        if part == 2:
+            vset(A("half"), 0.5)
+            vset(A("d0D"), 1.0)
+            vset(A("TM0"), 0.0)
+            vts(A("PC", 0, 8), LI, 896.0, add)
+            vscan(A("POW"), A("half"), A("TM0"), mul, add, 2.0 ** 65)
+            vset(A("d0D", 0, 128, 16), 0.0)
+            vts(A("PC", 8, 16), LI, 1408.0, add)
+            vts(A("TM0"), A("M1", 0, 128), -1e29, mul, 1e29, add)
+            vtt(A("wt"), A("POW", 64, 80), A("M1", 0, 16), mul)
+            vts(A("half"), A("POW"), 80.0, mul)
+            vts(A("PC", 24, 32), LI, 1024.0, add)
+            vscan(A("lh", 0, 16), A("d0D", 0, 16), A("wt"), mul, add)
+            vtt(A("TM"), A("half"), A("TM0"), mx)
+            vts(A("PC", 16, 24), A("POW", 0, 128, 16), A("lh", 15, 16), mul)
+        if part == 3:
+            vcopy(OD, A("PI", 2, 3))
+            vts(IK, LI, -4096.0, add)
+            vcopy(A("LH"), LI)
+            vts(EV, A("PI", 2, 3), 0, eq)
+            vset(A("cst"), -15.0 / 32)
+            vts(ODB, A("Q16", 56, 88, 8), OD, mul)
+            vcopy(A("FR0", 896, 1408), A("FR1", 896, 1408))
+            vts(A("FO", 80, 88), LI, 1280.0, add)
 
-    vcopy(A("Z32", 16, 144, 16), A("BO", 0, 128, 16))
-    vcopy(A("Z1"), A("Z32"))
-    vts(A("Z32", 16, 144, 16), A("BO", 0, 128, 16), 32.0, mul)
-    vset(A("d0P", 0, 128, 16), -BIG)
-    vset(A("d0Q", 0, 128, 16), BIG)
-    vts(K15, LIc, 16.0, mul, 15.0, add)
-
-    def to_list(bank, o, src, q):
-        return [(T[bank][:, o:o + 8 * q], T.Z1[:, 16 - r:144 - r], src(r), r == 0, r == 15) for r in range(16)]
+    later_constants(0)
+    later_constants(1)
+    vcopy(A("FL", 0, 56), A("FW"))
+    vcopy(A("abc", 0, 128), A("C", 0, 128))
+    act(A("THF", parts=8), A("TH8", parts=8), scale=32.0, bias=15.0)
+    act(A("FR0", 0, 896), ind(A("FR1", 0, 896), A("FL", 0, 56)))
+    mms("psk", [(A("psk", 0, 8), A("ZT", 16 - r, 144 - r, parts=8), A("THF", r, 128, 16, parts=8)) for r in range(16)])
+    act(A("W", 0, 896), ind(A("Y", 0, 896), A("FL", 0, 56)), scale=0.5)
 
     FRc, FRn = "FR0", "FR1"
     for t in range(RO):
         last = t == RO - 1
+        made = 896 + 128 * t
+        v = A("v16", 8 * t, 8 * t + 8)
+        own = A("Y", 0, 128) if t == 0 else A("own")
+        a16, P, Q = A("abc", 0, 128), A("po", 0, 8), A("po", 8, 16)
 
-        def gather_links(q):
-            src = A("LI") if t == 0 else A("L", 0, 1024)
-            vcopy(A("Lg", 512 * q, 512 * q + 512), ind(src, A("a16", 32 * q, 32 * q + 32)))
-
-        def list_at(h, z):
-            return ("psm", 400) if h and z else ("psb%d" % h, z)
+        def links(e, q):
+            copy(e, A("Lg", 512 * q, 512 * q + 512), ind(A("LI") if t == 0 else A("L", 0, 1024), A("abc", 32 * q, 32 * q + 32)))
 
         def lists(h):
-            for z, nm in ((0, "E"), (64, "E5")):
-                bank, o = list_at(h, z)
-                mms(bank, [(nm, 0, 2048), ("Lg", 1024 * h, 1024 * h + 1024)],
-                    [(T[bank][:, o:o + 64], T[nm][:, 128 * k:128 * k + 128], T.Lg[:, 1024 * h + k:1024 * h + 1024:16],
-                      k == 0, k == 15) for k in range(16)])
+            mms("psb%d" % h, [(A("psb%d" % h, 0, 64), A3("EE", T.EE[:, k, 15 - k:143 - k]), A("Lg", 1024 * h + k, 1024 * h + 1024, 16))
+                              for k in range(16)])
 
-        def lists_out(h, z):
-            bank, o = list_at(h, z)
-            vts(A("bc16", 128 * h + z, 128 * h + z + 64), A(bank, o, o + 64), 512.0, add)
+        def lists_out(h):
+            ps = A("psb%d" % h, 0, 64)
+            vts(A("abc", 128 + 64 * h, 192 + 64 * h), ps, 1.0 / 4096, mul)
+            vts(A("lh", 64 * h, 64 * h + 64), ps, unit(4096), add, unit(4096), sub)
+
+        def lists_c(h):
+            vtt(A("abc", 256 + 64 * h, 320 + 64 * h), A("psb%d" % h, 0, 64), A("lh", 64 * h, 64 * h + 64), sub)
 
         def own_in(n):
-            ps = T["psd%d" % n]
-            mms("psd%d" % n, [("I16", 0, 128), ("nown", 0, 128)],
-                [(ps[:, k:512:16], T.I16[:, :], T.nown[:, 32 * n:32 * n + 32], k == 0, False) for k in range(16)])
+            part = slice(32 * n, 32 * n + 32)
+            mms("psd%d" % n, [(A("psd%d" % n), A3("nT", T.nT[part, :]), A3("R", T.R[part, :]))], last=False)
 
-        def blend_b(n):
-            o = 128 * (n // 2) + 32 * (n % 2)
-            act(A("xb", 512 * n, 512 * n + 512), ind(A("W"), A("bc16", o, o + 32)), AF.Copy, bias=1087.75)
+        def blend_b(e, n):
+            o, x = A("xb", 512 * n, 512 * n + 512), ind(A("W", 0, made), A("abc", 128 + 32 * n, 160 + 32 * n))
+            if e == "a":
+                act(o, x, bias=1087.75)
+            else:
+                vts(o, x, 1087.75, add)
 
         def blend_c(n):
-            o = 128 * (n // 2) + 64 + 32 * (n % 2)
-            vtt(A("y16", 512 * n, 512 * n + 512), ind(A("W"), A("bc16", o, o + 32)), A("xb", 512 * n, 512 * n + 512), add)
-            mms("psd%d" % n, [("I16", 0, 128), ("y16", 512 * n, 512 * n + 512)],
-                [(T["psd%d" % n][:, :], T.I16[:, :], T.y16[:, 512 * n:512 * n + 512], False, True)])
+            y = A("y16", 512 * n, 512 * n + 512)
+            vtt(y, ind(A("W", 0, made), A("abc", 256 + 32 * n, 288 + 32 * n)), A("xb", 512 * n, 512 * n + 512), add)
+            mms("psd%d" % n, [(A("psd%d" % n), A("I"), y)], first=False)
+            copy("g", A("yS", 512 * n, 512 * n + 512), y)
 
         def size_d(n):
             act((T.dA[:, 2 * n:2 * n + 2, :], [("dA", 2 * n, 2 * n + 2)], []), A("psd%d" % n), AF.Abs)
 
-        def keep_d(n):
-            vcopy(A("dS", 512 * n, 512 * n + 512), A("psd%d" % n))
-
         def sum_d(h):
-            bank = "psb1" if h else "psk"
-            mms(bank, [("Z32", 0, 144), ("dA", 4 * h, 4 * h + 4)],
-                [(T[bank][:, 0:64], T.Z32[:, 16 - r:144 - r], T.dA[:, 4 * h:4 * h + 4, 16 * r:16 * r + 16], r == 0, r == 15)
-                 for r in range(16)])
+            bank = "psm" if h else "psk"
+            mms(bank, [(A(bank, 0, 64), A("Z", 144 * X32 + 16 - r, 144 * X32 + 144 - r),
+                        (T.dA[:, 4 * h:4 * h + 4, 16 * r:16 * r + 16], [("dA", 4 * h, 4 * h + 4)], [])) for r in range(16)])
 
         def scans(h):
-            bank, o = ("psb1" if h else "psk"), 64 * h
-            vscan(A("SC", o, o + 64), A("d0P", o, o + 64), A(bank, 0, 64), add, mx)
-            vscan(A("SC", 128 + o, 192 + o), A("d0Q", o, o + 64), A(bank, 0, 64), add, mn)
+            bank, o = ("psm" if h else "psk"), 64 * h
+            vscan(A("SC", o, o + 64), A("d0P"), A(bank, 0, 64), add, mx)
+            vscan(A("SC", 128 + o, 192 + o), A("d0Q"), A(bank, 0, 64), add, mn)
 
-        def room():
-            vtt(A("Y", 128 * t, 128 * t + 128), ind(A("dS"), P), A("own"), add)
+        def compose(e, lo, hi):
+            copy(e, A(FRn, lo, hi), ind(A(FRc, 0, made), A("FL", lo // 16, hi // 16)))
 
-        def fix():
-            vcopy(ind(A(FRn, 0, 1536), A("vo16")), A("fx"))
-            lo = 640 if t == 0 else 128
-            mms("psm", [("EF", 0, 2048), (FRn, 128, 1536)],
-                [(T.psm[:, 0:(1536 - lo) // 16], T.EF[:, 128 * r:128 * r + 128], T[FRn][:, lo + r:1536:16], r == 0, r == 15)
-                 for r in range(16)])
-
-        gather_links(0)
-        vts(A("nown"), A("own"), -1.0, mul, -1088.0, add)
-        gather_links(1)
-        if t == 0:
-            vts(A8("T4"), A8("T4"), 4, shr)
-            vset(A("d0S", 0, 128, 16), 0.0)
-            vcopy(A("CL"), A("SMI", 16, 24))
-            vts(A8("BT8"), A8("T4"), 0, eq)
-        else:
-            vcopy(A("FL", 32 if t == 1 else 0, 88), A("psm", 0, 56 if t == 1 else 88))
+        links("v", 0)
+        mms("psb1", [(A("psb1", 0, 128), own, A("I"))])
+        act(A("nT"), A("psb1", 0, 128), scale=-1.0, bias=-1088.0)
+        links("v", 1)
         lists(0)
         own_in(0)
-        gather_links(2)
-        if t > 0:
-            do("v", lambda: g.vector.tensor_reduce(out=T.ar[:, :], in_=T.REF[:, :], axis=AxisListType.X, op=add),
-               [("REF", 0, 8)], [("ar", 0, 1)])
-        vcopy(A("af"), A("a16"))
-        if t > 0:
-            vcopy(A("arh"), A("ar"))
-            act(A("Y", 1024, 1408), A("LAND", 384 * t - 384, 384 * t), AF.Copy)
-            act(A("W", 512, 1408), ind(A("Y"), A("FL", 32, 88)), AF.Copy, scale=0.5)
-            act(A("W", 0, 128 * t), ind(A("Y"), A("FL", 0, 8 * t)), AF.Copy, scale=0.5)
-        lists_out(0, 0)
-        lists_out(0, 64)
-        gather_links(3)
-        lists(1)
-        vts(A("al0"), A("vB"), 512.0, ge, 128.0, mul)
-        if t == 0:
-            vcopy(A("L", 0, 1024), A("LI"))
-            vcopy(A8("THF"), A8("TH8"))
-            mms("psk", [("BT8", 0, 128), ("THF", 0, 128)], [(T.psk[:, 128:256], T.BT8[0:8, :], T.THF[0:8, :], True, True)])
-        else:
-            vtt(ind(A("LO", 0, 1152), A("lo16")), A("LE"), A("ODDO"), add)
-        lists_out(1, 0)
-        blend_b(0)
         own_in(1)
-        blend_b(1)
-        blend_c(0)
-        lists_out(1, 64)
+        links("a", 2)
+        links("v", 3)
         if t == 0:
-            vtt(A("em"), A("psk", 128, 256), A("MK"), mul)
-        blend_b(2)
-        blend_b(3)
+            vcopy(A("thr"), A("psk", 0, 8))
+            vts(A("thr0"), A("psk", 0, 8), 240.0, add)
+        lists_out(0)
+        lists(1)
         own_in(2)
-        blend_c(1)
-        if t == 0:
-            vscan(A("es"), A("d0S"), A("em"), mul, add)
-        size_d(0)
         own_in(3)
+        blend_b("a", 0)
+        lists_c(0)
+        blend_b("v", 1)
+        lists_out(1)
+        blend_b("a", 2)
+        blend_c(0)
+        lists_c(1)
+        blend_b("a", 3)
+        blend_c(1)
+        size_d(0)
         blend_c(2)
-        if t == 0:
-            vts(A("thr0"), A("es", 15, 128, 16), 32.0, mul, 15.0, add)
         size_d(1)
-        blend_c(3)
-        vts(A("vp"), A("vB"), 128.0, add)
-        if t == 0:
-            vcopy(A("thr"), A("thr0"))
-            vset(A("d0D", 0, 1024, 128), 2048.0)
-        mms("psm", [("BO", 0, 128), ("nown", 0, 128)], [(T.psm[:, 256:384], T.BO[:, :], T.nown[:, :], True, True)])
-        if t > 0:
-            mms("psm", [("BO", 0, 128), ("arh", 0, 1)], [(T.psm[:, 500:501], T.BO[:, :], T.arh[:, :], True, True)])
-        size_d(2)
         sum_d(0)
-        keep_d(0)
-        keep_d(1)
+        blend_c(3)
+        size_d(2)
         size_d(3)
-        act(A("dS", 1536, 2048), A("psd3"), AF.Copy)
         sum_d(1)
-        if t > 0:
-            vcopy(A("ai"), A("psm", 500, 501))
-        vcopy(A("bt", 0, 64), A("bc16", 0, 64))
-        keep_d(2)
-        if t > 0:
-            vts(A("aj"), A("ai"), 15, band)
-        scans(0)
-        if t > 0:
-            vts(A("ak"), A("aj"), 32.0, mul)
-        vcopy(A("bt", 64, 128), A("bc16", 128, 192))
-        if t > 0:
-            vts(A("thr"), A("thr0"), A("ak"), add)
+        if not last:
+            mms("psb1", [(A("psb1", 0, 128), A("BO"), own)])
+            act(A("u1"), A("psb1", 0, 128), scale=1.0 / 32, bias=float(t + 1))
+            copy("g", A("C", made, made + 128), a16)
         if t == 0:
-            act(A("FR0", 640, 1536), ind(A("FR1", 128, 1536), A("FL", 32, 88)), AF.Copy)
+            later_constants(2)
+            later_constants(3)
+            act(A("L", 0, 1024), A("LI"))
+            dma("s", T.lo[0:128:2, :], T.L[0:128:2, 0:1024], [("L", 0, 1024)], [], "out0")
+        if not last:
+            vts(A("ai"), v, 128.0, add)
+        scans(0)
+        if not last:
+            vts(A("al"), A("ai"), 511, band)
+        act(A("ODN"), A("JR"), AF.Identity, scale=OD, bias=A("SF", 32 + t, 33 + t))
 
         scans(1)
-        vtt(A("al1"), A("vB"), A("al0"), add)
-        vts(A("hi"), A("SC", 15, 256, 16), MAG, add, MAG, sub)
-        vtt(A("pkc", 0, 8), K15, A("SC", 15, 128, 16), sub)
-        vtt(A("pkc", 8, 16), K15, A("SC", 143, 256, 16), add)
-        vts(A("al2"), A("al1"), 384, band)
-        vtt(A("of", 0, 8), A("pkc", 0, 8), A("hi", 0, 8), add)
-        vtt(A("of", 8, 16), A("pkc", 8, 16), A("hi", 8, 16), sub)
-        vtt(A("NREF"), A("SC", 15, 128, 16), A("thr"), le)
-        vcopy(A("po"), A("of"))
-        vtt(A("REF"), A("SC", 15, 128, 16), A("thr"), gt)
-        P, Q = A("po", 0, 8), A("po", 8, 16)
-        act(A("sg"), ind(A("dS"), Q), AF.Sign)
-        if not last:
-            act(A("u1"), A("psm", 256, 384), AF.Identity, scale=-1.0, bias=float(t + 1 - 17408))
-        if t > 0:
-            act(A("ODDN"), A("ODDN"), AF.Identity, bias=SF(5))
-            act(A("ODDO"), A("ODDO"), AF.Identity, bias=SF(5))
-        vtt(A("vo"), A("vp"), A("NREF"), mul)
-        vtt(PR(0), ind(A("M1"), Q), A("bt"), mul)
-        vtt(PR(1), ind(A("M1"), P), A("bt"), mul)
-        mms("psb0", [("Z1", 0, 144), ("pr", 0, 2)], to_list("psb0", 0, lambda r: T.pr[:, 0:2, r:128:16], 2))
-        vtt(A("vq"), A("vo"), LIc, add)
-        vtt(PR(2), ind(A("M1"), P), A("af"), mul)
-        vtt(A("nrm"), ind(A("NREF"), A("CL")), A("MKH"), mul)
-        mms("psk", [("Z1", 0, 144), ("pr", 2, 3)], to_list("psk", 256, lambda r: T.pr[:, 2, r:128:16], 1))
-        for nm in ("psd0", "psd1") if last else ("psd0",):
-            mms(nm, [("BO", 0, 128), ("pr", 2, 3), ("nrm", 0, 128)],
-                [(T[nm][:, 0:128], T.BO[:, :], T.pr[:, 2, :], True, False), (T[nm][:, 0:128], T.BO[:, :], T.nrm[:, :], False, True)])
-        vcopy(A("vo16"), A("vq"))
+        vts(A("hi"), A("SC", 15, 256, 16), unit(32), add, unit(32), sub)
+        vtt(A("pk", 0, 8), K15, A("SC", 15, 128, 16), sub)
+        vtt(A("pk", 8, 16), K15, A("SC", 143, 256, 16), add)
+        vtt(P, A("pk", 0, 8), A("hi", 0, 8), add)
+        vtt(Q, A("pk", 8, 16), A("hi", 8, 16), sub)
+        vtt(A("RN", 0, 8), A("SC", 15, 128, 16), A("thr"), gt)
+        vtt(A("RN", 8, 16), A("SC", 15, 128, 16), A("thr"), le)
+        vtt(A("pr", 0, 256), ind(A("M1"), A("po")), A("abc", 0, 256), mul)
+        mms("psd0", to_list(A("psd0", 0, 16), ONE, "pr", 0, 256))
+        mms("psd2", [(A("psd2", 0, 128), A("BO"), A("pr", 0, 128))])
+        vtt(A("dq"), ind(A("yS"), Q), own, sub)
+        act(A("sg"), A("dq"), AF.Sign, bias=-1088.0)
+        vtt(A("pd"), ind(A("RN"), A("CL", 32, 34)), A("PC"), mul)
+        vcopy(A("l16", 0, 16), A("psd0", 0, 16))
+        act(A("er"), ind(A(FRc, 0, made), A("l16", 8, 16)))
+        act(A("apr"), A("psd2", 0, 128), scale=1.0 / 32)
+        vtt(A("vo16"), v, A("pd", 8, 16), mx)
         nw = A("NEW", 128 * t, 128 * t + 128)
-        vtt(nw, A("own"), A("sg"), add)
+        vtt(nw, own, A("sg"), add)
         waits("g", nw[1], [])
         used, transfers = set(), []
         others = sorted([c for c in cores if c != core], key=lambda c: len(topo.engines(core, c)))
@@ -455,93 +416,70 @@ def rank_program(g, core, T, topo):
         total["snt%d" % t] = 12
         note("r", {}, [], [("LAND", 384 * t, 384 * t + 384)], "arr%d" % t, 12)
 
-        vts(A("al3"), A("al2"), 512.0, add)
-        vcopy(A("l16"), A("psb0", 0, 16))
+        vcopy(ind(A(FRc), A("vo16")), A("er"))
+        mms("psk", to_list(A("psk", 0, made // 16), FULL, FRc, 0, made))
+        act(A("LE"), ind(A("L", 0, 1024), A("l16", 0, 8)), scale=EV)
+        compose("a", 512, 896)
+        act(A("FL", 0, made // 16), A("psk", 0, made // 16))
+        for q in range(8):
+            vts(A("EQ", 128 * q, 128 * q + 128), A("apr"), A("psd0", q, q + 1), eq, A("pd", 16 + q, 17 + q), mul)
+            if q % 4 == 3:
+                mms("psd3", [(A("psd3", 0, 128), A("BO"), A("EQ", 128 * j, 128 * j + 128)) for j in range(q - 3, q + 1)],
+                    first=q == 3, last=q == 7)
+        vtt(A("m1"), A("psd0", 0, 8), A("pd", 24, 32), mx)
+        compose("a", 0, 512)
         if not last:
-            vts(A("al4"), A("REF"), float(128 * t), mul)
-        vcopy(A("er"), ind(A(FRc, 128, 1536), A("l16", 0, 8)))
-        if not last:
-            vcopy(A("C", 128 * t, 128 * t + 128), A("a16"))
-            vtt(A("alt"), A("al3"), A("NREF"), mul)
-        act(A("lamA"), A("psk", 256, 264), AF.Copy)
-        vcopy(ind(A(FRc, 0, 1536), A("vo16")), A("er"))
-        if not last:
-            mms("psb1", [("EF", 0, 2048), ("er", 0, 128)],
-                [(T.psb1[:, 384:392], T.EF[:, 128 * r:128 * r + 128], T.er[:, r:128:16], r == 0, r == 15) for r in range(16)])
-        vcopy(A("ap16"), A("psk", 256, 264))
-        if not last:
-            vtt(A("aln"), A("alt"), A("al4"), add)
-        for c in range(4 if last else 8):
-            act(A("DD", 128 * c, 128 * c + 128), A("psd0", 0, 128), AF.Abs, scale=-1.0, bias=A("lamA", c, c + 1))
-        act(A("LE"), ind(A("L", 0, 1024), A("ap16")), AF.Copy, scale=EV)
-        act(A(FRn, 640, 1536), ind(A(FRc, 128, 1536), A("FL", 32, 88)), AF.Copy)
+            vtt(A("pr", 256, 384), ind(A("M1"), P), A("abc", 128, 256), mul)
+            mms("psd1", to_list(A("psd1", 0, 8), ONE, "pr", 256, 384))
+        mms("psm", to_list(A("psm", 0, 56), FULL, FRn, 0, 896))
         if t > 0:
-            act(A(FRn, 128, 128 + 128 * t), ind(A(FRc, 128, 1536), A("FL", 0, 8 * t)), AF.Copy)
-        if not last:
-            vtt(A("wm"), ind(A(FRc, 128, 1536), A("l16", 8, 16)), A("MK"), mul)
-            vtt(A("t0"), A("lamA"), TRc, sub)
-            vscan(A("ws"), A("d0S"), A("wm"), mul, add)
-            vtt(A("t1"), A("t0"), A("REF"), mul)
-            vcopy(A("w16"), A("ws", 15, 128, 16))
-            vtt(A("em"), ind(A(FRc, 128, 1536), A("w16")), A("MK"), mul)
-            vscan(A("es"), A("d0S"), A("em"), mul, add)
-            vtt(A("um"), ind(A("M1"), P), A("u1"), mul)
-            vcopy(A("wi"), A("es", 15, 128, 16))
-            vts(A("gh"), A("es", 15, 128, 16), 1024.0, ge)
-            vts(A("ng"), A("es", 15, 128, 16), 1024.0, lt)
-            vts(A("wB"), A("wi"), 1920, band)
-            vtt(A("cn"), A("um"), A("af"), add)
-            vtt(A("x1"), A("wB"), A("ng"), mul)
-            vts(A("cm"), A("cn"), 1023, band)
-            vtt(A("ga"), A("gh"), A("aln"), mul)
-            vcopy(ind(A("C"), A("v16")), A("cm"))
-            vtt(A("gb"), A("ga"), LIc, add)
-            vcopy(A("e16"), A("psb1", 384, 392))
-        else:
-            vtt(A("em"), A("er"), A("MK"), mul)
-            vtt(A("t0"), A("lamA"), TRc, sub)
-            vscan(A("es"), A("d0S"), A("em"), mul, add)
-            vtt(A("t1"), A("t0"), A("REF"), mul)
-            vcopy(A("e16"), A("es", 15, 128, 16))
-            for c in range(4, 8):
-                vts(A("DD", 128 * c, 128 * c + 128), A("psd1", 0, 128), A("lamA", c, c + 1), ne)
-            room()
-        act(A("fx"), ind(A(FRc, 128, 1536), A("e16")), AF.Copy)
+            compose("a", 896, made)
+            mms("psk", to_list(A("psk", 0, 8 * t), FULL, FRn, 896, made))
         if t == 0:
-            act(A("LO", 0, 1024), A("L", 0, 1024), AF.Copy)
-            dma("s", T.lo[0:128:2, :], T.LO[0:128:2, 0:1024], [("LO", 0, 1024)], [], "out0")
-        vscan(A("DS"), A("d0D"), A("DD"), add, mn)
-        if not last:
-            vtt(A("vf"), A("x1"), A("gb"), add)
-        vtt(A("t2"), A("DS", 127, 1024, 128), TD, ge)
-        if not last:
-            vtt(A("vB"), A("x1"), A("ga"), add)
-            fix()
-        vtt(A("t3"), A("t2"), A("t1"), mul)
-        if not last:
-            room()
-        vtt(A("t4"), A("t3"), TRc, add)
-        if not last:
-            vcopy(ind(A("Y", 0, 1024), A("v16")), nw)
-        vcopy(A("lo16"), A("t4"))
-        if not last:
-            vcopy(A("v16"), A("vf"))
-            vtt(ind(A("L", 0, 1152), A("lo16")), A("LE"), A("ODDN"), add)
-            vcopy(A("a16"), ind(A("C"), A("v16")))
-            act(A("own"), ind(A("Y", 0, 1024), A("v16")), AF.Copy)
+            vcopy(own, nw)
         else:
-            vtt(ind(A("LO", 0, 1152), A("lo16")), A("LE"), A("ODDO"), add)
-            fix()
-            vcopy(ind(A("Y", 0, 1024), A("v16")), nw)
+            vcopy(ind(A("Y", 0, made), v), nw)
+        vtt(A("DD"), A("psd3", 0, 128), A("TM"), gt)
+        if not last:
+            vcopy(A("l16", 16, 24), A("psd1", 0, 8))
+            act(A("hw"), ind(A(FRn, 0, made), A("l16", 16, 24)))
+            mms("psd1", to_list(A("psd1", 0, 8), BLOCK, "hw", 0, 128) + [(A("psd1", 0, 8), A("I"), A("LH"))])
+        act(A("Y", made, made + 128), ind(A("yS"), P), bias=-1088.0)
+        vscan(A("DS"), A("d0D"), A("DD"), mul, mx)
+        if not last:
+            vtt(A("um"), ind(A("M1"), P), A("u1"), mul)
+        vtt(A("m2"), A("DS", 15, 128, 16), A("PC", 24, 32), mul)
+        if not last:
+            vtt(A("mx"), A("al"), A("pd", 0, 8), mx)
+        vtt(A("lo16"), A("m1"), A("m2"), mx)
+        if not last:
+            vtt(A("cn"), A("um"), a16, add)
+            vtt(A("B"), A("mx"), IK, add)
+            vts(A("C", 0, 128) if t == 0 else A("cm"), A("cn"), 1023, band)
+        vtt(ind(A("L"), A("lo16")), A("LE"), A("ODN"), add)
+        if not last:
+            vcopy(A("Y", 512, 896), A("LAND", 384 * t, 384 * t + 384))
+            act(A("FL", 0, 56), A("psm", 0, 56))
+            if t > 0:
+                act(A("FL", 56, 56 + 8 * t), A("psk", 0, 8 * t))
+                vcopy(ind(A("C", 0, made), v), A("cm"))
+            vtt(A("s2"), A("B"), A("psd1", 0, 8), sub)
+            mms("psd2", [(A("psd2", 0, 1), A("BO"), A("RN", q, q + 1)) for q in range(8)] + [(A("psd2", 0, 1), A("BO"), A("cst", 0, 1))])
+            vts(A("PC", 0, 8), A("PC", 0, 8), 128.0, add)
+            vn = A("v16", 8 * t + 8, 8 * t + 16)
+            vtt(vn, A("psd1", 0, 8), A("s2"), mx)
+            act(A("W", 0, made + 128), ind(A("Y", 0, made + 128), A("FL", 0, made // 16 + 8)), scale=0.5)
+            vts(A("ah"), A("psd2", 0, 1), unit(512), add, unit(512), sub)
+            vcopy(a16, ind(A("C", 0, made + 128), vn))
+            vts(A("thr"), A("thr0"), A("psd2", 0, 1), add, A("ah"), sub)
+            act(A("own"), ind(A("Y", 0, made + 128), vn))
         FRc, FRn = FRn, FRc
 
-    dma("s", T.lo[1:128:2, :], T.LO[1:128:2, 0:1024], [("LO", 0, 1024)], [], "out5")
-    dma("s", T.yo[:, 0:512], T.Y[:, 512:1024], [("Y", 512, 1024)], [], "out1")
-    dma("s", T.yo[:, 896:1408], T.Y[:, 0:512], [("Y", 0, 512)], [], "out2")
-    vts(A("FOt"), A("psm", 0, 88), 512.0, lt, 1408.0, mul)
-    vtt(A("FOu"), A("psm", 0, 88), A("FOt"), add)
-    vts(A("FO", 0, 56), A("FOu", 32, 88), -512.0, add)
-    vts(A("FO", 56, 88), A("FOu", 0, 32), -512.0, add)
+    dma("s", T.yo[:, 0:512], T.Y[:, 0:512], [("Y", 0, 512)], [], "out1")
+    dma("s", T.yo[:, 896:1408], T.Y[:, 896:1408], [("Y", 896, 1408)], [], "out2")
+    dma("s", T.lo[1:128:2, :], T.L[1:128:2, 0:1024], [("L", 0, 1024)], [], "out5")
+    act(A("FO", 0, 56), A("psm", 0, 56))
+    act(A("FO", 56, 80), A("psk", 0, 24))
     dma("a", T.fo[:, :], T.FO[:, :], [("FO", 0, 88)], [], "out3")
     p = 384 * (RO - 1)
     dma("s", T.yo[:, 512:896], T.LAND[:, p:p + 384], [("LAND", p, p + 384)], [], "out4")

@@ -2,8 +2,26 @@ from concourse.bass import DstId, RemoteDMATransfer
 from concourse.mybir import AluOpType, ActivationFunctionType
 
 RO = 4
+HOOK = []
 BIG = 262144.0
 F32, BF, I32, U16, F16 = "float32", "bfloat16", "int32", "uint16", "float16"
+OPT = {"links0": "vvav", "links": "vvav", "b": "avaa", "ghost": "vgg", "b16": "av", "nw": "v"}
+ORDER = """
+link0 link1 own link2 lists0 b0 turn link3 nT lists1 h0 fetch1 fetch0 in0 in1 limits_in c0 b1 in2 h1 fetch2 fetch3 room_atoms
+blend0 c1 limits_turn size0 blend1 size1 in3 sums blend2 size2 blend3 in4 blend4 next_room limits sum0 size3 size4 ai consts
+scan0 count limit sum1
+scan1 pkP hi pkQ P Q ref pick yq sign listed er nref pick_b u row al products moved send dummy m1 odd mx list_b
+scatter_f turn_f compose_g list_f compose_b compose_r equal state even flags um first cn m2 B cm turn_n lo scatter_c
+scatter_l hop s2 v list_n ghosts room W atoms
+""".split()
+LAST = """
+link0 link1 own link2 lists0 b0 turn link3 nT lists1 h0 fetch1 fetch0 in0 in1 c0 b1 in2 h1 fetch2 fetch3
+blend0 c1 size0 blend1 size1 in3 sums blend2 size2 blend3 in4 blend4 sum0 size3 size4 scan0 count limit sum1
+scan1 pkP hi pkQ odd P last_rooms Q pick yq sign ref listed er nref products dummy row m1 moved send
+scatter_f even room compose_g turn_f state out_room equal list_f compose_r flags first m2 lo scatter_l out_base compose_b
+out_ghosts turn_n out_f out_links
+""".split()
+PIECES = (("psd0", 0, 2), ("psd1", 2, 2), ("psd2", 4, 2), ("psd3", 6, 1), ("psb0", 7, 1))
 
 
 def unit(u):
@@ -19,19 +37,20 @@ for _n, _c, _d in (
         ("dA", [8, 256], BF), ("own", 128, BF), ("nT", 128, F16), ("u1", 128, F32), ("SC", 256, F32), ("hi", 16, F32),
         ("pk", 16, F32), ("po", 16, U16), ("RN", 16, BF), ("pd", 32, F32), ("pr", 384, F16), ("dq", 128, F16), ("sg", 128, BF),
         ("l16", 24, U16), ("vo16", 8, U16), ("er", 128, BF), ("hw", 128, BF), ("apr", 128, F16), ("EQ", 1024, BF),
-        ("DD", 128, BF), ("DS", 128, BF), ("m1", 8, F32), ("m2", 8, F32), ("lo16", 8, U16), ("LE", 128, F32), ("ODN", 128, F32), ("um", 128, F32),
-        ("cn", 128, I32), ("cm", 128, I32), ("ai", 8, I32), ("al", 8, I32), ("mx", 8, F32), ("B", 8, F32), ("s2", 8, U16),
-        ("thr", 8, F32), ("thr0", 8, F32), ("ah", 1, F32),
+        ("DD", 128, BF), ("DS", 128, BF), ("m1", 8, F32), ("m2", 8, F32), ("lo16", 8, U16), ("LE", 128, F32),
+        ("ODN", 128, F32), ("um", 128, F32), ("cn", 128, I32), ("cm", 128, I32), ("ai", 8, I32), ("al", 8, I32), ("mx", 8, F32),
+        ("B", 8, F32), ("s2", 8, U16), ("thr", 8, F32), ("thr0", 8, F32), ("ah", 1, F32),
         ("T1", 128, I32), ("T1a", 128, I32), ("TK", 128, I32), ("Q16", 88, I32), ("PI", 8, I32), ("JR", 128, BF),
-        ("I", 128, F16), ("M1", 2048, BF), ("M32", 32, BF), ("R", 512, F16), ("EE", [16, 144], F16), ("e1", 128, F16),
-        ("e2", 128, F16), ("BC", 16, BF), ("BO", 128, BF), ("Z", 576, BF), ("ZT", 144, F32), ("d0P", 64, F32), ("d0Q", 64, F32),
-        ("d0D", 128, BF), ("half", 128, F32), ("POW", 128, F32), ("TM", 128, F32), ("TM0", 128, F32), ("PC", 32, F32),
-        ("SF", 64, F32), ("LH", 8, F16), ("CL", 34, U16), ("RB", 12, F32), ("wt", 16, F32), ("cst", 2, BF)):
+        ("I", 128, F16), ("NI", 128, F16), ("M1", 2048, BF), ("M32", 32, BF), ("R", 512, F16), ("EE", [16, 144], F16),
+        ("e1", 128, F16), ("e2", 128, F16), ("BC", 16, BF), ("BO", 128, BF), ("Z", 576, BF), ("ZT", 144, F32),
+        ("d0P", 64, F32), ("d0Q", 64, F32), ("d0D", 128, BF), ("half", 128, F32), ("POW", 128, F32), ("TM", 128, F32),
+        ("TM0", 128, F32), ("PC", 32, F32), ("SF", 64, F32), ("LH", 8, F16), ("CL", 34, U16), ("RB", 12, F32), ("wt", 32, F32),
+        ("cst", 2, BF)):
     SCRATCH[_n] = ("sbuf", [128] + (_c if isinstance(_c, list) else [_c]), _d)
 for _n in ("psb0", "psb1", "psd0", "psd1", "psd2", "psd3", "psk", "psm"):
     SCRATCH[_n] = ("psum", [128, 512], F32)
 
-SEMAPHORES = ["dv", "ac", "pe", "gp"] + ["in%d" % i for i in range(6)] + ["out%d" % i for i in range(6)] + \
+SEMAPHORES = ["dv", "ac", "pe", "gp"] + ["in%d" % i for i in range(8)] + ["out%d" % i for i in range(6)] + \
              ["arr%d" % t for t in range(RO)] + ["snt%d" % t for t in range(RO)]
 
 
@@ -93,12 +112,18 @@ def rank_program(g, core, T, topo):
         count[sem] += 1
         fn().then_inc(T.sem[sem], 1)
         note(e, dict(known[e]), reads, writes, sem, count[sem])
+        HOOK.append(("do", e, reads, writes))
+
+    def dmas(e, pairs, reads, writes, sem):
+        waits(e, reads, writes)
+        for out, in_ in pairs:
+            queues[e].dma_start(out=out, in_=in_).then_inc(T.sem[sem], 16)
+        total[sem] = 16 * len(pairs)
+        note("d", dict(known[e]), reads, writes, sem, total[sem])
+        HOOK.append(("dma", e, reads, writes, len(pairs)))
 
     def dma(e, out, in_, reads, writes, sem):
-        waits(e, reads, writes)
-        queues[e].dma_start(out=out, in_=in_).then_inc(T.sem[sem], 16)
-        total[sem] = 16
-        note("d", dict(known[e]), reads, writes, sem, 16)
+        dmas(e, [(out, in_)], reads, writes, sem)
 
     def A(nm, lo=0, hi=None, st=1, parts=128):
         if hi is None:
@@ -135,11 +160,13 @@ def rank_program(g, core, T, topo):
     def vset(o, c):
         do("v", lambda: g.vector.memset(o[0], c), [], [o])
 
-    def act(o, x, f=AF.Copy, bias=None, scale=None):
+    def act(o, x, f=None, bias=None, scale=None):
         kw = {}
         for key, z in (("bias", bias), ("scale", scale)):
             if z is not None:
                 kw[key] = val(z)
+        if f is None:
+            f = AF.Identity if isinstance(bias, tuple) else AF.Copy
         do("a", lambda: g.scalar.activation(out=o[0], in_=x[0], func=f, **kw), [x, bias, scale], [o])
 
     def copy(e, o, x):
@@ -164,325 +191,349 @@ def rank_program(g, core, T, topo):
         kw = {"allow_small_or_imprecise_dtypes": True} if flag else {}
         do("g", lambda: g.iota(o[0], pattern=pattern, base=base, channel_multiplier=cmul, **kw), [], [o])
 
+    def fill(o, c, flag=True):
+        iota(o, [[0, o[1][0][2] - o[1][0][1]]], c, 0, flag)
+
     def to_list(out, z, nm, lo, hi):
         return [(out, A("Z", 144 * z + 16 - r, 144 * z + 144 - r), A(nm, lo + r, hi, 16)) for r in range(16)]
 
     ONE, X32, FULL, BLOCK = range(4)
-    SF = lambda j, n=1: A("SF", j, j + n)
-    RC, EV, OD, R1, R2, RF, RO2, PW = SF(0), SF(1), SF(2), SF(3), SF(4), SF(5), SF(6), SF(7)
+
+    def SF(j, n=1):
+        return A("SF", j, j + n)
+    RC, EV, OD, R1, R2, RF, RO2, R0, RH = SF(0), SF(1), SF(2), SF(3), SF(4), SF(5), SF(38), SF(36), SF(37)
     LI, K15, IK, ODB = SF(8, 8), SF(16, 8), SF(24, 8), SF(32, 4)
-    R0, RH = SF(36), SF(37)
 
     dma("s", T.LI[:, :], T.lk[:, :], [], [("LI", 0, 1024)], "in0")
     dma("a", T.C[:, 0:128], T.cl[:, 0:128], [], [("C", 0, 128)], "in1")
     dma("a", T.FW[:, :], T.fw0[:, :], [], [("FW", 0, 56)], "in2")
     dma("s", T.Y[:, 0:896], T.y0[:, :], [], [("Y", 0, 896)], "in3")
     dma("a", T.TH8[0:8, :], T.th[:, :], [], [("TH8", 0, 128)], "in5")
-    dma("s", T.C[:, 128:512], T.cl[:, 128:512], [("LI", 0, 1024)], [("C", 128, 512)], "in4")
 
     iota(A("TK"), [[1, 16], [16, 8]], 0, -1)
     iota(A("T1"), [[1, 128]], 128, -1)
     iota(A("PI", 0, 1), [[0, 1]], 0, 1)
     iota(A("Q16"), [[16, 88]], 0, 0)
     iota(A("JR"), [[1, 128]], 0, 0, True)
-    iota(A("C", 512, 896), [[0, 384]], 0, 0)
+    fill(A("ZT", parts=8), 0)
+    fill(A("Z"), 0)
+    fill(A("d0P"), 1)
+    fill(A("d0Q"), -1)
+    fill(A("d0D"), 1)
+    fill(A("TM0"), 0)
+    fill(A("C", 512, 896), 0, False)
 
     vset(A3("EE", T.EE[:, :, :]), 0.0)
     vts(A("e1"), A("TK"), 0, eq, 4096.0, mul)
     vts(A("e2", 0, 88), A("TK", 0, 88), -5, eq)
     vts(A("e2", 88, 128), A("TK", 88, 128), 11, eq)
     vts(A("T1a"), A("T1"), 15, band)
+    vts(A("PI", 1, 2), A("PI", 0, 1), 15, band)
+    vts(A("ai"), A("TK", 120, 128), 4, shr)
+    vts(A("M1", 0, 128), A("T1a"), 0, eq)
+    vcopy(RC, A("PI", 1, 2))
+    vts(A("T1a", 0, 32), A("T1", 0, 32), 31, band)
+    vts(A("CL", 0, 32), A("Q16", 0, 32), 1.0 / 16, mul)
+    vset(A("BC", 8, 16), 0.0)
+    vts(A("M32"), A("T1a", 0, 32), 0, eq)
+    vts(A("BC", 0, 8), A("ai"), 0, eq)
     vts(A("I"), A("T1"), 128, eq)
     vtt(A3("EE", T.EE[:, :, 15:143:16]), A("e1"), A("e2"), add)
-    vts(A("M1", 0, 128), A("T1a"), 0, eq)
-    vts(A("T1a", 0, 32), A("T1", 0, 32), 31, band)
-    vts(A("PI", 1, 2), A("PI", 0, 1), 15, band)
-    vts(A("PI", 2, 3), A("PI", 0, 1), 1, band)
-    vts(A("PI", 3, 4), A("PI", 0, 1), 7, band)
-    vts(A("ai"), A("TK", 120, 128), 4, shr)
-    vts(A("CL", 0, 32), A("Q16", 0, 32), 1.0 / 16, mul)
-    vts(A("M32"), A("T1a", 0, 32), 0, eq)
-    vcopy(RC, A("PI", 1, 2))
-    vset(A("BC", 8, 16), 0.0)
-    vts(A("BC", 0, 8), A("ai"), 0, eq)
-    act(A("R"), ind(A("M32"), A("CL", 0, 32)))
+    vcopy(SF(36, 3), A("M1", 0, 3))
+    vts(RF, RC, 1.0, le)
+    vcopy(A("ZT", 16, 144, 16, parts=8), A("I", 0, 8, parts=8))
     vts(R1, RC, 1.0, ge)
     vts(R2, RC, 2.0, ge, -4096.0, mul)
-    vcopy(SF(36, 2), A("M1", 0, 2))
-    act(A("BO"), ind(A("BC"), A("CL", 0, 8)), scale=32.0)
-    for j in (128, 256, 512, 1024):
-        act(A("M1", j, 2 * j), A("M1", 0, j))
-
-    def later_constants(part):
-        if part == 0:
-            vts(A("RB", 0, 11), A("Q16", 0, 88, 8), R1, mul)
-            vset(A("Z"), 0.0)
-            vts(A("RB", 4, 7), A("Q16", 32, 56, 8), RH, mul, R2, add)
-            vts(LI, A("Q16", 0, 8), RC, add)
-            vts(RF, RC, 1.0, le)
-            vts(RO2, RC, 2.0, eq)
-            for b in range(11):
-                vts(A("FR1", 128 * b, 128 * b + 128), A("JR"), R0, mul, A("RB", b, b + 1), add)
-            for z, s in ((ONE, 1.0), (X32, 32.0), (FULL, RF), (BLOCK, RO2)):
-                vts(A("Z", 144 * z + 16, 144 * z + 144, 16), A("BC", 0, 8), s, mul)
-        if part == 1:
-            vset(A("ZT", parts=8), 0.0)
-            vset(A("d0P"), 1.0)
-            vset(A("d0Q"), -1.0)
-            vcopy(A("ZT", 16, 144, 16, parts=8), A("I", 0, 8, parts=8))
-            vset(A("d0P", 0, 64, 16), -BIG)
-            vset(A("d0Q", 0, 64, 16), BIG)
-            vts(K15, LI, 16.0, mul, 15.0, add)
-            vts(A("v16", 0, 8), A("Q16", 0, 8), RC, add)
-            vts(A("FL", 56, 88), A("Q16", 56, 88), RC, add)
-            vcopy(A("CL", 32, 33), A("PI", 3, 4))
-            vcopy(A("CL", 33, 34), A("PI", 1, 2))
-        if part == 2:
-            vset(A("half"), 0.5)
-            vset(A("d0D"), 1.0)
-            vset(A("TM0"), 0.0)
-            vts(A("PC", 0, 8), LI, 896.0, add)
-            vscan(A("POW"), A("half"), A("TM0"), mul, add, 2.0 ** 65)
-            vset(A("d0D", 0, 128, 16), 0.0)
-            vts(A("PC", 8, 16), LI, 1408.0, add)
-            vts(A("TM0"), A("M1", 0, 128), -1e29, mul, 1e29, add)
-            vtt(A("wt"), A("POW", 64, 80), A("M1", 0, 16), mul)
-            vts(A("half"), A("POW"), 80.0, mul)
-            vts(A("PC", 24, 32), LI, 1024.0, add)
-            vscan(A("lh", 0, 16), A("d0D", 0, 16), A("wt"), mul, add)
-            vtt(A("TM"), A("half"), A("TM0"), mx)
-            vts(A("PC", 16, 24), A("POW", 0, 128, 16), A("lh", 15, 16), mul)
-        if part == 3:
-            vcopy(OD, A("PI", 2, 3))
-            vts(IK, LI, -4096.0, add)
-            vcopy(A("LH"), LI)
-            vts(EV, A("PI", 2, 3), 0, eq)
-            vset(A("cst"), -15.0 / 32)
-            vts(ODB, A("Q16", 56, 88, 8), OD, mul)
-            vcopy(A("FR0", 896, 1408), A("FR1", 896, 1408))
-            vts(A("FO", 80, 88), LI, 1280.0, add)
-
-    later_constants(0)
-    later_constants(1)
+    vts(A("PI", 2, 3), A("PI", 0, 1), 1, band)
+    vts(A("PI", 3, 4), A("PI", 0, 1), 7, band)
+    vts(A("RB", 0, 11), A("Q16", 0, 88, 8), R1, mul)
+    vcopy(OD, A("PI", 2, 3))
+    vts(A("RB", 4, 7), A("Q16", 32, 56, 8), RH, mul, R2, add)
+    vts(EV, A("PI", 2, 3), 0, eq)
+    for b in range(11):
+        vts(A("FR1", 128 * b, 128 * b + 128), A("JR"), R0, mul, A("RB", b, b + 1), add)
     vcopy(A("FL", 0, 56), A("FW"))
     vcopy(A("abc", 0, 128), A("C", 0, 128))
-    act(A("THF", parts=8), A("TH8", parts=8), scale=32.0, bias=15.0)
-    act(A("FR0", 0, 896), ind(A("FR1", 0, 896), A("FL", 0, 56)))
-    mms("psk", [(A("psk", 0, 8), A("ZT", 16 - r, 144 - r, parts=8), A("THF", r, 128, 16, parts=8)) for r in range(16)])
+
+    dmas("s", [(T.M1[:, 128 * j:128 * j + 128], T.M1[:, 0:128]) for j in (1, 2, 3)], [("M1", 0, 128)], [("M1", 128, 512)], "in6")
+    dma("s", T.C[:, 128:512], T.cl[:, 128:512], [("LI", 0, 1024)], [("C", 128, 512)], "in4")
+    dmas("s", [(T.M1[:, 512 * j:512 * j + 512], T.M1[:, 0:512]) for j in (1, 2, 3)], [("M1", 0, 512)], [("M1", 512, 2048)], "in7")
+
+    act(LI, A("Q16", 0, 8), bias=RC)
+    act(A("v16", 0, 8), A("Q16", 0, 8), bias=RC)
+    act(A("FL", 56, 88), A("Q16", 56, 88), bias=RC)
+    act(A("R"), ind(A("M32"), A("CL", 0, 32)))
+    act(A("BO"), ind(A("BC"), A("CL", 0, 8)), scale=32.0)
+    act(K15, LI, scale=16.0, bias=15.0)
+    for o, c in ((A("PC", 0, 8), 896.0), (A("PC", 8, 16), 1408.0), (A("PC", 24, 32), 1024.0), (IK, -4096.0), (A("LH"), 0.0)):
+        act(o, LI, bias=c)
+    for z, s in ((ONE, 1.0), (X32, 32.0), (FULL, RF), (BLOCK, RO2)):
+        act(A("Z", 144 * z + 16, 144 * z + 144, 16), A("BC", 0, 8), scale=s)
     act(A("W", 0, 896), ind(A("Y", 0, 896), A("FL", 0, 56)), scale=0.5)
 
-    FRc, FRn = "FR0", "FR1"
-    for t in range(RO):
-        last = t == RO - 1
-        made = 896 + 128 * t
-        v = A("v16", 8 * t, 8 * t + 8)
-        own = A("Y", 0, 128) if t == 0 else A("own")
-        a16, P, Q = A("abc", 0, 128), A("po", 0, 8), A("po", 8, 16)
+    def later_constants():
+        vset(A("half"), 0.5)
+        vset(A("d0D", 0, 128, 16), 0.0)
+        vcopy(A("CL", 32, 33), A("PI", 3, 4))
+        vscan(A("POW"), A("half"), A("TM0"), mul, add, 2.0 ** 65)
+        vcopy(A("CL", 33, 34), A("PI", 1, 2))
+        vts(A("TM0"), A("M1", 0, 128), -1e29, mul, 1e29, add)
+        vtt(A("wt", 0, 16), A("POW", 64, 80), A("M1", 0, 16), mul)
+        vts(A("half"), A("POW"), 80.0, mul)
+        vscan(A("wt", 16, 32), A("d0D", 0, 16), A("wt", 0, 16), mul, add)
+        vtt(A("TM"), A("half"), A("TM0"), mx)
+        vts(A("PC", 16, 24), A("POW", 0, 128, 16), A("wt", 31, 32), mul)
+        vset(A("cst"), -15.0 / 32)
+        act(A("FR0", 0, 896), ind(A("FR1", 0, 896), A("FL", 0, 56)))
+        act(A("L", 0, 1024), A("LI"))
+        dma("s", T.lo[0:128:2, :], T.L[0:128:2, 0:1024], [("L", 0, 1024)], [], "out0")
 
-        def links(e, q):
-            copy(e, A("Lg", 512 * q, 512 * q + 512), ind(A("LI") if t == 0 else A("L", 0, 1024), A("abc", 32 * q, 32 * q + 32)))
+    def one_round(t, FRc, FRn):
+        first, last = t == 0, t == RO - 1
+        made = 896 + 128 * t
+        v, vn = A("v16", 8 * t, 8 * t + 8), A("v16", 8 * t + 8, 8 * t + 16) if not last else None
+        own = A("Y", 0, 128) if first else A("own")
+        a16, P, Q = A("abc", 0, 128), A("po", 0, 8), A("po", 8, 16)
+        nw = A("NEW", 128 * t, 128 * t + 128)
+        big = A("SC", 15, 128, 16)
+
+        def link(q):
+            e = OPT["links0" if first else "links"][q]
+            copy(e, A("Lg", 512 * q, 512 * q + 512), ind(A("LI") if first else A("L", 0, 1024), A("abc", 32 * q, 32 * q + 32)))
 
         def lists(h):
             mms("psb%d" % h, [(A("psb%d" % h, 0, 64), A3("EE", T.EE[:, k, 15 - k:143 - k]), A("Lg", 1024 * h + k, 1024 * h + 1024, 16))
                               for k in range(16)])
 
-        def lists_out(h):
-            ps = A("psb%d" % h, 0, 64)
-            vts(A("abc", 128 + 64 * h, 192 + 64 * h), ps, 1.0 / 4096, mul)
-            vts(A("lh", 64 * h, 64 * h + 64), ps, unit(4096), add, unit(4096), sub)
+        def list_b(h):
+            o, ps = A("abc", 128 + 64 * h, 192 + 64 * h), A("psb%d" % h, 0, 64)
+            if OPT["b16"][h] == "a":
+                act(o, ps, scale=1.0 / 4096)
+            else:
+                vts(o, ps, 1.0 / 4096, mul)
 
-        def lists_c(h):
+        def list_h(h):
+            vts(A("lh", 64 * h, 64 * h + 64), A("psb%d" % h, 0, 64), unit(4096), add, unit(4096), sub)
+
+        def list_c(h):
             vtt(A("abc", 256 + 64 * h, 320 + 64 * h), A("psb%d" % h, 0, 64), A("lh", 64 * h, 64 * h + 64), sub)
 
         def own_in(n):
-            part = slice(32 * n, 32 * n + 32)
-            mms("psd%d" % n, [(A("psd%d" % n), A3("nT", T.nT[part, :]), A3("R", T.R[part, :]))], last=False)
+            bank, q, k = PIECES[n]
+            part, o = slice(32 * (q // 2), 32 * (q // 2) + 32), 256 * (q % 2)
+            mms(bank, [(A(bank, 0, 256 * k), A3("nT", T.nT[part, :]), A3("R", T.R[part, o:o + 256 * k]))], last=False)
 
-        def blend_b(e, n):
+        def fetch(n):
             o, x = A("xb", 512 * n, 512 * n + 512), ind(A("W", 0, made), A("abc", 128 + 32 * n, 160 + 32 * n))
-            if e == "a":
+            if OPT["b"][n] == "a":
                 act(o, x, bias=1087.75)
             else:
                 vts(o, x, 1087.75, add)
 
-        def blend_c(n):
-            y = A("y16", 512 * n, 512 * n + 512)
-            vtt(y, ind(A("W", 0, made), A("abc", 256 + 32 * n, 288 + 32 * n)), A("xb", 512 * n, 512 * n + 512), add)
-            mms("psd%d" % n, [(A("psd%d" % n), A("I"), y)], first=False)
-            copy("g", A("yS", 512 * n, 512 * n + 512), y)
+        def blend(n):
+            bank, q, k = PIECES[n]
+            lo, hi = 256 * q, 256 * (q + k)
+            vtt(A("y16", lo, hi), ind(A("W", 0, made), A("abc", 256 + lo // 16, 256 + hi // 16)), A("xb", lo, hi), add)
+            mms(bank, [(A(bank, 0, hi - lo), A("I"), A("y16", lo, hi))], first=False)
+            copy("g", A("yS", lo, hi), A("y16", lo, hi))
 
-        def size_d(n):
-            act((T.dA[:, 2 * n:2 * n + 2, :], [("dA", 2 * n, 2 * n + 2)], []), A("psd%d" % n), AF.Abs)
+        def size(n):
+            bank, q, k = PIECES[n]
+            act((T.dA[:, q:q + k, :], [("dA", q, q + k)], []), A(bank, 0, 256 * k), AF.Abs)
 
-        def sum_d(h):
+        def sums(h):
             bank = "psm" if h else "psk"
             mms(bank, [(A(bank, 0, 64), A("Z", 144 * X32 + 16 - r, 144 * X32 + 144 - r),
                         (T.dA[:, 4 * h:4 * h + 4, 16 * r:16 * r + 16], [("dA", 4 * h, 4 * h + 4)], [])) for r in range(16)])
 
-        def scans(h):
+        def scan(h):
             bank, o = ("psm" if h else "psk"), 64 * h
+            if first and h == 0:
+                vset(A("d0P", 0, 64, 16), -BIG)
+                vset(A("d0Q", 0, 64, 16), BIG)
             vscan(A("SC", o, o + 64), A("d0P"), A(bank, 0, 64), add, mx)
             vscan(A("SC", 128 + o, 192 + o), A("d0Q"), A(bank, 0, 64), add, mn)
 
         def compose(e, lo, hi):
-            copy(e, A(FRn, lo, hi), ind(A(FRc, 0, made), A("FL", lo // 16, hi // 16)))
+            if hi > lo:
+                copy(e, A(FRn, lo, hi), ind(A(FRc, 0, made), A("FL", lo // 16, hi // 16)))
 
-        links("v", 0)
-        mms("psb1", [(A("psb1", 0, 128), own, A("I"))])
-        act(A("nT"), A("psb1", 0, 128), scale=-1.0, bias=-1088.0)
-        links("v", 1)
-        lists(0)
-        own_in(0)
-        own_in(1)
-        links("a", 2)
-        links("v", 3)
-        if t == 0:
-            vcopy(A("thr"), A("psk", 0, 8))
-            vts(A("thr0"), A("psk", 0, 8), 240.0, add)
-        lists_out(0)
-        lists(1)
-        own_in(2)
-        own_in(3)
-        blend_b("a", 0)
-        lists_c(0)
-        blend_b("v", 1)
-        lists_out(1)
-        blend_b("a", 2)
-        blend_c(0)
-        lists_c(1)
-        blend_b("a", 3)
-        blend_c(1)
-        size_d(0)
-        blend_c(2)
-        size_d(1)
-        sum_d(0)
-        blend_c(3)
-        size_d(2)
-        size_d(3)
-        sum_d(1)
-        if not last:
-            mms("psb1", [(A("psb1", 0, 128), A("BO"), own)])
-            act(A("u1"), A("psb1", 0, 128), scale=1.0 / 32, bias=float(t + 1))
-            copy("g", A("C", made, made + 128), a16)
-        if t == 0:
-            later_constants(2)
-            later_constants(3)
-            act(A("L", 0, 1024), A("LI"))
-            dma("s", T.lo[0:128:2, :], T.L[0:128:2, 0:1024], [("L", 0, 1024)], [], "out0")
-        if not last:
-            vts(A("ai"), v, 128.0, add)
-        scans(0)
-        if not last:
-            vts(A("al"), A("ai"), 511, band)
-        act(A("ODN"), A("JR"), AF.Identity, scale=OD, bias=A("SF", 32 + t, 33 + t))
+        def turn():
+            mms("psb1", [(A("psb1", 0, 128), own, A("I"))])
 
-        scans(1)
-        vts(A("hi"), A("SC", 15, 256, 16), unit(32), add, unit(32), sub)
-        vtt(A("pk", 0, 8), K15, A("SC", 15, 128, 16), sub)
-        vtt(A("pk", 8, 16), K15, A("SC", 143, 256, 16), add)
-        vtt(P, A("pk", 0, 8), A("hi", 0, 8), add)
-        vtt(Q, A("pk", 8, 16), A("hi", 8, 16), sub)
-        vtt(A("RN", 0, 8), A("SC", 15, 128, 16), A("thr"), gt)
-        vtt(A("RN", 8, 16), A("SC", 15, 128, 16), A("thr"), le)
-        vtt(A("pr", 0, 256), ind(A("M1"), A("po")), A("abc", 0, 256), mul)
-        mms("psd0", to_list(A("psd0", 0, 16), ONE, "pr", 0, 256))
-        mms("psd2", [(A("psd2", 0, 128), A("BO"), A("pr", 0, 128))])
-        vtt(A("dq"), ind(A("yS"), Q), own, sub)
-        act(A("sg"), A("dq"), AF.Sign, bias=-1088.0)
-        vtt(A("pd"), ind(A("RN"), A("CL", 32, 34)), A("PC"), mul)
-        vcopy(A("l16", 0, 16), A("psd0", 0, 16))
-        act(A("er"), ind(A(FRc, 0, made), A("l16", 8, 16)))
-        act(A("apr"), A("psd2", 0, 128), scale=1.0 / 32)
-        vtt(A("vo16"), v, A("pd", 8, 16), mx)
-        nw = A("NEW", 128 * t, 128 * t + 128)
-        vtt(nw, own, A("sg"), add)
-        waits("g", nw[1], [])
-        used, transfers = set(), []
-        others = sorted([c for c in cores if c != core], key=lambda c: len(topo.engines(core, c)))
-        for c in others:
-            fewest = topo.engines(core, others[0])
-            eng = [e for e in topo.engines(core, c) if e not in used]
-            if len(topo.engines(core, c)) > len(fewest):
-                eng = [e for e in eng if e not in fewest]
-            eng = eng[:4]
-            used.update(eng)
-            s = (rank - T.rank_of(c) - 1) % len(cores)
-            rid, pid = topo.addr(c, core)
-            transfers.append(RemoteDMATransfer(dst_ids=[DstId(rid=rid, pnc=pid)], dma_engine_mask=sum(1 << e for e in eng),
-                                               remote_sem=T.sem["arr%d" % t], src=nw[0],
-                                               dst=T.LAND[:, 384 * t + 128 * s:384 * t + 128 * s + 128]))
-        g.remote_dma_fused(transfers, local_sem=T.sem["snt%d" % t])
-        total["arr%d" % t] = 12
-        total["snt%d" % t] = 12
-        note("r", {}, [], [("LAND", 384 * t, 384 * t + 384)], "arr%d" % t, 12)
+        def states_sum():
+            ps = A("psb1", 128, 129)
+            mms("psb1", ([] if last else [(A("psb1", 0, 128), A("BO"), own)])
+                + ([] if first else [(ps, A("BO"), A("RN", q, q + 1)) for q in range(8)] + [(ps, A("BO"), A("cst", 0, 1))]))
 
-        vcopy(ind(A(FRc), A("vo16")), A("er"))
-        mms("psk", to_list(A("psk", 0, made // 16), FULL, FRc, 0, made))
-        act(A("LE"), ind(A("L", 0, 1024), A("l16", 0, 8)), scale=EV)
-        compose("a", 512, 896)
-        act(A("FL", 0, made // 16), A("psk", 0, made // 16))
-        for q in range(8):
-            vts(A("EQ", 128 * q, 128 * q + 128), A("apr"), A("psd0", q, q + 1), eq, A("pd", 16 + q, 17 + q), mul)
-            if q % 4 == 3:
-                mms("psd3", [(A("psd3", 0, 128), A("BO"), A("EQ", 128 * j, 128 * j + 128)) for j in range(q - 3, q + 1)],
-                    first=q == 3, last=q == 7)
-        vtt(A("m1"), A("psd0", 0, 8), A("pd", 24, 32), mx)
-        compose("a", 0, 512)
-        if not last:
+        def limits():
+            if first:
+                vcopy(A("thr"), A("psk", 0, 8))
+                vts(A("thr0"), A("psk", 0, 8), 240.0, add)
+
+        def limits_in():
+            if first:
+                act(A("THF", parts=8), A("TH8", parts=8), scale=32.0, bias=15.0)
+
+        def limits_turn():
+            if first:
+                mms("psk", [(A("psk", 0, 8), A("ZT", 16 - r, 144 - r, parts=8), A("THF", r, 128, 16, parts=8)) for r in range(16)])
+
+        def out_f():
+            act(A("FO", 0, 80), A("psk", 0, 80))
+            dma("a", T.fo[:, :], T.FO[:, :], [("FO", 0, 88)], [], "out3")
+
+        def counted():
+            if first:
+                vcopy(A("FR0", 896, 1408), A("FR1", 896, 1408))
+                vts(ODB, A("Q16", 56, 88, 8), OD, mul)
+            else:
+                vts(A("ah"), A("psb1", 128, 129), unit(512), add, unit(512), sub)
+
+        def pick():
+            vtt(A("pr", 0, 256), ind(A("M1"), A("po")), A("abc", 0, 256), mul)
+            mms("psd0", to_list(A("psd0", 0, 16), ONE, "pr", 0, 256))
+
+        def pick_b():
             vtt(A("pr", 256, 384), ind(A("M1"), P), A("abc", 128, 256), mul)
             mms("psd1", to_list(A("psd1", 0, 8), ONE, "pr", 256, 384))
-        mms("psm", to_list(A("psm", 0, 56), FULL, FRn, 0, 896))
-        if t > 0:
-            compose("a", 896, made)
-            mms("psk", to_list(A("psk", 0, 8 * t), FULL, FRn, 896, made))
-        if t == 0:
-            vcopy(own, nw)
-        else:
-            vcopy(ind(A("Y", 0, made), v), nw)
-        vtt(A("DD"), A("psd3", 0, 128), A("TM"), gt)
-        if not last:
-            vcopy(A("l16", 16, 24), A("psd1", 0, 8))
+
+        def row():
+            mms("psd2", [(A("psd2", 0, 128), A("BO"), A("pr", 0, 128))])
+            act(A("apr"), A("psd2", 0, 128), scale=1.0 / 32)
+
+        def send():
+            waits("g", nw[1], [])
+            used, transfers = set(), []
+            others = sorted([c for c in cores if c != core], key=lambda c: len(topo.engines(core, c)))
+            for c in others:
+                fewest = topo.engines(core, others[0])
+                eng = [e for e in topo.engines(core, c) if e not in used]
+                if len(topo.engines(core, c)) > len(fewest):
+                    eng = [e for e in eng if e not in fewest]
+                eng = eng[:4]
+                used.update(eng)
+                s = (rank - T.rank_of(c) - 1) % len(cores)
+                rid, pid = topo.addr(c, core)
+                transfers.append(RemoteDMATransfer(dst_ids=[DstId(rid=rid, pnc=pid)], dma_engine_mask=sum(1 << e for e in eng),
+                                                   remote_sem=T.sem["arr%d" % t], src=nw[0],
+                                                   dst=T.LAND[:, 384 * t + 128 * s:384 * t + 128 * s + 128]))
+            g.remote_dma_fused(transfers, local_sem=T.sem["snt%d" % t])
+            total["arr%d" % t] = 12
+            total["snt%d" % t] = 12
+            note("r", {}, [], [("LAND", 384 * t, 384 * t + 384)], "arr%d" % t, 12)
+            HOOK.append(("rdma", "g", nw[1], [("LAND", 384 * t, 384 * t + 384)]))
+
+        def equal():
+            for q in range(8):
+                vts(A("EQ", 128 * q, 128 * q + 128), A("apr"), A("psd0", q, q + 1), eq, A("pd", 16 + q, 17 + q), mul)
+                if q % 4 == 3:
+                    mms("psd3", [(A("psd3", 0, 128), A("BO"), A("EQ", 128 * j, 128 * j + 128)) for j in range(q - 3, q + 1)],
+                        first=q == 3, last=q == 7)
+
+        def hop():
             act(A("hw"), ind(A(FRn, 0, made), A("l16", 16, 24)))
             mms("psd1", to_list(A("psd1", 0, 8), BLOCK, "hw", 0, 128) + [(A("psd1", 0, 8), A("I"), A("LH"))])
-        act(A("Y", made, made + 128), ind(A("yS"), P), bias=-1088.0)
-        vscan(A("DS"), A("d0D"), A("DD"), mul, mx)
-        if not last:
-            vtt(A("um"), ind(A("M1"), P), A("u1"), mul)
-        vtt(A("m2"), A("DS", 15, 128, 16), A("PC", 24, 32), mul)
-        if not last:
-            vtt(A("mx"), A("al"), A("pd", 0, 8), mx)
-        vtt(A("lo16"), A("m1"), A("m2"), mx)
-        if not last:
-            vtt(A("cn"), A("um"), a16, add)
-            vtt(A("B"), A("mx"), IK, add)
-            vts(A("C", 0, 128) if t == 0 else A("cm"), A("cn"), 1023, band)
-        vtt(ind(A("L"), A("lo16")), A("LE"), A("ODN"), add)
-        if not last:
-            vcopy(A("Y", 512, 896), A("LAND", 384 * t, 384 * t + 384))
-            act(A("FL", 0, 56), A("psm", 0, 56))
-            if t > 0:
-                act(A("FL", 56, 56 + 8 * t), A("psk", 0, 8 * t))
-                vcopy(ind(A("C", 0, made), v), A("cm"))
-            vtt(A("s2"), A("B"), A("psd1", 0, 8), sub)
-            mms("psd2", [(A("psd2", 0, 1), A("BO"), A("RN", q, q + 1)) for q in range(8)] + [(A("psd2", 0, 1), A("BO"), A("cst", 0, 1))])
-            vts(A("PC", 0, 8), A("PC", 0, 8), 128.0, add)
-            vn = A("v16", 8 * t + 8, 8 * t + 16)
-            vtt(vn, A("psd1", 0, 8), A("s2"), mx)
-            act(A("W", 0, made + 128), ind(A("Y", 0, made + 128), A("FL", 0, made // 16 + 8)), scale=0.5)
-            vts(A("ah"), A("psd2", 0, 1), unit(512), add, unit(512), sub)
-            vcopy(a16, ind(A("C", 0, made + 128), vn))
-            vts(A("thr"), A("thr0"), A("psd2", 0, 1), add, A("ah"), sub)
-            act(A("own"), ind(A("Y", 0, made + 128), vn))
-        FRc, FRn = FRn, FRc
 
-    dma("s", T.yo[:, 0:512], T.Y[:, 0:512], [("Y", 0, 512)], [], "out1")
-    dma("s", T.yo[:, 896:1408], T.Y[:, 896:1408], [("Y", 896, 1408)], [], "out2")
-    dma("s", T.lo[1:128:2, :], T.L[1:128:2, 0:1024], [("L", 0, 1024)], [], "out5")
-    act(A("FO", 0, 56), A("psm", 0, 56))
-    act(A("FO", 56, 80), A("psk", 0, 24))
-    dma("a", T.fo[:, :], T.FO[:, :], [("FO", 0, 88)], [], "out3")
-    p = 384 * (RO - 1)
-    dma("s", T.yo[:, 512:896], T.LAND[:, p:p + 384], [("LAND", p, p + 384)], [], "out4")
+        def state():
+            vcopy(own if first else ind(A("Y", 0, made), v), nw)
+
+        S = OPT["nw"] == "s"
+        steps = {
+            "own": lambda: first or act(A("own"), ind(A("Y", 0, made), v)),
+            "turn": turn,
+            "nT": lambda: act(A("nT"), A("psb1", 0, 128), scale=-1.0, bias=-1088.0),
+            "consts": lambda: first and later_constants(),
+            "odd": lambda: act(A("ODN"), A("JR"), scale=OD, bias=SF(32 + t)),
+            "count": counted,
+            "limit": lambda: first or vts(A("thr"), A("thr0"), A("psb1", 128, 129), add, A("ah"), sub),
+            "limits": limits,
+            "limits_in": limits_in,
+            "limits_turn": limits_turn,
+            "sums": states_sum,
+            "hi": lambda: vts(A("hi"), A("SC", 15, 256, 16), unit(32), add, unit(32), sub),
+            "pkP": lambda: vtt(A("pk", 0, 8), K15, big, sub),
+            "pkQ": lambda: vtt(A("pk", 8, 16), K15, A("SC", 143, 256, 16), add),
+            "P": lambda: vtt(P, A("pk", 0, 8), A("hi", 0, 8), add),
+            "Q": lambda: vtt(Q, A("pk", 8, 16), A("hi", 8, 16), sub),
+            "ref": lambda: vtt(A("RN", 0, 8), big, A("thr"), gt),
+            "nref": lambda: vtt(A("RN", 8, 16), big, A("thr"), le),
+            "products": lambda: vtt(A("pd"), ind(A("RN"), A("CL", 32, 34)), A("PC"), mul),
+            "pick": pick,
+            "row": row,
+            "yq": lambda: act(A("dq"), ind(A("yS"), Q), bias=-1088.0) if S else vtt(A("dq"), ind(A("yS"), Q), own, sub),
+            "less": lambda: S and mms("psb1", [(A("psb1", 0, 128), A("I"), A("dq")), (A("psb1", 0, 128), A("NI"), own)]),
+            "sign": lambda: act(A("sg"), A("psb1", 0, 128), AF.Sign) if S else act(A("sg"), A("dq"), AF.Sign, bias=-1088.0),
+            "more": lambda: OPT["nw"] != "v" and mms("psb0", [(A("psb0", 0, 128), A("I"), A("sg")), (A("psb0", 0, 128), A("I"), own)]),
+            "moved": lambda: act(nw, A("psb0", 0, 128)) if OPT["nw"] != "v" else vtt(nw, own, A("sg"), add),
+            "listed": lambda: act(A("l16", 0, 16), A("psd0", 0, 16)),
+            "er": lambda: act(A("er"), ind(A(FRc, 0, made), A("l16", 8, 16))),
+            "dummy": lambda: vtt(A("vo16"), v, A("pd", 8, 16), mx),
+            "send": send,
+            "scatter_f": lambda: vcopy(ind(A(FRc), A("vo16")), A("er")),
+            "turn_f": lambda: mms("psk", to_list(A("psk", 0, made // 16), FULL, FRc, 0, made)),
+            "even": lambda: act(A("LE"), ind(A("L", 0, 1024), A("l16", 0, 8)), scale=EV),
+            "compose_g": lambda: compose("a", 512, 896),
+            "list_f": lambda: act(A("FL", 0, made // 16), A("psk", 0, made // 16)),
+            "equal": equal,
+            "m1": lambda: vtt(A("m1"), A("psd0", 0, 8), A("pd", 24, 32), mx),
+            "compose_b": lambda: compose("a", 0, 512),
+            "compose_r": lambda: compose("v" if last else "a", 896, made),
+            "flags": lambda: vtt(A("DD"), A("psd3", 0, 128), A("TM"), gt),
+            "turn_n": lambda: mms("psk", to_list(A("psk", 0, made // 16), FULL, FRn, 0, made)),
+            "room": lambda: act(A("Y", made, made + 128), ind(A("yS"), P), bias=-1088.0),
+            "first": lambda: vscan(A("DS"), A("d0D"), A("DD"), mul, mx),
+            "m2": lambda: vtt(A("m2"), A("DS", 15, 128, 16), A("PC", 24, 32), mul),
+            "lo": lambda: vtt(A("lo16"), A("m1"), A("m2"), mx),
+            "state": state,
+            "scatter_l": lambda: vtt(ind(A("L"), A("lo16")), A("LE"), A("ODN"), add),
+        }
+        for j in range(5):
+            for name, fn in (("link", link), ("lists", lists), ("b", list_b), ("h", list_h), ("c", list_c), ("in", own_in),
+                             ("fetch", fetch), ("blend", blend), ("size", size), ("sum", sums), ("scan", scan)):
+                steps[name + str(j)] = lambda fn=fn, j=j: fn(j)
+        if not last:
+            steps.update({
+                "room_atoms": lambda: copy("g", A("C", made, made + 128), a16),
+                "u": lambda: act(A("u1"), A("psb1", 0, 128), scale=1.0 / 32, bias=float(t + 1)),
+                "ai": lambda: act(A("ai"), v, bias=128.0),
+                "al": lambda: vts(A("al"), A("ai"), 511, band),
+                "next_room": lambda: first or vts(A("PC", 0, 8), A("PC", 0, 8), 128.0, add),
+                "pick_b": pick_b,
+                "list_b": lambda: act(A("l16", 16, 24), A("psd1", 0, 8)),
+                "um": lambda: vtt(A("um"), ind(A("M1"), P), A("u1"), mul),
+                "cn": lambda: vtt(A("cn"), A("um"), a16, add),
+                "cm": lambda: vts(A("C", 0, 128) if first else A("cm"), A("cn"), 1023, band),
+                "scatter_c": lambda: first or vcopy(ind(A("C", 0, made), v), A("cm")),
+                "hop": hop,
+                "mx": lambda: vtt(A("mx"), A("al"), A("pd", 0, 8), mx),
+                "B": lambda: vtt(A("B"), A("mx"), IK, add),
+                "ghosts": lambda: copy(OPT["ghost"][t], A("Y", 512, 896), A("LAND", 384 * t, 384 * t + 384)),
+                "list_n": lambda: act(A("FL", 0, made // 16), A("psk", 0, made // 16)),
+                "W": lambda: act(A("W", 0, made + 128), ind(A("Y", 0, made + 128), A("FL", 0, made // 16 + 8)), scale=0.5),
+                "s2": lambda: vtt(A("s2"), A("B"), A("psd1", 0, 8), sub),
+                "v": lambda: vtt(vn, A("psd1", 0, 8), A("s2"), mx),
+                "atoms": lambda: vcopy(a16, ind(A("C", 0, made + 128), vn)),
+            })
+        else:
+            steps.update({
+                "out_base": lambda: dma("s", T.yo[:, 0:512], T.Y[:, 0:512], [("Y", 0, 512)], [], "out1"),
+                "out_room": lambda: dma("s", T.yo[:, 896:1408], T.Y[:, 896:1408], [("Y", 896, 1408)], [], "out2"),
+                "out_links": lambda: dma("s", T.lo[1:128:2, :], T.L[1:128:2, 0:1024], [("L", 0, 1024)], [], "out5"),
+                "out_ghosts": lambda: dma("s", T.yo[:, 512:896], T.LAND[:, 384 * t:384 * t + 384], [("LAND", 384 * t, 384 * t + 384)],
+                                          [], "out4"),
+                "last_rooms": lambda: act(A("FO", 80, 88), LI, bias=1280.0),
+                "out_f": out_f,
+            })
+        for name in LAST if last else ORDER:
+            if name in steps:
+                HOOK.append(("step", t, name))
+                steps[name]()
+        HOOK.append(("step", -1, "end"))
+
+    for t in range(RO):
+        one_round(t, "FR%d" % (t % 2), "FR%d" % (1 - t % 2))
+
     for sem in ("dv", "ac", "pe", "gp"):
         g.wait_ge(T.sem[sem], count[sem])
     for sem in sorted(total):

@@ -3,25 +3,44 @@ from concourse.mybir import AluOpType, ActivationFunctionType
 
 RO = 4
 HOOK = []
-BIG = 262144.0
+OPT = {}
+BIG, LIFT = 1048576.0, 262144.0
 F32, BF, I32, U16, F16 = "float32", "bfloat16", "int32", "uint16", "float16"
-OPT = {"links0": "vvav", "links": "vvav", "b": "avaa", "ghost": "vgg", "b16": "av", "nw": "v"}
-ORDER = """
-link0 link1 own link2 lists0 b0 turn link3 nT lists1 h0 fetch1 fetch0 in0 in1 limits_in c0 b1 in2 h1 fetch2 fetch3 room_atoms
-blend0 c1 limits_turn size0 blend1 size1 in3 sums blend2 size2 blend3 in4 blend4 next_room limits sum0 size3 size4 ai consts
-scan0 count limit sum1
-scan1 pkP hi pkQ P Q ref pick yq sign listed er nref pick_b u row al products moved send dummy m1 odd mx list_b
-scatter_f turn_f compose_g list_f compose_b compose_r equal state even flags um first cn m2 B cm turn_n lo scatter_c
-scatter_l hop s2 v list_n ghosts room W atoms
+START = """
+g_p g_q g_m g_j k_zero k_places k_list k_lanes k_atoms k_lanes2 k_m32 k_diagonal k_unit g_z g_g k_pick k_turn8 k_steps k_fills
+k_links@g link2 link0 k_parts k_numbers@v k_odd@v link3@v lists1 own@v k_groups W2@v W1@v link1 lists0 turn k_rows W0
+k_thresholds@v b1@v h1 k_sums@v b0 fetch5 c1 k_spread@v k_rows2 h0 fetch1 k_load k_ones k_ones2 out_even fetch0 nT fetch2
+k_scans c0 ai@v k_small in4 in3 blend4 blend3 k_limits size4 k_block in1 in0 size3 blend1 blend0 in2 size1 size0 blend2 rows0
+in5 blend5 k_turns@v k_weights srow0 sum0 size2 k_spare scan0 size5 keep3 keep4 room_atoms@g af@g keep0@g keep1@g keep2@g
+room_f wrap rows1 sum1 k_forwards sums delta srow1 scan1 al low al2 k_clusters
 """.split()
-LAST = """
-link0 link1 own link2 lists0 b0 turn link3 nT lists1 h0 fetch1 fetch0 in0 in1 c0 b1 in2 h1 fetch2 fetch3
-blend0 c1 size0 blend1 size1 in3 sums blend2 size2 blend3 in4 blend4 sum0 size3 size4 scan0 count limit sum1
-scan1 pkP hi pkQ odd P last_rooms Q pick yq sign ref listed er nref products dummy row m1 moved send
-scatter_f even room compose_g turn_f state out_room equal list_f compose_r flags first m2 lo scatter_l out_base compose_b
-out_ghosts turn_n out_f out_links
+FIRST = """
+Q P pick ref yq products pick_b dummy sign listed er list_b even row moved um scatter_f h1_@v send turn_f turn_h compose_g
+list_f room compose_b equal list_h@v h2_@v flags state hop first scatter_c s2 lo turn_n v atoms own ghosts@g scatter_l ai@v
+link1@v link0 lists0 turn Wlist@v link2@v al link3 lists1 h0 b0@v W1@v W2 W0 c0 h1 fetch1@v nT b1 fetch0 fetch5 fetch2 in0 in1
+in4 c1 sums blend1 in3 keep1@g af@g size1 blend0 blend4 in2 blend2 size0 size4 in5 blend3 rows0 blend5 sum0 count size2
+room_atoms@v srow0 limit size5 size3 rows1 sum1 next_room room_f keep3 keep2@g keep4@g wrap keep0 delta scan0 srow1 al2 scan1
+low
 """.split()
-PIECES = (("psd0", 0, 2), ("psd1", 2, 2), ("psd2", 4, 2), ("psd3", 6, 1), ("psb0", 7, 1))
+MIDDLE = """
+ref Q P pick room yq products pick_b sign last_rooms listed er um dummy moved scatter_f even list_b row h1_ send compose_g
+turn_f turn_h equal scatter_c list_h h2_@v flags state first list_f hop s2 lo v compose_r compose_b turn_n scatter_l atoms
+link1 own@v ghosts@g room_atoms@g af@g link3 link0@v Wlist@v lists0 turn W0 W1 nT link2@v lists1 W2@v h0 b0@v c0 h1 fetch1@v
+b1 c1 fetch0 in2 in1 in4 in3 in0 blend1 keep1@g fetch5 fetch2 blend0 sums keep0@g blend4 size1 blend2 size0 size4 in5 blend5
+rows0 blend3 count ai@v room_f@v limit srow0 al size2 sum0 size5 size3 rows1 next_room sum1 keep2 wrap keep3@g keep4@g scan0
+srow1 scan1 al2 low delta
+""".split()
+END = """
+Q P pick ref yq products dummy listed@v room sign er even moved row@v scatter_f turn_f send equal state compose_g list_f flags
+first lo compose_r compose_b out_room out_base scatter_l out_ghosts out_links turn_n out_f@v
+""".split()
+WRITES = set([_n.split("@")[0] for _n in END] + "pick_b list_b um h1_ turn_h list_h h2_ hop scatter_c s2 v atoms".split())
+PIECES = (("psd0", 1024, 512), ("psd1", 1536, 512), ("psd2", 512, 512), ("psd3", 256, 256), ("psb0", 0, 128), ("psd0", 128, 128))
+QUARTERS = (2, 3, 1, 0)
+FETCH = ((1024, 512), (1536, 512), (512, 512), (256, 256), (0, 256), (0, 512))
+KEEP = FETCH
+SUMS = (("psk", 4, 8), ("psm", 1, 4))
+ROWS = ("psd1", "psd2")
 
 
 def unit(u):
@@ -30,22 +49,22 @@ def unit(u):
 
 SCRATCH = {}
 for _n, _c, _d in (
-        ("Y", 1408, BF), ("C", 1408, I32), ("LI", 1024, I32), ("L", 1152, F32), ("FW", 56, I32), ("FL", 88, U16),
-        ("FR0", 1536, BF), ("FR1", 1536, BF), ("W", 1408, BF), ("TH8", 128, I32), ("THF", 128, F32), ("NEW", 512, BF),
+        ("Y", 1408, BF), ("CI", 512, I32), ("C", 1408, F32), ("LI", 1024, I32), ("L", 1152, F32), ("FW", 56, I32), ("FL", 88, U16),
+        ("FR0", 1664, BF), ("FR1", 1664, BF), ("W", 1408, BF), ("TH8", 128, I32), ("THF", 128, F32), ("NEW", 512, BF),
         ("LAND", 1536, BF), ("FO", 88, F32), ("v16", 32, U16),
-        ("abc", 384, U16), ("Lg", 2048, F16), ("lh", 128, F32), ("xb", 2048, F32), ("y16", 2048, F16), ("yS", 2048, F32),
-        ("dA", [8, 256], BF), ("own", 128, BF), ("nT", 128, F16), ("u1", 128, F32), ("SC", 256, F32), ("hi", 16, F32),
-        ("pk", 16, F32), ("po", 16, U16), ("RN", 16, BF), ("pd", 32, F32), ("pr", 384, F16), ("dq", 128, F16), ("sg", 128, BF),
-        ("l16", 24, U16), ("vo16", 8, U16), ("er", 128, BF), ("hw", 128, BF), ("apr", 128, F16), ("EQ", 1024, BF),
-        ("DD", 128, BF), ("DS", 128, BF), ("m1", 8, F32), ("m2", 8, F32), ("lo16", 8, U16), ("LE", 128, F32),
-        ("ODN", 128, F32), ("um", 128, F32), ("cn", 128, I32), ("cm", 128, I32), ("ai", 8, I32), ("al", 8, I32), ("mx", 8, F32),
-        ("B", 8, F32), ("s2", 8, U16), ("thr", 8, F32), ("thr0", 8, F32), ("ah", 1, F32),
-        ("T1", 128, I32), ("T1a", 128, I32), ("TK", 128, I32), ("Q16", 88, I32), ("PI", 8, I32), ("JR", 128, BF),
-        ("I", 128, F16), ("NI", 128, F16), ("M1", 2048, BF), ("M32", 32, BF), ("R", 512, F16), ("EE", [16, 144], F16),
-        ("e1", 128, F16), ("e2", 128, F16), ("BC", 16, BF), ("BO", 128, BF), ("Z", 576, BF), ("ZT", 144, F32),
-        ("d0P", 64, F32), ("d0Q", 64, F32), ("d0D", 128, BF), ("half", 128, F32), ("POW", 128, F32), ("TM", 128, F32),
-        ("TM0", 128, F32), ("PC", 32, F32), ("SF", 64, F32), ("LH", 8, F16), ("CL", 34, U16), ("RB", 12, F32), ("wt", 32, F32),
-        ("cst", 2, BF)):
+        ("abc", 384, U16), ("Lg", 2048, F16), ("xb", 2048, F32), ("y16", 2048, F16), ("yS", 2048, F32),
+        ("dA", [8, 256], BF), ("own", 128, BF), ("nT", 128, F16), ("SA", 256, F32), ("SC", [4, 256], I32), ("low", 16, I32),
+        ("po", 16, U16), ("RN", 16, BF), ("pd", 32, F32), ("pr", 384, F16), ("dq", 128, F16), ("sg", 128, F16),
+        ("l16", 32, U16), ("vo16", 16, U16), ("er", 128, BF), ("hw", 256, BF), ("apr", [8, 18], F16), ("EQ", [8, 8, 18], BF),
+        ("DD", 144, F16), ("DS", 144, F16), ("lo16", 8, U16), ("LE", 128, F32),
+        ("um", 128, F32), ("wr", 128, F16), ("dl", 128, F32), ("af", 128, F16), ("al", 8, I32), ("mx", 16, I32),
+        ("s2", 8, U16), ("thr0", 16, F32), ("ah", 1, F32),
+        ("T1", 128, I32), ("T1a", 128, I32), ("TK", 32, I32), ("Q16", 88, I32), ("PI", 16, I32), ("JR", 128, BF),
+        ("I", 128, F16), ("NI", 128, F16), ("I64", 128, F16), ("IH", 128, F16), ("M1", 2048, BF), ("M32", 32, BF),
+        ("R", 512, F16), ("EE", [16, 144], F16), ("lh", 128, F32), ("BC", 16, BF), ("BO", 128, BF), ("Z", 576, BF), ("ZT", 144, F32),
+        ("d0P", 64, F32), ("d0Q", 64, F32), ("d0R", 512, BF), ("d0D", 144, F16), ("half", 128, F32), ("POW", 128, F32),
+        ("TM", [8, 18], F32), ("TM0", 128, F32), ("PC", 32, F32), ("SF", 64, F32), ("LH", 8, F16), ("CL", 34, U16), ("RB", 12, F32),
+        ("wt", 32, F32), ("cst", 2, BF), ("C15", 128, BF), ("ODN", 128, F32)):
     SCRATCH[_n] = ("sbuf", [128] + (_c if isinstance(_c, list) else [_c]), _d)
 for _n in ("psb0", "psb1", "psd0", "psd1", "psd2", "psd3", "psk", "psm"):
     SCRATCH[_n] = ("psum", [128, 512], F32)
@@ -69,6 +88,7 @@ def rank_program(g, core, T, topo):
     known = {"v": {}, "a": {}, "p": {}, "g": {}, "s": {}}
     log = {}
     total = {}
+    lane = ["a"]
 
     def waits(e, reads, writes):
         need = {}
@@ -128,11 +148,16 @@ def rank_program(g, core, T, topo):
     def A(nm, lo=0, hi=None, st=1, parts=128):
         if hi is None:
             hi = SCRATCH[nm][1][1]
+        elif nm[:2] == "FR":
+            lo, hi = lo + 128, hi + 128
         ap = T[nm][0:parts, lo:hi] if st == 1 else T[nm][0:parts, lo:hi:st]
         return (ap, [(nm, lo, hi)], [])
 
-    def A3(nm, ap):
-        return (ap, [(nm, 0, 1 << 20)], [])
+    def A3(nm, ap, lo=0, hi=1 << 20):
+        return (ap, [(nm, lo, hi)], [])
+
+    def abc(j, lo=0, hi=128):
+        return A("abc", 128 * j + lo, 128 * j + hi)
 
     def ind(win, off):
         return (win[0].indirect(off[0]), win[1], off[1])
@@ -154,13 +179,22 @@ def rank_program(g, core, T, topo):
                [x, s1, s2], [o])
 
     def vscan(o, d0, d1, op0, op1, first=0.0):
-        do("v", lambda: g.vector.tensor_tensor_scan(out=o[0], data0=d0[0], data1=d1[0], initial=first, op0=op0, op1=op1),
-           [d0, d1], [o])
+        do("v", lambda: g.vector.tensor_tensor_scan(out=o[0], data0=d0[0], data1=d1[0], initial=val(first), op0=op0, op1=op1),
+           [d0, d1, first], [o])
 
     def vset(o, c):
         do("v", lambda: g.vector.memset(o[0], c), [], [o])
 
+    def gcopy(o, x):
+        n = o[1][0][2] - o[1][0][1]
+        do("g", lambda: g.affine_select(out=o[0], in_=x[0], pattern=[[0, n]], compare_op=ge, fill=0.0, base=0,
+                                        channel_multiplier=0), [x], [o])
+
     def act(o, x, f=None, bias=None, scale=None):
+        if f is None and lane[0] != "a":
+            if bias is None and scale is None:
+                return (vcopy if lane[0] == "v" else gcopy)(o, x)
+            return vts(o, x, 1.0 if scale is None else scale, mul, 0.0 if bias is None else bias, add)
         kw = {}
         for key, z in (("bias", bias), ("scale", scale)):
             if z is not None:
@@ -168,16 +202,6 @@ def rank_program(g, core, T, topo):
         if f is None:
             f = AF.Identity if isinstance(bias, tuple) else AF.Copy
         do("a", lambda: g.scalar.activation(out=o[0], in_=x[0], func=f, **kw), [x, bias, scale], [o])
-
-    def copy(e, o, x):
-        if e == "v":
-            vcopy(o, x)
-        elif e == "a":
-            act(o, x)
-        else:
-            n = o[1][0][2] - o[1][0][1]
-            do("g", lambda: g.affine_select(out=o[0], in_=x[0], pattern=[[0, n]], compare_op=ge, fill=0.0, base=0,
-                                            channel_multiplier=0), [x], [o])
 
     def mms(bank, jobs, first=True, last=True):
         def fn():
@@ -191,8 +215,12 @@ def rank_program(g, core, T, topo):
         kw = {"allow_small_or_imprecise_dtypes": True} if flag else {}
         do("g", lambda: g.iota(o[0], pattern=pattern, base=base, channel_multiplier=cmul, **kw), [], [o])
 
-    def fill(o, c, flag=True):
-        iota(o, [[0, o[1][0][2] - o[1][0][1]]], c, 0, flag)
+    def fill(o, c):
+        iota(o, [[0, o[1][0][2] - o[1][0][1]]], c, 0, True)
+
+    def mark(o, pattern, base, c):
+        do("g", lambda: g.affine_select(out=o[0], in_=o[0], pattern=pattern, compare_op=AluOpType.not_equal, fill=c, base=base,
+                                        channel_multiplier=-1), [o], [o])
 
     def to_list(out, z, nm, lo, hi):
         return [(out, A("Z", 144 * z + 16 - r, 144 * z + 144 - r), A(nm, lo + r, hi, 16)) for r in range(16)]
@@ -201,79 +229,106 @@ def rank_program(g, core, T, topo):
 
     def SF(j, n=1):
         return A("SF", j, j + n)
-    RC, EV, OD, R1, R2, RF, RO2, R0, RH = SF(0), SF(1), SF(2), SF(3), SF(4), SF(5), SF(38), SF(36), SF(37)
-    LI, K15, IK, ODB = SF(8, 8), SF(16, 8), SF(24, 8), SF(32, 4)
+    RC, EV, OD, R1, R2, RF, R0, RH, RO2 = SF(0), SF(1), SF(2), SF(3), SF(4), SF(5), SF(36), SF(37), SF(38)
+    LI, KQ, KP, IK, ODB = SF(8, 8), SF(16, 8), SF(40, 8), SF(24, 8), SF(32, 4)
 
-    dma("s", T.LI[:, :], T.lk[:, :], [], [("LI", 0, 1024)], "in0")
-    dma("a", T.C[:, 0:128], T.cl[:, 0:128], [], [("C", 0, 128)], "in1")
     dma("a", T.FW[:, :], T.fw0[:, :], [], [("FW", 0, 56)], "in2")
-    dma("s", T.Y[:, 0:896], T.y0[:, :], [], [("Y", 0, 896)], "in3")
+    dma("s", T.CI[:, 0:128], T.cl[:, 0:128], [], [("CI", 0, 128)], "in1")
+    dma("s", T.LI[:, :], T.lk[:, :], [], [("LI", 0, 1024)], "in0")
     dma("a", T.TH8[0:8, :], T.th[:, :], [], [("TH8", 0, 128)], "in5")
+    dma("a", T.Y[:, 0:896], T.y0[:, :], [], [("Y", 0, 896)], "in3")
 
-    iota(A("TK"), [[1, 16], [16, 8]], 0, -1)
-    iota(A("T1"), [[1, 128]], 128, -1)
-    iota(A("PI", 0, 1), [[0, 1]], 0, 1)
-    iota(A("Q16"), [[16, 88]], 0, 0)
-    iota(A("JR"), [[1, 128]], 0, 0, True)
-    fill(A("ZT", parts=8), 0)
-    fill(A("Z"), 0)
-    fill(A("d0P"), 1)
-    fill(A("d0Q"), -1)
-    fill(A("d0D"), 1)
-    fill(A("TM0"), 0)
-    fill(A("C", 512, 896), 0, False)
+    def k_pick():
+        mark(A3("EE", T.EE[:, :, 15:143:16]), [[1, 16], [16, 8]], 0, 4096.0)
+        mark(A3("EE", T.EE[:, 0:11, 15:143:16]), [[1, 11], [16, 8]], 5, 1.0)
+        mark(A3("EE", T.EE[:, 11:16, 15:143:16]), [[1, 5], [16, 8]], 0, 1.0)
 
-    vset(A3("EE", T.EE[:, :, :]), 0.0)
-    vts(A("e1"), A("TK"), 0, eq, 4096.0, mul)
-    vts(A("e2", 0, 88), A("TK", 0, 88), -5, eq)
-    vts(A("e2", 88, 128), A("TK", 88, 128), 11, eq)
-    vts(A("T1a"), A("T1"), 15, band)
-    vts(A("PI", 1, 2), A("PI", 0, 1), 15, band)
-    vts(A("ai"), A("TK", 120, 128), 4, shr)
-    vts(A("M1", 0, 128), A("T1a"), 0, eq)
-    vcopy(RC, A("PI", 1, 2))
-    vts(A("T1a", 0, 32), A("T1", 0, 32), 31, band)
-    vts(A("CL", 0, 32), A("Q16", 0, 32), 1.0 / 16, mul)
-    vset(A("BC", 8, 16), 0.0)
-    vts(A("M32"), A("T1a", 0, 32), 0, eq)
-    vts(A("BC", 0, 8), A("ai"), 0, eq)
-    vts(A("I"), A("T1"), 128, eq)
-    vtt(A3("EE", T.EE[:, :, 15:143:16]), A("e1"), A("e2"), add)
-    vcopy(SF(36, 3), A("M1", 0, 3))
-    vts(RF, RC, 1.0, le)
-    vcopy(A("ZT", 16, 144, 16, parts=8), A("I", 0, 8, parts=8))
-    vts(R1, RC, 1.0, ge)
-    vts(R2, RC, 2.0, ge, -4096.0, mul)
-    vts(A("PI", 2, 3), A("PI", 0, 1), 1, band)
-    vts(A("PI", 3, 4), A("PI", 0, 1), 7, band)
-    vts(A("RB", 0, 11), A("Q16", 0, 88, 8), R1, mul)
-    vcopy(OD, A("PI", 2, 3))
-    vts(A("RB", 4, 7), A("Q16", 32, 56, 8), RH, mul, R2, add)
-    vts(EV, A("PI", 2, 3), 0, eq)
-    for b in range(11):
-        vts(A("FR1", 128 * b, 128 * b + 128), A("JR"), R0, mul, A("RB", b, b + 1), add)
-    vcopy(A("FL", 0, 56), A("FW"))
-    vcopy(A("abc", 0, 128), A("C", 0, 128))
+    def k_diagonal():
+        vts(A("T1a"), A("T1"), 15, band)
+        vts(A("M1", 0, 128), A("T1a"), 0, eq)
+        vcopy(SF(36, 3), A("M1", 0, 3))
 
-    dmas("s", [(T.M1[:, 128 * j:128 * j + 128], T.M1[:, 0:128]) for j in (1, 2, 3)], [("M1", 0, 128)], [("M1", 128, 512)], "in6")
-    dma("s", T.C[:, 128:512], T.cl[:, 128:512], [("LI", 0, 1024)], [("C", 128, 512)], "in4")
-    dmas("s", [(T.M1[:, 512 * j:512 * j + 512], T.M1[:, 0:512]) for j in (1, 2, 3)], [("M1", 0, 512)], [("M1", 512, 2048)], "in7")
+    def k_parts():
+        vts(R1, R0, -1.0, mul, 1.0, add)
+        vtt(RF, R0, RH, add)
+        vts(R2, R1, RH, sub, 4096.0, mul)
+        vts(A("RB", 0, 11), A("Q16", 0, 88, 8), R1, mul)
+        vts(A("RB", 4, 7), A("Q16", 32, 56, 8), RH, mul, R2, add)
 
-    act(LI, A("Q16", 0, 8), bias=RC)
-    act(A("v16", 0, 8), A("Q16", 0, 8), bias=RC)
-    act(A("FL", 56, 88), A("Q16", 56, 88), bias=RC)
-    act(A("R"), ind(A("M32"), A("CL", 0, 32)))
-    act(A("BO"), ind(A("BC"), A("CL", 0, 8)), scale=32.0)
-    act(K15, LI, scale=16.0, bias=15.0)
-    for o, c in ((A("PC", 0, 8), 896.0), (A("PC", 8, 16), 1408.0), (A("PC", 24, 32), 1024.0), (IK, -4096.0), (A("LH"), 0.0)):
-        act(o, LI, bias=c)
-    for z, s in ((ONE, 1.0), (X32, 32.0), (FULL, RF), (BLOCK, RO2)):
-        act(A("Z", 144 * z + 16, 144 * z + 144, 16), A("BC", 0, 8), scale=s)
-    act(A("W", 0, 896), ind(A("Y", 0, 896), A("FL", 0, 56)), scale=0.5)
+    def k_numbers(nm, lo, hi):
+        for b in range(lo, hi):
+            act(A(nm, 128 * b, 128 * b + 128), A("JR"), scale=R0, bias=A("RB", b, b + 1))
 
-    def later_constants():
+    def k_places():
+        vts(A("PI", 1, 2), A("PI", 0, 1), 15, band)
+        vts(A("PI", 2, 3), A("PI", 0, 1), 1, band)
+        vts(A("PI", 3, 4), A("PI", 0, 1), 7, band)
+        vcopy(RC, A("PI", 1, 2))
+        vcopy(OD, A("PI", 2, 3))
+        vts(EV, A("PI", 2, 3), 0, eq)
+
+    def k_groups():
+        vts(A("al"), A("PI", 8, 16), 4, shr)
+        vts(A("CL", 0, 32), A("Q16", 0, 32), 1.0 / 16, mul)
+        vset(A("BC", 8, 16), 0.0)
+        vts(A("BC", 0, 8), A("al"), 0, eq)
+
+    def k_m32():
+        vts(A("TK"), A("T1", 0, 32), 31, band)
+        vts(A("M32"), A("TK"), 0, eq)
+
+    def k_lanes():
+        act(LI, A("Q16", 0, 8), bias=RC)
+        act(A("v16", 0, 8), A("Q16", 0, 8), bias=RC)
+        act(A("FL", 56, 88), A("Q16", 56, 88), bias=RC)
+
+    def k_lanes2():
+        act(KQ, LI, scale=16.0)
+        act(KP, LI, scale=16.0, bias=30.0)
+        act(A("PC", 0, 8), LI, scale=2.0, bias=896.0 + 4096)
+        for o, c in ((A("PC", 8, 16), 1536.0), (A("PC", 24, 32), 1024.0), (IK, 4096.0), (A("LH"), 0.0)):
+            act(o, LI, bias=c)
+
+    def k_thresholds():
+        act(A("THF", 0, 15, parts=8), A("TH8", 0, 15, parts=8), scale=32.0, bias=30.0 + LIFT)
+        act(A("THF", 15, 128, parts=8), A("TH8", 15, 128, parts=8), scale=32.0, bias=30.0)
+        mms("psk", [(A("psk", 0, 8), A("ZT", 16 - r, 144 - r, parts=8), A("THF", r, 128, 16, parts=8)) for r in range(16)])
+
+    def k_limits():
+        for j in range(2):
+            act(A3("SC", T.SC[:, 2 * j, 127:240:16], 512 * j, 512 * j + 256), A("psk", 0, 8), bias=float(j))
+        act(A("thr0"), A3("SC", T.SC[:, 0:3:2, 127:240:16], 0, 768), bias=240.0)
+
+    def k_windows(which):
+        for z, s in which:
+            act(A("Z", 144 * z + 16, 144 * z + 144, 16), A("BC", 0, 8), scale=s)
+
+    def k_steps():
+        fill(A("d0P"), 1)
+        fill(A("d0Q"), -1)
+
+    def k_turn8():
+        fill(A("ZT", parts=8), 0)
+        mark(A("ZT", 16, 144, 16, parts=8), [[1, 8]], 0, 1.0)
+
+    def k_rows():
+        act(A("d0R", 0, 256), ind(A("M1", 0, 16), A("CL", 0, 16)))
+        act(A("hw", 0, 16), A("M1", 15, 31), scale=LIFT)
+        act(A("hw", 16, 32), A("M1", 0, 16), scale=-BIG)
+
+    def k_rows2():
+        vtt(A("d0R", 0, 256, 16), A("hw", 0, 16), A("hw", 16, 32), add)
+        vts(A("d0R", 256, 512), A("d0R", 0, 256), -1.0, mul)
+
+    def k_scans():
+        vset(A("C15"), 15.0 / 512)
+        vset(A("d0P", 0, 64, 16), -BIG)
+        vset(A("d0Q", 0, 64, 16), BIG)
+        vts(A("IH"), A("I"), 0.5, mul)
+
+    def k_weights():
         vset(A("half"), 0.5)
-        vset(A("d0D", 0, 128, 16), 0.0)
+        vset(A("d0D", 0, 144, 18), 0.0)
         vcopy(A("CL", 32, 33), A("PI", 3, 4))
         vscan(A("POW"), A("half"), A("TM0"), mul, add, 2.0 ** 65)
         vcopy(A("CL", 33, 34), A("PI", 1, 2))
@@ -281,126 +336,180 @@ def rank_program(g, core, T, topo):
         vtt(A("wt", 0, 16), A("POW", 64, 80), A("M1", 0, 16), mul)
         vts(A("half"), A("POW"), 80.0, mul)
         vscan(A("wt", 16, 32), A("d0D", 0, 16), A("wt", 0, 16), mul, add)
-        vtt(A("TM"), A("half"), A("TM0"), mx)
+        vtt(A3("TM", T.TM[:, :, 0:16]), A("half"), A("TM0"), mx)
         vts(A("PC", 16, 24), A("POW", 0, 128, 16), A("wt", 31, 32), mul)
+
+    def k_small():
         vset(A("cst"), -15.0 / 32)
-        act(A("FR0", 0, 896), ind(A("FR1", 0, 896), A("FL", 0, 56)))
-        act(A("L", 0, 1024), A("LI"))
-        dma("s", T.lo[0:128:2, :], T.L[0:128:2, 0:1024], [("L", 0, 1024)], [], "out0")
+        vts(A("NI"), A("I"), -32768.0, mul)
+        vts(A("I64"), A("I"), 64.0, mul)
+        vts(ODB, A("Q16", 56, 88, 8), OD, mul)
+
+    def k_spare():
+        vset(A3("apr", T.apr[:, :, 16:18]), -1.0)
+        vset(A3("TM", T.TM[:, :, 16:18]), 1.0)
+        act(A("d0D", 17, 144, 18), A("PC", 24, 32))
+
+    def k_fills():
+        fill(A("d0D"), 1)
+        fill(A("TM0"), 0)
+
+    def k_clusters():
+        gcopy(A("C", 128, 512), A("CI", 128, 512))
+        fill(A("C", 512, 896), 0)
+
+    constants = {
+        "g_m": lambda: iota(A("T1"), [[1, 128]], 128, -1),
+        "g_p": lambda: iota(A("PI", 0, 1), [[0, 1]], 0, 1),
+        "g_g": lambda: iota(A("PI", 8, 16), [[16, 8]], 15, -1),
+        "g_q": lambda: iota(A("Q16"), [[16, 88]], 0, 0),
+        "g_j": lambda: iota(A("JR"), [[1, 128]], 0, 0, True),
+        "g_z": lambda: fill(A("Z"), 0),
+        "k_zero": lambda: vset(A3("EE", T.EE[:, :, :]), 0.0),
+        "k_unit": lambda: vts(A("I"), A("T1"), 128, eq),
+        "k_atoms": lambda: act(abc(0), A("CI", 0, 128)),
+        "k_list": lambda: act(A("FL", 0, 56), A("FW")),
+        "k_spread": lambda: act(A("R"), ind(A("M32"), A("CL", 0, 32))),
+        "k_block": lambda: act(A("BO"), ind(A("BC"), A("CL", 0, 8)), scale=32.0),
+        "k_sums": lambda: k_windows(((ONE, 1.0), (X32, 32.0))),
+        "k_turns": lambda: k_windows(((FULL, RF), (BLOCK, RO2))),
+        "k_numbers": lambda: k_numbers("FR1", 0, 7),
+        "k_links": lambda: act(A("L", 0, 1024), A("LI")),
+        "k_forwards": lambda: act(A("FR0", 0, 896), ind(A("FR1", 0, 896), A("FL", 0, 56))),
+        "k_odd": lambda: act(A("ODN"), A("JR"), scale=OD),
+        "k_ones": lambda: dmas("s", [(T.M1[:, 128 * j:128 * j + 128], T.M1[:, 0:128]) for j in (1, 2, 3)],
+                               [("M1", 0, 128), ("Y", 0, 896)], [("M1", 128, 512)], "in6"),
+        "k_load": lambda: dma("s", T.CI[:, 128:512], T.cl[:, 128:512], [("Y", 0, 896)], [("CI", 128, 512)], "in4"),
+        "k_ones2": lambda: dmas("s", [(T.M1[:, 512 * j:512 * j + 512], T.M1[:, 0:512]) for j in (1, 2, 3)],
+                                [("M1", 0, 512)], [("M1", 512, 2048)], "in7"),
+        "out_even": lambda: dma("s", T.lo[0:128:2, :], T.L[0:128:2, 0:1024], [("L", 0, 1024)], [], "out0"),
+        "k_pick": k_pick, "k_diagonal": k_diagonal, "k_parts": k_parts, "k_places": k_places, "k_groups": k_groups,
+        "k_m32": k_m32, "k_lanes": k_lanes, "k_lanes2": k_lanes2, "k_thresholds": k_thresholds, "k_steps": k_steps,
+        "k_turn8": k_turn8, "k_limits": k_limits, "k_rows": k_rows, "k_rows2": k_rows2, "k_scans": k_scans,
+        "k_weights": k_weights, "k_small": k_small, "k_spare": k_spare, "k_fills": k_fills, "k_clusters": k_clusters,
+    }
 
     def one_round(t, FRc, FRn):
         first, last = t == 0, t == RO - 1
         made = 896 + 128 * t
         v, vn = A("v16", 8 * t, 8 * t + 8), A("v16", 8 * t + 8, 8 * t + 16) if not last else None
-        own = A("Y", 0, 128) if first else A("own")
-        a16, P, Q = A("abc", 0, 128), A("po", 0, 8), A("po", 8, 16)
+        own = A("own")
+        a16, P, Q = abc(0), A("po", 0, 8), A("po", 8, 16)
         nw = A("NEW", 128 * t, 128 * t + 128)
-        big = A("SC", 15, 128, 16)
 
-        def link(q):
-            e = OPT["links0" if first else "links"][q]
-            copy(e, A("Lg", 512 * q, 512 * q + 512), ind(A("LI") if first else A("L", 0, 1024), A("abc", 32 * q, 32 * q + 32)))
+        def rows_of(j0, j1):
+            return A3("SC", T.SC[:, j0:j1 + 1:j1 - j0, 127:240:16], 256 * j0, 256 * j1 + 256)
 
-        def lists(h):
-            mms("psb%d" % h, [(A("psb%d" % h, 0, 64), A3("EE", T.EE[:, k, 15 - k:143 - k]), A("Lg", 1024 * h + k, 1024 * h + 1024, 16))
+        def link(n):
+            q = QUARTERS[n]
+            act(A("Lg", 512 * q, 512 * q + 512), ind(A("LI") if first else A("L", 0, 1024), abc(0, 32 * q, 32 * q + 32)))
+
+        def lists(n):
+            h = 1 - n
+            mms("psb%d" % n, [(A("psb%d" % n, 0, 64), A3("EE", T.EE[:, k, 15 - k:143 - k]), A("Lg", 1024 * h + k, 1024 * h + 1024, 16))
                               for k in range(16)])
 
-        def list_b(h):
-            o, ps = A("abc", 128 + 64 * h, 192 + 64 * h), A("psb%d" % h, 0, 64)
-            if OPT["b16"][h] == "a":
-                act(o, ps, scale=1.0 / 4096)
-            else:
-                vts(o, ps, 1.0 / 4096, mul)
+        def list_b(n):
+            act(abc(1, 64 - 64 * n, 128 - 64 * n), A("psb%d" % n, 0, 64), scale=1.0 / 4096)
 
-        def list_h(h):
-            vts(A("lh", 64 * h, 64 * h + 64), A("psb%d" % h, 0, 64), unit(4096), add, unit(4096), sub)
+        def list_h(n):
+            vts(A("lh", 64 * n, 64 * n + 64), A("psb%d" % n, 0, 64), unit(4096), add, unit(4096), sub)
 
-        def list_c(h):
-            vtt(A("abc", 256 + 64 * h, 320 + 64 * h), A("psb%d" % h, 0, 64), A("lh", 64 * h, 64 * h + 64), sub)
+        def list_c(n):
+            vtt(abc(2, 64 - 64 * n, 128 - 64 * n), A("psb%d" % n, 0, 64), A("lh", 64 * n, 64 * n + 64), sub)
+
+        def states(n):
+            lo, hi = (0, 384, 768, made)[n:n + 2]
+            act(A("W", lo, hi), ind(A("Y", 0, made), A("FL", lo // 16, hi // 16)))
 
         def own_in(n):
-            bank, q, k = PIECES[n]
-            part, o = slice(32 * (q // 2), 32 * (q // 2) + 32), 256 * (q % 2)
-            mms(bank, [(A(bank, 0, 256 * k), A3("nT", T.nT[part, :]), A3("R", T.R[part, o:o + 256 * k]))], last=False)
+            bank, lo, k = PIECES[n]
+            part = slice(32 * (lo // 512), 32 * (lo // 512) + 32)
+            mms(bank, [(A(bank, 0, k), A3("nT", T.nT[part, :]), A3("R", T.R[part, lo % 512:lo % 512 + k]))], last=False)
 
         def fetch(n):
-            o, x = A("xb", 512 * n, 512 * n + 512), ind(A("W", 0, made), A("abc", 128 + 32 * n, 160 + 32 * n))
-            if OPT["b"][n] == "a":
-                act(o, x, bias=1087.75)
-            else:
-                vts(o, x, 1087.75, add)
+            lo, k = FETCH[n]
+            act(A("xb", lo, lo + k), ind(A("W", 0, made), abc(1, lo // 16, (lo + k) // 16)), bias=2047.5)
 
         def blend(n):
-            bank, q, k = PIECES[n]
-            lo, hi = 256 * q, 256 * (q + k)
-            vtt(A("y16", lo, hi), ind(A("W", 0, made), A("abc", 256 + lo // 16, 256 + hi // 16)), A("xb", lo, hi), add)
-            mms(bank, [(A(bank, 0, hi - lo), A("I"), A("y16", lo, hi))], first=False)
-            copy("g", A("yS", lo, hi), A("y16", lo, hi))
+            bank, lo, k = PIECES[n]
+            hi = lo + k
+            vtt(A("y16", lo, hi), ind(A("W", 0, made), abc(2, lo // 16, hi // 16)), A("xb", lo, hi), add)
+            mms(bank, [(A(bank, 0, k), A("I"), A("y16", lo, hi))], first=False)
+
+        def keep(n):
+            lo, k = KEEP[n]
+            act(A("yS", lo, lo + k), A("y16", lo, lo + k))
+
+        def sizes(lo, hi):
+            q = lo // 256
+            return A3("dA", T.dA[:, q:hi // 256, :] if hi - lo >= 256 else T.dA[:, q, lo % 256:lo % 256 + hi - lo], lo, hi)
 
         def size(n):
-            bank, q, k = PIECES[n]
-            act((T.dA[:, q:q + k, :], [("dA", q, q + k)], []), A(bank, 0, 256 * k), AF.Abs)
+            bank, lo, k = PIECES[n]
+            act(sizes(lo, lo + k), A(bank, 0, k), AF.Abs, scale=0.5)
 
-        def sums(h):
-            bank = "psm" if h else "psk"
-            mms(bank, [(A(bank, 0, 64), A("Z", 144 * X32 + 16 - r, 144 * X32 + 144 - r),
-                        (T.dA[:, 4 * h:4 * h + 4, 16 * r:16 * r + 16], [("dA", 4 * h, 4 * h + 4)], [])) for r in range(16)])
+        def sums(n):
+            bank, q0, q1 = SUMS[n]
+            o = A(bank, 0, 16 * (q1 - q0))
+            mms(bank, [(o, A("BO"), A("C15", 0, 16 * (q1 - q0)))] +
+                [(o, A("Z", 144 * X32 + 16 - r, 144 * X32 + 144 - r),
+                  A3("dA", T.dA[:, q0:q1, 16 * r:16 * r + 16], 256 * q0, 256 * q1)) for r in range(16)])
 
-        def scan(h):
-            bank, o = ("psm" if h else "psk"), 64 * h
-            if first and h == 0:
-                vset(A("d0P", 0, 64, 16), -BIG)
-                vset(A("d0Q", 0, 64, 16), BIG)
-            vscan(A("SC", o, o + 64), A("d0P"), A(bank, 0, 64), add, mx)
-            vscan(A("SC", 128 + o, 192 + o), A("d0Q"), A(bank, 0, 64), add, mn)
+        def scan(n):
+            bank, q0, q1 = SUMS[n]
+            k = 16 * (q1 - q0)
+            for j, d0, op in ((1, "d0P", mx), (3, "d0Q", mn)):
+                o = A3("SC", T.SC[:, j, 112 + 16 * q0:112 + 16 * q1], 256 * j + 112 + 16 * q0, 256 * j + 112 + 16 * q1)
+                vscan(o, A(d0, 0, k), A(bank, 0, k), add, op)
 
-        def compose(e, lo, hi):
+        def rows(n):
+            o = A(ROWS[n], 0, 128)
+            mms(ROWS[n], [(o, A("BO"), A("C15")), (o, A("BO"), sizes(128 * n, 128 * n + 128))])
+
+        def scan_rows(n):
+            for j, op in ((0, mx), (1, mn)):
+                d0 = A("d0R", 256 * j + 128 * n, 256 * j + 128 * n + 128)
+                if n:
+                    vscan(A3("SC", T.SC[:, 2 * j + 1, 0:128], 512 * j + 256, 512 * j + 384), d0, A(ROWS[n], 0, 128), add, op,
+                          A("SA", 128 * j + 127, 128 * j + 128))
+                else:
+                    vscan(A("SA", 128 * j, 128 * j + 128), d0, A(ROWS[n], 0, 128), add, op)
+
+        def compose(lo, hi):
             if hi > lo:
-                copy(e, A(FRn, lo, hi), ind(A(FRc, 0, made), A("FL", lo // 16, hi // 16)))
-
-        def turn():
-            mms("psb1", [(A("psb1", 0, 128), own, A("I"))])
+                act(A(FRn, lo, hi), ind(A(FRc, 0, made), A("FL", lo // 16, hi // 16)))
 
         def states_sum():
-            ps = A("psb1", 128, 129)
-            mms("psb1", ([] if last else [(A("psb1", 0, 128), A("BO"), own)])
+            ps, o = A("psb1", 256, 257), A("psb1", 128, 256)
+            mms("psb1", [(o, A("IH"), own)]
                 + ([] if first else [(ps, A("BO"), A("RN", q, q + 1)) for q in range(8)] + [(ps, A("BO"), A("cst", 0, 1))]))
-
-        def limits():
-            if first:
-                vcopy(A("thr"), A("psk", 0, 8))
-                vts(A("thr0"), A("psk", 0, 8), 240.0, add)
-
-        def limits_in():
-            if first:
-                act(A("THF", parts=8), A("TH8", parts=8), scale=32.0, bias=15.0)
-
-        def limits_turn():
-            if first:
-                mms("psk", [(A("psk", 0, 8), A("ZT", 16 - r, 144 - r, parts=8), A("THF", r, 128, 16, parts=8)) for r in range(16)])
 
         def out_f():
             act(A("FO", 0, 80), A("psk", 0, 80))
             dma("a", T.fo[:, :], T.FO[:, :], [("FO", 0, 88)], [], "out3")
-
-        def counted():
-            if first:
-                vcopy(A("FR0", 896, 1408), A("FR1", 896, 1408))
-                vts(ODB, A("Q16", 56, 88, 8), OD, mul)
-            else:
-                vts(A("ah"), A("psb1", 128, 129), unit(512), add, unit(512), sub)
 
         def pick():
             vtt(A("pr", 0, 256), ind(A("M1"), A("po")), A("abc", 0, 256), mul)
             mms("psd0", to_list(A("psd0", 0, 16), ONE, "pr", 0, 256))
 
         def pick_b():
-            vtt(A("pr", 256, 384), ind(A("M1"), P), A("abc", 128, 256), mul)
+            vtt(A("pr", 256, 384), ind(A("M1"), P), abc(1), mul)
             mms("psd1", to_list(A("psd1", 0, 8), ONE, "pr", 256, 384))
 
         def row():
             mms("psd2", [(A("psd2", 0, 128), A("BO"), A("pr", 0, 128))])
-            act(A("apr"), A("psd2", 0, 128), scale=1.0 / 32)
+            act(A3("apr", T.apr[:, :, 0:16]), A("psd2", 0, 128), scale=1.0 / 32)
+
+        def wrap():
+            o = A("psd3", 0, 128)
+            mms("psd3", [(o, A("BO"), own), (o, A("I64"), A("af"))])
+            act(A("wr"), o, scale=1.0 / 32768, bias=2049.0 + (2 * t + 3) / 1024)
+
+        def delta():
+            o = A("psd3", 0, 128)
+            mms("psd3", [(o, A("BO"), own), (o, A("NI"), A("wr"))])
+            act(A("dl"), o, scale=1.0 / 64, bias=1024.0 * 1025 + t + 1)
 
         def send():
             waits("g", nw[1], [])
@@ -426,94 +535,79 @@ def rank_program(g, core, T, topo):
 
         def equal():
             for q in range(8):
-                vts(A("EQ", 128 * q, 128 * q + 128), A("apr"), A("psd0", q, q + 1), eq, A("pd", 16 + q, 17 + q), mul)
+                vts(A3("EQ", T.EQ[:, q, q:8, :], q, q + 1), A3("apr", T.apr[:, q:8, :]), A("psd0", q, q + 1), eq,
+                    A("pd", 16 + q, 17 + q), mul)
                 if q % 4 == 3:
-                    mms("psd3", [(A("psd3", 0, 128), A("BO"), A("EQ", 128 * j, 128 * j + 128)) for j in range(q - 3, q + 1)],
-                        first=q == 3, last=q == 7)
+                    mms("psd3", [(A("psd3", 18 * j, 144), A("BO"), A3("EQ", T.EQ[:, j, j:8, :], j, j + 1)) for j in range(q - 3, q + 1)]
+                        + [(A("psd3", 16, 144, 18), A("I64"), A("RN", 8, 16))] * (q == 3), first=q == 3, last=q == 7)
 
-        def hop():
-            act(A("hw"), ind(A(FRn, 0, made), A("l16", 16, 24)))
-            mms("psd1", to_list(A("psd1", 0, 8), BLOCK, "hw", 0, 128) + [(A("psd1", 0, 8), A("I"), A("LH"))])
-
-        def state():
-            vcopy(own if first else ind(A("Y", 0, made), v), nw)
-
-        S = OPT["nw"] == "s"
         steps = {
-            "own": lambda: first or act(A("own"), ind(A("Y", 0, made), v)),
-            "turn": turn,
-            "nT": lambda: act(A("nT"), A("psb1", 0, 128), scale=-1.0, bias=-1088.0),
-            "consts": lambda: first and later_constants(),
-            "odd": lambda: act(A("ODN"), A("JR"), scale=OD, bias=SF(32 + t)),
-            "count": counted,
-            "limit": lambda: first or vts(A("thr"), A("thr0"), A("psb1", 128, 129), add, A("ah"), sub),
-            "limits": limits,
-            "limits_in": limits_in,
-            "limits_turn": limits_turn,
+            "own": lambda: act(own, A("Y", 0, 128) if first else ind(A("Y", 0, made), v), scale=2.0),
+            "turn": lambda: mms("psm", [(A("psm", 0, 128), own, A("I"))]),
+            "nT": lambda: act(A("nT"), A("psm", 0, 128), scale=-1.0, bias=-2048.0),
+            "Wlist": lambda: first or act(A("FL", 0, made // 16 - 8), A("psk", 0, made // 16 - 8)),
+            "ghosts": lambda: first or act(A("Y", 512, 896), A("LAND", 384 * t - 384, 384 * t)),
+            "count": lambda: first or vts(A("ah"), A("psb1", 256, 257), unit(512), add, unit(512), sub),
+            "limit": lambda: first or vts(rows_of(0, 2), A("thr0"), A("psb1", 256, 257), add, A("ah"), sub),
             "sums": states_sum,
-            "hi": lambda: vts(A("hi"), A("SC", 15, 256, 16), unit(32), add, unit(32), sub),
-            "pkP": lambda: vtt(A("pk", 0, 8), K15, big, sub),
-            "pkQ": lambda: vtt(A("pk", 8, 16), K15, A("SC", 143, 256, 16), add),
-            "P": lambda: vtt(P, A("pk", 0, 8), A("hi", 0, 8), add),
-            "Q": lambda: vtt(Q, A("pk", 8, 16), A("hi", 8, 16), sub),
-            "ref": lambda: vtt(A("RN", 0, 8), big, A("thr"), gt),
-            "nref": lambda: vtt(A("RN", 8, 16), big, A("thr"), le),
+            "low": lambda: vts(A("low"), rows_of(1, 3), 31, band),
+            "P": lambda: vtt(P, KP, A("low", 0, 8), sub),
+            "Q": lambda: vtt(Q, KQ, A("low", 8, 16), add),
+            "ref": lambda: vtt(A("RN"), rows_of(1, 2), rows_of(0, 1), gt),
             "products": lambda: vtt(A("pd"), ind(A("RN"), A("CL", 32, 34)), A("PC"), mul),
             "pick": pick,
             "row": row,
-            "yq": lambda: act(A("dq"), ind(A("yS"), Q), bias=-1088.0) if S else vtt(A("dq"), ind(A("yS"), Q), own, sub),
-            "less": lambda: S and mms("psb1", [(A("psb1", 0, 128), A("I"), A("dq")), (A("psb1", 0, 128), A("NI"), own)]),
-            "sign": lambda: act(A("sg"), A("psb1", 0, 128), AF.Sign) if S else act(A("sg"), A("dq"), AF.Sign, bias=-1088.0),
-            "more": lambda: OPT["nw"] != "v" and mms("psb0", [(A("psb0", 0, 128), A("I"), A("sg")), (A("psb0", 0, 128), A("I"), own)]),
-            "moved": lambda: act(nw, A("psb0", 0, 128)) if OPT["nw"] != "v" else vtt(nw, own, A("sg"), add),
+            "yq": lambda: vtt(A("dq"), ind(A("yS"), Q), own, sub),
+            "sign": lambda: act(A("sg"), A("dq"), AF.Sign, bias=-2048.0),
+            "moved": lambda: vtt(nw, A("sg"), A("psb1", 128, 256), add),
             "listed": lambda: act(A("l16", 0, 16), A("psd0", 0, 16)),
             "er": lambda: act(A("er"), ind(A(FRc, 0, made), A("l16", 8, 16))),
-            "dummy": lambda: vtt(A("vo16"), v, A("pd", 8, 16), mx),
+            "ai": lambda: act(A("mx", 8, 16), v, bias=128.0),
+            "dummy": lambda: vtt(A("vo16", 8 * last, 16), A("mx", 8 * last, 16), A("pd", 8 * last, 16), mx),
             "send": send,
-            "scatter_f": lambda: vcopy(ind(A(FRc), A("vo16")), A("er")),
+            "scatter_f": lambda: vcopy(ind(A(FRc), A("vo16", 8, 16)), A("er")),
             "turn_f": lambda: mms("psk", to_list(A("psk", 0, made // 16), FULL, FRc, 0, made)),
-            "even": lambda: act(A("LE"), ind(A("L", 0, 1024), A("l16", 0, 8)), scale=EV),
-            "compose_g": lambda: compose("a", 512, 896),
+            "even": lambda: act(A("LE"), ind(A("L", 0, 1024), A("l16", 0, 8)), scale=EV, bias=SF(32 + t)),
+            "compose_g": lambda: compose(512, 896),
             "list_f": lambda: act(A("FL", 0, made // 16), A("psk", 0, made // 16)),
             "equal": equal,
-            "m1": lambda: vtt(A("m1"), A("psd0", 0, 8), A("pd", 24, 32), mx),
-            "compose_b": lambda: compose("a", 0, 512),
-            "compose_r": lambda: compose("v" if last else "a", 896, made),
-            "flags": lambda: vtt(A("DD"), A("psd3", 0, 128), A("TM"), gt),
+            "compose_b": lambda: compose(0, 512),
+            "compose_r": lambda: compose(896, made),
+            "flags": lambda: vtt(A("DD"), A("psd3", 0, 144), A3("TM", T.TM[:, :, :]), gt),
             "turn_n": lambda: mms("psk", to_list(A("psk", 0, made // 16), FULL, FRn, 0, made)),
-            "room": lambda: act(A("Y", made, made + 128), ind(A("yS"), P), bias=-1088.0),
+            "room": lambda: act(A("Y", made, made + 128), ind(A("yS"), P), scale=0.5, bias=-1024.0),
             "first": lambda: vscan(A("DS"), A("d0D"), A("DD"), mul, mx),
-            "m2": lambda: vtt(A("m2"), A("DS", 15, 128, 16), A("PC", 24, 32), mul),
-            "lo": lambda: vtt(A("lo16"), A("m1"), A("m2"), mx),
-            "state": state,
+            "lo": lambda: vtt(A("lo16"), A("psd0", 0, 8), A("DS", 17, 144, 18), mx),
+            "state": lambda: vcopy(A("Y", 0, 128) if first else ind(A("Y", 0, made), v), nw),
             "scatter_l": lambda: vtt(ind(A("L"), A("lo16")), A("LE"), A("ODN"), add),
         }
-        for j in range(5):
+        for j in range(6):
             for name, fn in (("link", link), ("lists", lists), ("b", list_b), ("h", list_h), ("c", list_c), ("in", own_in),
-                             ("fetch", fetch), ("blend", blend), ("size", size), ("sum", sums), ("scan", scan)):
+                             ("fetch", fetch), ("blend", blend), ("keep", keep), ("size", size), ("sum", sums), ("scan", scan),
+                             ("rows", rows), ("srow", scan_rows), ("W", states)):
                 steps[name + str(j)] = lambda fn=fn, j=j: fn(j)
         if not last:
             steps.update({
-                "room_atoms": lambda: copy("g", A("C", made, made + 128), a16),
-                "u": lambda: act(A("u1"), A("psb1", 0, 128), scale=1.0 / 32, bias=float(t + 1)),
-                "ai": lambda: act(A("ai"), v, bias=128.0),
-                "al": lambda: vts(A("al"), A("ai"), 511, band),
-                "next_room": lambda: first or vts(A("PC", 0, 8), A("PC", 0, 8), 128.0, add),
+                "room_atoms": lambda: act(A("C", made, made + 128), a16),
+                "room_f": lambda: k_numbers(FRn, 7 + t, 8 + t),
+                "af": lambda: act(A("af"), a16),
+                "al": lambda: vts(A("al"), A("mx", 8, 16), 511, band),
+                "al2": lambda: vtt(A("mx", 0, 8), A("al"), IK, add),
+                "next_room": lambda: first or act(A("PC", 0, 8), A("PC", 0, 8), bias=128.0),
+                "wrap": wrap,
+                "delta": delta,
+                "um": lambda: vtt(A("um"), ind(A("M1"), P), A("dl"), mul),
+                "scatter_c": lambda: vtt(A("C", 0, 128) if first else ind(A("C", 0, made), v), A("um"), A("C", made, made + 128), add),
                 "pick_b": pick_b,
                 "list_b": lambda: act(A("l16", 16, 24), A("psd1", 0, 8)),
-                "um": lambda: vtt(A("um"), ind(A("M1"), P), A("u1"), mul),
-                "cn": lambda: vtt(A("cn"), A("um"), a16, add),
-                "cm": lambda: vts(A("C", 0, 128) if first else A("cm"), A("cn"), 1023, band),
-                "scatter_c": lambda: first or vcopy(ind(A("C", 0, made), v), A("cm")),
-                "hop": hop,
-                "mx": lambda: vtt(A("mx"), A("al"), A("pd", 0, 8), mx),
-                "B": lambda: vtt(A("B"), A("mx"), IK, add),
-                "ghosts": lambda: copy(OPT["ghost"][t], A("Y", 512, 896), A("LAND", 384 * t, 384 * t + 384)),
-                "list_n": lambda: act(A("FL", 0, made // 16), A("psk", 0, made // 16)),
-                "W": lambda: act(A("W", 0, made + 128), ind(A("Y", 0, made + 128), A("FL", 0, made // 16 + 8)), scale=0.5),
-                "s2": lambda: vtt(A("s2"), A("B"), A("psd1", 0, 8), sub),
-                "v": lambda: vtt(vn, A("psd1", 0, 8), A("s2"), mx),
-                "atoms": lambda: vcopy(a16, ind(A("C", 0, made + 128), vn)),
+                "h1_": lambda: act(A("hw", 0, 128), ind(A(FRc, 0, made), A("l16", 16, 24))),
+                "turn_h": lambda: mms("psm", to_list(A("psm", 0, 8), FULL, "hw", 0, 128)),
+                "list_h": lambda: act(A("l16", 24, 32), A("psm", 0, 8)),
+                "h2_": lambda: act(A("hw", 128, 256), ind(A(FRc, 0, made), A("l16", 24, 32))),
+                "hop": lambda: mms("psd1", [(A("psd1", 0, 8), A("I"), A("LH"))] + to_list(A("psd1", 0, 8), BLOCK, "hw", 128, 256)),
+                "s2": lambda: vtt(A("s2"), A("vo16", 0, 8), A("psd1", 0, 8), sub),
+                "v": lambda: vtt(vn, A("psd1", 0, 8), A("s2"), mn),
+                "atoms": lambda: act(a16, ind(A("C", 0, made + 128), vn)),
             })
         else:
             steps.update({
@@ -525,14 +619,17 @@ def rank_program(g, core, T, topo):
                 "last_rooms": lambda: act(A("FO", 80, 88), LI, bias=1280.0),
                 "out_f": out_f,
             })
-        for name in LAST if last else ORDER:
+        return steps
+
+    rounds = [one_round(t, "FR%d" % (t % 2), "FR%d" % (1 - t % 2)) for t in range(RO)]
+    for n, names in enumerate((START, FIRST, MIDDLE, MIDDLE, END)):
+        for name in names:
+            name, lane[0] = (name + "@a").split("@")[:2]
+            steps = constants if name in constants else rounds[n - 1] if name in WRITES else rounds[n]
             if name in steps:
-                HOOK.append(("step", t, name))
+                HOOK.append(("step", n, name))
                 steps[name]()
         HOOK.append(("step", -1, "end"))
-
-    for t in range(RO):
-        one_round(t, "FR%d" % (t % 2), "FR%d" % (1 - t % 2))
 
     for sem in ("dv", "ac", "pe", "gp"):
         g.wait_ge(T.sem[sem], count[sem])

from concourse.bass import DstId, RemoteDMATransfer
from concourse.mybir import AluOpType, ActivationFunctionType

RO = 4
HOOK = []
OPT = {}
BIG, LIFT = 1048576.0, 262144.0
F32, BF, I32, U16, F16 = "float32", "bfloat16", "int32", "uint16", "float16"
START = """
g_p g_q g_m g_j k_zero k_places k_list k_lanes k_atoms k_lanes2 k_m32 k_diagonal k_unit g_z g_g k_pick k_turn8 k_steps k_fills
k_links@g link2 link0 k_parts k_numbers@v k_odd@v link3@v lists1 own@v k_groups W2@v W1@v link1 lists0 turn k_rows W0
k_thresholds@v b1@v h1 k_sums@v b0 fetch5 c1 k_spread@v k_rows2 h0 fetch1 k_load k_ones k_ones2 out_even fetch0 nT fetch2
k_scans c0 ai@v k_small in4 in3 blend4 blend3 k_limits size4 k_block in1 in0 size3 blend1 blend0 in2 size1 size0 blend2 rows0
in5 blend5 k_turns@v k_weights srow0 sum0 size2 k_spare scan0 size5 keep3 keep4 room_atoms@g af@g keep0@g keep1@g keep2@g
room_f wrap rows1 sum1 k_forwards sums delta srow1 scan1 al low al2 k_clusters
""".split()
FIRST = """
Q P pick ref yq products pick_b dummy sign listed er list_b even row moved um scatter_f h1_@v send turn_f turn_h compose_g
list_f room compose_b equal list_h@v h2_@v flags state hop first scatter_c s2 lo turn_n v atoms own ghosts@g scatter_l ai@v
link1@v link0 lists0 turn Wlist@v link2@v al link3 lists1 h0 b0@v W1@v W2 W0 c0 h1 fetch1@v nT b1 fetch0 fetch5 fetch2 in0 in1
in4 c1 sums blend1 in3 keep1@g af@g size1 blend0 blend4 in2 blend2 size0 size4 in5 blend3 rows0 blend5 sum0 count size2
room_atoms@v srow0 limit size5 size3 rows1 sum1 next_room room_f keep3 keep2@g keep4@g wrap keep0 delta scan0 srow1 al2 scan1
low
""".split()
MIDDLE = """
ref Q P pick room yq products pick_b sign last_rooms listed er um dummy moved scatter_f even list_b row h1_ send compose_g
turn_f turn_h equal scatter_c list_h h2_@v flags state first list_f hop s2 lo v compose_r compose_b turn_n scatter_l atoms
link1 own@v ghosts@g room_atoms@g af@g link3 link0@v Wlist@v lists0 turn W0 W1 nT link2@v lists1 W2@v h0 b0@v c0 h1 fetch1@v
b1 c1 fetch0 in2 in1 in4 in3 in0 blend1 keep1@g fetch5 fetch2 blend0 sums keep0@g blend4 size1 blend2 size0 size4 in5 blend5
rows0 blend3 count ai@v room_f@v limit srow0 al size2 sum0 size5 size3 rows1 next_room sum1 keep2 wrap keep3@g keep4@g scan0
srow1 scan1 al2 low delta
""".split()
END = """
Q P pick ref yq products dummy listed@v room sign er even moved row@v scatter_f turn_f send equal state compose_g list_f flags
first lo compose_r compose_b out_room out_base scatter_l out_ghosts out_links turn_n out_f@v
""".split()
WRITES = set([_n.split("@")[0] for _n in END] + "pick_b list_b um h1_ turn_h list_h h2_ hop scatter_c s2 v atoms".split())
PIECES = (("psd0", 1024, 512), ("psd1", 1536, 512), ("psd2", 512, 512), ("psd3", 256, 256), ("psb0", 0, 128), ("psd0", 128, 128))
QUARTERS = (2, 3, 1, 0)
FETCH = ((1024, 512), (1536, 512), (512, 512), (256, 256), (0, 256), (0, 512))
KEEP = FETCH
SUMS = (("psk", 4, 8), ("psm", 1, 4))
ROWS = ("psd1", "psd2")


def unit(u):
    return 1.5 * 2.0 ** 23 * u


SCRATCH = {}
for _n, _c, _d in (
        ("Y", 1408, BF), ("CI", 512, I32), ("C", 1408, F32), ("LI", 1024, I32), ("L", 1152, F32), ("FW", 56, I32), ("FL", 88, U16),
        ("FR0", 1664, BF), ("FR1", 1664, BF), ("W", 1408, BF), ("TH8", 128, I32), ("THF", 128, F32), ("NEW", 512, BF),
        ("LAND", 1536, BF), ("FO", 88, F32), ("v16", 32, U16),
        ("abc", 384, U16), ("Lg", 2048, F16), ("xb", 2048, F32), ("y16", 2048, F16), ("yS", 2048, F32),
        ("dA", [8, 256], BF), ("own", 128, BF), ("nT", 128, F16), ("SA", 256, F32), ("SC", [4, 256], I32), ("low", 16, I32),
        ("po", 16, U16), ("RN", 16, BF), ("pd", 32, F32), ("pr", 384, F16), ("dq", 128, F16), ("sg", 128, F16),
        ("l16", 32, U16), ("vo16", 16, U16), ("er", 128, BF), ("hw", 256, BF), ("apr", [8, 18], F16), ("EQ", [8, 8, 18], BF),
        ("DD", 144, F16), ("DS", 144, F16), ("lo16", 8, U16), ("LE", 128, F32),
        ("um", 128, F32), ("wr", 128, F16), ("dl", 128, F32), ("af", 128, F16), ("al", 8, I32), ("mx", 16, I32),
        ("s2", 8, U16), ("thr0", 16, F32), ("ah", 1, F32),
        ("T1", 128, I32), ("T1a", 128, I32), ("TK", 32, I32), ("Q16", 88, I32), ("PI", 16, I32), ("JR", 128, BF),
        ("I", 128, F16), ("NI", 128, F16), ("I64", 128, F16), ("IH", 128, F16), ("M1", 2048, BF), ("M32", 32, BF),
        ("R", 512, F16), ("EE", [16, 144], F16), ("lh", 128, F32), ("BC", 16, BF), ("BO", 128, BF), ("Z", 576, BF), ("ZT", 144, F32),
        ("d0P", 64, F32), ("d0Q", 64, F32), ("d0R", 512, BF), ("d0D", 144, F16), ("half", 128, F32), ("POW", 128, F32),
        ("TM", [8, 18], F32), ("TM0", 128, F32), ("PC", 32, F32), ("SF", 64, F32), ("LH", 8, F16), ("CL", 34, U16), ("RB", 12, F32),
        ("wt", 32, F32), ("cst", 2, BF), ("C15", 128, BF), ("ODN", 128, F32)):
    SCRATCH[_n] = ("sbuf", [128] + (_c if isinstance(_c, list) else [_c]), _d)
for _n in ("psb0", "psb1", "psd0", "psd1", "psd2", "psd3", "psk", "psm"):
    SCRATCH[_n] = ("psum", [128, 512], F32)

SEMAPHORES = ["dv", "ac", "pe", "gp"] + ["in%d" % i for i in range(8)] + ["out%d" % i for i in range(6)] + \
             ["arr%d" % t for t in range(RO)] + ["snt%d" % t for t in range(RO)]


def rank_program(g, core, T, topo):
    rank = T.rank_of(core)
    if rank is None:
        return
    cores = T.cores
    add, sub, mul, mx, mn = AluOpType.add, AluOpType.subtract, AluOpType.mult, AluOpType.max, AluOpType.min
    ge, gt, le, eq = AluOpType.is_ge, AluOpType.is_gt, AluOpType.is_le, AluOpType.is_equal
    band, shr = AluOpType.bitwise_and, AluOpType.arith_shift_right
    AF = ActivationFunctionType
    queues = {"v": g.vector, "a": g.scalar, "p": g.tensor, "g": g, "s": g.sync}
    semof = {"v": "dv", "a": "ac", "p": "pe", "g": "gp"}
    count = {"dv": 0, "ac": 0, "pe": 0, "gp": 0}
    known = {"v": {}, "a": {}, "p": {}, "g": {}, "s": {}}
    log = {}
    total = {}
    lane = ["a"]

    def waits(e, reads, writes):
        need = {}
        for toks, wr in ((reads, False), (writes, True)):
            for nm, lo, hi in toks:
                ps = nm[:2] == "ps"
                for ent in log.get(nm, []):
                    if ps:
                        if ent[3] == e:
                            continue
                    elif ent[1] <= lo or ent[0] >= hi or not (wr or ent[2]):
                        continue
                    if ent[4] not in need or need[ent[4]][0] < ent[5]:
                        need[ent[4]] = (ent[5], ent[6])
        for sem in sorted(need, key=lambda s: -len(need[s][1])):
            val, clk = need[sem]
            k = known[e]
            if k.get(sem, 0) >= val:
                continue
            queues[e].wait_ge(T.sem[sem], val)
            k[sem] = val
            for s2 in clk:
                if k.get(s2, 0) < clk[s2]:
                    k[s2] = clk[s2]

    def note(e, clk, reads, writes, sem, val):
        for toks, wr in ((reads, False), (writes, True)):
            for nm, lo, hi in toks:
                ents = log.setdefault(nm, [])
                if nm[:2] == "ps":
                    ents[:] = []
                elif wr:
                    ents[:] = [x for x in ents if not (x[0] >= lo and x[1] <= hi)]
                ents.append((lo, hi, wr, e, sem, val, clk))

    def do(e, fn, ins, outs):
        reads = [tok for x in ins if isinstance(x, tuple) for tok in x[1] + x[2]] + [tok for x in outs for tok in x[2]]
        writes = [tok for x in outs for tok in x[1]]
        waits(e, reads, writes)
        sem = semof[e]
        count[sem] += 1
        fn().then_inc(T.sem[sem], 1)
        note(e, dict(known[e]), reads, writes, sem, count[sem])
        HOOK.append(("do", e, reads, writes))

    def dmas(e, pairs, reads, writes, sem):
        waits(e, reads, writes)
        for out, in_ in pairs:
            queues[e].dma_start(out=out, in_=in_).then_inc(T.sem[sem], 16)
        total[sem] = 16 * len(pairs)
        note("d", dict(known[e]), reads, writes, sem, total[sem])
        HOOK.append(("dma", e, reads, writes, len(pairs)))

    def dma(e, out, in_, reads, writes, sem):
        dmas(e, [(out, in_)], reads, writes, sem)

    def A(nm, lo=0, hi=None, st=1, parts=128):
        if hi is None:
            hi = SCRATCH[nm][1][1]
        elif nm[:2] == "FR":
            lo, hi = lo + 128, hi + 128
        ap = T[nm][0:parts, lo:hi] if st == 1 else T[nm][0:parts, lo:hi:st]
        return (ap, [(nm, lo, hi)], [])

    def A3(nm, ap, lo=0, hi=1 << 20):
        return (ap, [(nm, lo, hi)], [])

    def abc(j, lo=0, hi=128):
        return A("abc", 128 * j + lo, 128 * j + hi)

    def ind(win, off):
        return (win[0].indirect(off[0]), win[1], off[1])

    def val(z):
        return z[0] if isinstance(z, tuple) else z

    def vcopy(o, x):
        do("v", lambda: g.vector.tensor_copy(out=o[0], in_=x[0]), [x], [o])

    def vtt(o, x, y, op):
        do("v", lambda: g.vector.tensor_tensor(out=o[0], in0=x[0], in1=y[0], op=op), [x, y], [o])

    def vts(o, x, s1, op0, s2=None, op1=None):
        if op1 is None:
            do("v", lambda: g.vector.tensor_scalar(out=o[0], in0=x[0], scalar1=val(s1), scalar2=None, op0=op0), [x, s1], [o])
        else:
            do("v", lambda: g.vector.tensor_scalar(out=o[0], in0=x[0], scalar1=val(s1), scalar2=val(s2), op0=op0, op1=op1),
               [x, s1, s2], [o])

    def vscan(o, d0, d1, op0, op1, first=0.0):
        do("v", lambda: g.vector.tensor_tensor_scan(out=o[0], data0=d0[0], data1=d1[0], initial=val(first), op0=op0, op1=op1),
           [d0, d1, first], [o])

    def vset(o, c):
        do("v", lambda: g.vector.memset(o[0], c), [], [o])

    def gcopy(o, x):
        n = o[1][0][2] - o[1][0][1]
        do("g", lambda: g.affine_select(out=o[0], in_=x[0], pattern=[[0, n]], compare_op=ge, fill=0.0, base=0,
                                        channel_multiplier=0), [x], [o])

    def act(o, x, f=None, bias=None, scale=None):
        if f is None and lane[0] != "a":
            if bias is None and scale is None:
                return (vcopy if lane[0] == "v" else gcopy)(o, x)
            return vts(o, x, 1.0 if scale is None else scale, mul, 0.0 if bias is None else bias, add)
        kw = {}
        for key, z in (("bias", bias), ("scale", scale)):
            if z is not None:
                kw[key] = val(z)
        if f is None:
            f = AF.Identity if isinstance(bias, tuple) else AF.Copy
        do("a", lambda: g.scalar.activation(out=o[0], in_=x[0], func=f, **kw), [x, bias, scale], [o])

    def mms(bank, jobs, first=True, last=True):
        def fn():
            call = None
            for j, (o, l, r) in enumerate(jobs):
                call = g.tensor.matmul(out=o[0], lhsT=l[0], rhs=r[0], start=first and j == 0, stop=last and j == len(jobs) - 1)
            return call
        do("p", fn, [x for job in jobs for x in job[1:]], [A(bank)])

    def iota(o, pattern, base, cmul, flag=False):
        kw = {"allow_small_or_imprecise_dtypes": True} if flag else {}
        do("g", lambda: g.iota(o[0], pattern=pattern, base=base, channel_multiplier=cmul, **kw), [], [o])

    def fill(o, c):
        iota(o, [[0, o[1][0][2] - o[1][0][1]]], c, 0, True)

    def mark(o, pattern, base, c):
        do("g", lambda: g.affine_select(out=o[0], in_=o[0], pattern=pattern, compare_op=AluOpType.not_equal, fill=c, base=base,
                                        channel_multiplier=-1), [o], [o])

    def to_list(out, z, nm, lo, hi):
        return [(out, A("Z", 144 * z + 16 - r, 144 * z + 144 - r), A(nm, lo + r, hi, 16)) for r in range(16)]

    ONE, X32, FULL, BLOCK = range(4)

    def SF(j, n=1):
        return A("SF", j, j + n)
    RC, EV, OD, R1, R2, RF, R0, RH, RO2 = SF(0), SF(1), SF(2), SF(3), SF(4), SF(5), SF(36), SF(37), SF(38)
    LI, KQ, KP, IK, ODB = SF(8, 8), SF(16, 8), SF(40, 8), SF(24, 8), SF(32, 4)

    dma("a", T.FW[:, :], T.fw0[:, :], [], [("FW", 0, 56)], "in2")
    dma("s", T.CI[:, 0:128], T.cl[:, 0:128], [], [("CI", 0, 128)], "in1")
    dma("s", T.LI[:, :], T.lk[:, :], [], [("LI", 0, 1024)], "in0")
    dma("a", T.TH8[0:8, :], T.th[:, :], [], [("TH8", 0, 128)], "in5")
    dma("a", T.Y[:, 0:896], T.y0[:, :], [], [("Y", 0, 896)], "in3")

    def k_pick():
        mark(A3("EE", T.EE[:, :, 15:143:16]), [[1, 16], [16, 8]], 0, 4096.0)
        mark(A3("EE", T.EE[:, 0:11, 15:143:16]), [[1, 11], [16, 8]], 5, 1.0)
        mark(A3("EE", T.EE[:, 11:16, 15:143:16]), [[1, 5], [16, 8]], 0, 1.0)

    def k_diagonal():
        vts(A("T1a"), A("T1"), 15, band)
        vts(A("M1", 0, 128), A("T1a"), 0, eq)
        vcopy(SF(36, 3), A("M1", 0, 3))

    def k_parts():
        vts(R1, R0, -1.0, mul, 1.0, add)
        vtt(RF, R0, RH, add)
        vts(R2, R1, RH, sub, 4096.0, mul)
        vts(A("RB", 0, 11), A("Q16", 0, 88, 8), R1, mul)
        vts(A("RB", 4, 7), A("Q16", 32, 56, 8), RH, mul, R2, add)

    def k_numbers(nm, lo, hi):
        for b in range(lo, hi):
            act(A(nm, 128 * b, 128 * b + 128), A("JR"), scale=R0, bias=A("RB", b, b + 1))

    def k_places():
        vts(A("PI", 1, 2), A("PI", 0, 1), 15, band)
        vts(A("PI", 2, 3), A("PI", 0, 1), 1, band)
        vts(A("PI", 3, 4), A("PI", 0, 1), 7, band)
        vcopy(RC, A("PI", 1, 2))
        vcopy(OD, A("PI", 2, 3))
        vts(EV, A("PI", 2, 3), 0, eq)

    def k_groups():
        vts(A("al"), A("PI", 8, 16), 4, shr)
        vts(A("CL", 0, 32), A("Q16", 0, 32), 1.0 / 16, mul)
        vset(A("BC", 8, 16), 0.0)
        vts(A("BC", 0, 8), A("al"), 0, eq)

    def k_m32():
        vts(A("TK"), A("T1", 0, 32), 31, band)
        vts(A("M32"), A("TK"), 0, eq)

    def k_lanes():
        act(LI, A("Q16", 0, 8), bias=RC)
        act(A("v16", 0, 8), A("Q16", 0, 8), bias=RC)
        act(A("FL", 56, 88), A("Q16", 56, 88), bias=RC)

    def k_lanes2():
        act(KQ, LI, scale=16.0)
        act(KP, LI, scale=16.0, bias=30.0)
        act(A("PC", 0, 8), LI, scale=2.0, bias=896.0 + 4096)
        for o, c in ((A("PC", 8, 16), 1536.0), (A("PC", 24, 32), 1024.0), (IK, 4096.0), (A("LH"), 0.0)):
            act(o, LI, bias=c)

    def k_thresholds():
        act(A("THF", 0, 15, parts=8), A("TH8", 0, 15, parts=8), scale=32.0, bias=30.0 + LIFT)
        act(A("THF", 15, 128, parts=8), A("TH8", 15, 128, parts=8), scale=32.0, bias=30.0)
        mms("psk", [(A("psk", 0, 8), A("ZT", 16 - r, 144 - r, parts=8), A("THF", r, 128, 16, parts=8)) for r in range(16)])

    def k_limits():
        for j in range(2):
            act(A3("SC", T.SC[:, 2 * j, 127:240:16], 512 * j, 512 * j + 256), A("psk", 0, 8), bias=float(j))
        act(A("thr0"), A3("SC", T.SC[:, 0:3:2, 127:240:16], 0, 768), bias=240.0)

    def k_windows(which):
        for z, s in which:
            act(A("Z", 144 * z + 16, 144 * z + 144, 16), A("BC", 0, 8), scale=s)

    def k_steps():
        fill(A("d0P"), 1)
        fill(A("d0Q"), -1)

    def k_turn8():
        fill(A("ZT", parts=8), 0)
        mark(A("ZT", 16, 144, 16, parts=8), [[1, 8]], 0, 1.0)

    def k_rows():
        act(A("d0R", 0, 256), ind(A("M1", 0, 16), A("CL", 0, 16)))
        act(A("hw", 0, 16), A("M1", 15, 31), scale=LIFT)
        act(A("hw", 16, 32), A("M1", 0, 16), scale=-BIG)

    def k_rows2():
        vtt(A("d0R", 0, 256, 16), A("hw", 0, 16), A("hw", 16, 32), add)
        vts(A("d0R", 256, 512), A("d0R", 0, 256), -1.0, mul)

    def k_scans():
        vset(A("C15"), 15.0 / 512)
        vset(A("d0P", 0, 64, 16), -BIG)
        vset(A("d0Q", 0, 64, 16), BIG)
        vts(A("IH"), A("I"), 0.5, mul)

    def k_weights():
        vset(A("half"), 0.5)
        vset(A("d0D", 0, 144, 18), 0.0)
        vcopy(A("CL", 32, 33), A("PI", 3, 4))
        vscan(A("POW"), A("half"), A("TM0"), mul, add, 2.0 ** 65)
        vcopy(A("CL", 33, 34), A("PI", 1, 2))
        vts(A("TM0"), A("M1", 0, 128), -1e29, mul, 1e29, add)
        vtt(A("wt", 0, 16), A("POW", 64, 80), A("M1", 0, 16), mul)
        vts(A("half"), A("POW"), 80.0, mul)
        vscan(A("wt", 16, 32), A("d0D", 0, 16), A("wt", 0, 16), mul, add)
        vtt(A3("TM", T.TM[:, :, 0:16]), A("half"), A("TM0"), mx)
        vts(A("PC", 16, 24), A("POW", 0, 128, 16), A("wt", 31, 32), mul)

    def k_small():
        vset(A("cst"), -15.0 / 32)
        vts(A("NI"), A("I"), -32768.0, mul)
        vts(A("I64"), A("I"), 64.0, mul)
        vts(ODB, A("Q16", 56, 88, 8), OD, mul)

    def k_spare():
        vset(A3("apr", T.apr[:, :, 16:18]), -1.0)
        vset(A3("TM", T.TM[:, :, 16:18]), 1.0)
        act(A("d0D", 17, 144, 18), A("PC", 24, 32))

    def k_fills():
        fill(A("d0D"), 1)
        fill(A("TM0"), 0)

    def k_clusters():
        gcopy(A("C", 128, 512), A("CI", 128, 512))
        fill(A("C", 512, 896), 0)

    constants = {
        "g_m": lambda: iota(A("T1"), [[1, 128]], 128, -1),
        "g_p": lambda: iota(A("PI", 0, 1), [[0, 1]], 0, 1),
        "g_g": lambda: iota(A("PI", 8, 16), [[16, 8]], 15, -1),
        "g_q": lambda: iota(A("Q16"), [[16, 88]], 0, 0),
        "g_j": lambda: iota(A("JR"), [[1, 128]], 0, 0, True),
        "g_z": lambda: fill(A("Z"), 0),
        "k_zero": lambda: vset(A3("EE", T.EE[:, :, :]), 0.0),
        "k_unit": lambda: vts(A("I"), A("T1"), 128, eq),
        "k_atoms": lambda: act(abc(0), A("CI", 0, 128)),
        "k_list": lambda: act(A("FL", 0, 56), A("FW")),
        "k_spread": lambda: act(A("R"), ind(A("M32"), A("CL", 0, 32))),
        "k_block": lambda: act(A("BO"), ind(A("BC"), A("CL", 0, 8)), scale=32.0),
        "k_sums": lambda: k_windows(((ONE, 1.0), (X32, 32.0))),
        "k_turns": lambda: k_windows(((FULL, RF), (BLOCK, RO2))),
        "k_numbers": lambda: k_numbers("FR1", 0, 7),
        "k_links": lambda: act(A("L", 0, 1024), A("LI")),
        "k_forwards": lambda: act(A("FR0", 0, 896), ind(A("FR1", 0, 896), A("FL", 0, 56))),
        "k_odd": lambda: act(A("ODN"), A("JR"), scale=OD),
        "k_ones": lambda: dmas("s", [(T.M1[:, 128 * j:128 * j + 128], T.M1[:, 0:128]) for j in (1, 2, 3)],
                               [("M1", 0, 128), ("Y", 0, 896)], [("M1", 128, 512)], "in6"),
        "k_load": lambda: dma("s", T.CI[:, 128:512], T.cl[:, 128:512], [("Y", 0, 896)], [("CI", 128, 512)], "in4"),
        "k_ones2": lambda: dmas("s", [(T.M1[:, 512 * j:512 * j + 512], T.M1[:, 0:512]) for j in (1, 2, 3)],
                                [("M1", 0, 512)], [("M1", 512, 2048)], "in7"),
        "out_even": lambda: dma("s", T.lo[0:128:2, :], T.L[0:128:2, 0:1024], [("L", 0, 1024)], [], "out0"),
        "k_pick": k_pick, "k_diagonal": k_diagonal, "k_parts": k_parts, "k_places": k_places, "k_groups": k_groups,
        "k_m32": k_m32, "k_lanes": k_lanes, "k_lanes2": k_lanes2, "k_thresholds": k_thresholds, "k_steps": k_steps,
        "k_turn8": k_turn8, "k_limits": k_limits, "k_rows": k_rows, "k_rows2": k_rows2, "k_scans": k_scans,
        "k_weights": k_weights, "k_small": k_small, "k_spare": k_spare, "k_fills": k_fills, "k_clusters": k_clusters,
    }

    def one_round(t, FRc, FRn):
        first, last = t == 0, t == RO - 1
        made = 896 + 128 * t
        v, vn = A("v16", 8 * t, 8 * t + 8), A("v16", 8 * t + 8, 8 * t + 16) if not last else None
        own = A("own")
        a16, P, Q = abc(0), A("po", 0, 8), A("po", 8, 16)
        nw = A("NEW", 128 * t, 128 * t + 128)

        def rows_of(j0, j1):
            return A3("SC", T.SC[:, j0:j1 + 1:j1 - j0, 127:240:16], 256 * j0, 256 * j1 + 256)

        def link(n):
            q = QUARTERS[n]
            act(A("Lg", 512 * q, 512 * q + 512), ind(A("LI") if first else A("L", 0, 1024), abc(0, 32 * q, 32 * q + 32)))

        def lists(n):
            h = 1 - n
            mms("psb%d" % n, [(A("psb%d" % n, 0, 64), A3("EE", T.EE[:, k, 15 - k:143 - k]), A("Lg", 1024 * h + k, 1024 * h + 1024, 16))
                              for k in range(16)])

        def list_b(n):
            act(abc(1, 64 - 64 * n, 128 - 64 * n), A("psb%d" % n, 0, 64), scale=1.0 / 4096)

        def list_h(n):
            vts(A("lh", 64 * n, 64 * n + 64), A("psb%d" % n, 0, 64), unit(4096), add, unit(4096), sub)

        def list_c(n):
            vtt(abc(2, 64 - 64 * n, 128 - 64 * n), A("psb%d" % n, 0, 64), A("lh", 64 * n, 64 * n + 64), sub)

        def states(n):
            lo, hi = (0, 384, 768, made)[n:n + 2]
            act(A("W", lo, hi), ind(A("Y", 0, made), A("FL", lo // 16, hi // 16)))

        def own_in(n):
            bank, lo, k = PIECES[n]
            part = slice(32 * (lo // 512), 32 * (lo // 512) + 32)
            mms(bank, [(A(bank, 0, k), A3("nT", T.nT[part, :]), A3("R", T.R[part, lo % 512:lo % 512 + k]))], last=False)

        def fetch(n):
            lo, k = FETCH[n]
            act(A("xb", lo, lo + k), ind(A("W", 0, made), abc(1, lo // 16, (lo + k) // 16)), bias=2047.5)

        def blend(n):
            bank, lo, k = PIECES[n]
            hi = lo + k
            vtt(A("y16", lo, hi), ind(A("W", 0, made), abc(2, lo // 16, hi // 16)), A("xb", lo, hi), add)
            mms(bank, [(A(bank, 0, k), A("I"), A("y16", lo, hi))], first=False)

        def keep(n):
            lo, k = KEEP[n]
            act(A("yS", lo, lo + k), A("y16", lo, lo + k))

        def sizes(lo, hi):
            q = lo // 256
            return A3("dA", T.dA[:, q:hi // 256, :] if hi - lo >= 256 else T.dA[:, q, lo % 256:lo % 256 + hi - lo], lo, hi)

        def size(n):
            bank, lo, k = PIECES[n]
            act(sizes(lo, lo + k), A(bank, 0, k), AF.Abs, scale=0.5)

        def sums(n):
            bank, q0, q1 = SUMS[n]
            o = A(bank, 0, 16 * (q1 - q0))
            mms(bank, [(o, A("BO"), A("C15", 0, 16 * (q1 - q0)))] +
                [(o, A("Z", 144 * X32 + 16 - r, 144 * X32 + 144 - r),
                  A3("dA", T.dA[:, q0:q1, 16 * r:16 * r + 16], 256 * q0, 256 * q1)) for r in range(16)])

        def scan(n):
            bank, q0, q1 = SUMS[n]
            k = 16 * (q1 - q0)
            for j, d0, op in ((1, "d0P", mx), (3, "d0Q", mn)):
                o = A3("SC", T.SC[:, j, 112 + 16 * q0:112 + 16 * q1], 256 * j + 112 + 16 * q0, 256 * j + 112 + 16 * q1)
                vscan(o, A(d0, 0, k), A(bank, 0, k), add, op)

        def rows(n):
            o = A(ROWS[n], 0, 128)
            mms(ROWS[n], [(o, A("BO"), A("C15")), (o, A("BO"), sizes(128 * n, 128 * n + 128))])

        def scan_rows(n):
            for j, op in ((0, mx), (1, mn)):
                d0 = A("d0R", 256 * j + 128 * n, 256 * j + 128 * n + 128)
                if n:
                    vscan(A3("SC", T.SC[:, 2 * j + 1, 0:128], 512 * j + 256, 512 * j + 384), d0, A(ROWS[n], 0, 128), add, op,
                          A("SA", 128 * j + 127, 128 * j + 128))
                else:
                    vscan(A("SA", 128 * j, 128 * j + 128), d0, A(ROWS[n], 0, 128), add, op)

        def compose(lo, hi):
            if hi > lo:
                act(A(FRn, lo, hi), ind(A(FRc, 0, made), A("FL", lo // 16, hi // 16)))

        def states_sum():
            ps, o = A("psb1", 256, 257), A("psb1", 128, 256)
            mms("psb1", [(o, A("IH"), own)]
                + ([] if first else [(ps, A("BO"), A("RN", q, q + 1)) for q in range(8)] + [(ps, A("BO"), A("cst", 0, 1))]))

        def out_f():
            act(A("FO", 0, 80), A("psk", 0, 80))
            dma("a", T.fo[:, :], T.FO[:, :], [("FO", 0, 88)], [], "out3")

        def pick():
            vtt(A("pr", 0, 256), ind(A("M1"), A("po")), A("abc", 0, 256), mul)
            mms("psd0", to_list(A("psd0", 0, 16), ONE, "pr", 0, 256))

        def pick_b():
            vtt(A("pr", 256, 384), ind(A("M1"), P), abc(1), mul)
            mms("psd1", to_list(A("psd1", 0, 8), ONE, "pr", 256, 384))

        def row():
            mms("psd2", [(A("psd2", 0, 128), A("BO"), A("pr", 0, 128))])
            act(A3("apr", T.apr[:, :, 0:16]), A("psd2", 0, 128), scale=1.0 / 32)

        def wrap():
            o = A("psd3", 0, 128)
            mms("psd3", [(o, A("BO"), own), (o, A("I64"), A("af"))])
            act(A("wr"), o, scale=1.0 / 32768, bias=2049.0 + (2 * t + 3) / 1024)

        def delta():
            o = A("psd3", 0, 128)
            mms("psd3", [(o, A("BO"), own), (o, A("NI"), A("wr"))])
            act(A("dl"), o, scale=1.0 / 64, bias=1024.0 * 1025 + t + 1)

        def send():
            waits("g", nw[1], [])
            used, transfers = set(), []
            others = sorted([c for c in cores if c != core], key=lambda c: len(topo.engines(core, c)))
            for c in others:
                fewest = topo.engines(core, others[0])
                eng = [e for e in topo.engines(core, c) if e not in used]
                if len(topo.engines(core, c)) > len(fewest):
                    eng = [e for e in eng if e not in fewest]
                eng = eng[:4]
                used.update(eng)
                s = (rank - T.rank_of(c) - 1) % len(cores)
                rid, pid = topo.addr(c, core)
                transfers.append(RemoteDMATransfer(dst_ids=[DstId(rid=rid, pnc=pid)], dma_engine_mask=sum(1 << e for e in eng),
                                                   remote_sem=T.sem["arr%d" % t], src=nw[0],
                                                   dst=T.LAND[:, 384 * t + 128 * s:384 * t + 128 * s + 128]))
            g.remote_dma_fused(transfers, local_sem=T.sem["snt%d" % t])
            total["arr%d" % t] = 12
            total["snt%d" % t] = 12
            note("r", {}, [], [("LAND", 384 * t, 384 * t + 384)], "arr%d" % t, 12)
            HOOK.append(("rdma", "g", nw[1], [("LAND", 384 * t, 384 * t + 384)]))

        def equal():
            for q in range(8):
                vts(A3("EQ", T.EQ[:, q, q:8, :], q, q + 1), A3("apr", T.apr[:, q:8, :]), A("psd0", q, q + 1), eq,
                    A("pd", 16 + q, 17 + q), mul)
                if q % 4 == 3:
                    mms("psd3", [(A("psd3", 18 * j, 144), A("BO"), A3("EQ", T.EQ[:, j, j:8, :], j, j + 1)) for j in range(q - 3, q + 1)]
                        + [(A("psd3", 16, 144, 18), A("I64"), A("RN", 8, 16))] * (q == 3), first=q == 3, last=q == 7)

        steps = {
            "own": lambda: act(own, A("Y", 0, 128) if first else ind(A("Y", 0, made), v), scale=2.0),
            "turn": lambda: mms("psm", [(A("psm", 0, 128), own, A("I"))]),
            "nT": lambda: act(A("nT"), A("psm", 0, 128), scale=-1.0, bias=-2048.0),
            "Wlist": lambda: first or act(A("FL", 0, made // 16 - 8), A("psk", 0, made // 16 - 8)),
            "ghosts": lambda: first or act(A("Y", 512, 896), A("LAND", 384 * t - 384, 384 * t)),
            "count": lambda: first or vts(A("ah"), A("psb1", 256, 257), unit(512), add, unit(512), sub),
            "limit": lambda: first or vts(rows_of(0, 2), A("thr0"), A("psb1", 256, 257), add, A("ah"), sub),
            "sums": states_sum,
            "low": lambda: vts(A("low"), rows_of(1, 3), 31, band),
            "P": lambda: vtt(P, KP, A("low", 0, 8), sub),
            "Q": lambda: vtt(Q, KQ, A("low", 8, 16), add),
            "ref": lambda: vtt(A("RN"), rows_of(1, 2), rows_of(0, 1), gt),
            "products": lambda: vtt(A("pd"), ind(A("RN"), A("CL", 32, 34)), A("PC"), mul),
            "pick": pick,
            "row": row,
            "yq": lambda: vtt(A("dq"), ind(A("yS"), Q), own, sub),
            "sign": lambda: act(A("sg"), A("dq"), AF.Sign, bias=-2048.0),
            "moved": lambda: vtt(nw, A("sg"), A("psb1", 128, 256), add),
            "listed": lambda: act(A("l16", 0, 16), A("psd0", 0, 16)),
            "er": lambda: act(A("er"), ind(A(FRc, 0, made), A("l16", 8, 16))),
            "ai": lambda: act(A("mx", 8, 16), v, bias=128.0),
            "dummy": lambda: vtt(A("vo16", 8 * last, 16), A("mx", 8 * last, 16), A("pd", 8 * last, 16), mx),
            "send": send,
            "scatter_f": lambda: vcopy(ind(A(FRc), A("vo16", 8, 16)), A("er")),
            "turn_f": lambda: mms("psk", to_list(A("psk", 0, made // 16), FULL, FRc, 0, made)),
            "even": lambda: act(A("LE"), ind(A("L", 0, 1024), A("l16", 0, 8)), scale=EV, bias=SF(32 + t)),
            "compose_g": lambda: compose(512, 896),
            "list_f": lambda: act(A("FL", 0, made // 16), A("psk", 0, made // 16)),
            "equal": equal,
            "compose_b": lambda: compose(0, 512),
            "compose_r": lambda: compose(896, made),
            "flags": lambda: vtt(A("DD"), A("psd3", 0, 144), A3("TM", T.TM[:, :, :]), gt),
            "turn_n": lambda: mms("psk", to_list(A("psk", 0, made // 16), FULL, FRn, 0, made)),
            "room": lambda: act(A("Y", made, made + 128), ind(A("yS"), P), scale=0.5, bias=-1024.0),
            "first": lambda: vscan(A("DS"), A("d0D"), A("DD"), mul, mx),
            "lo": lambda: vtt(A("lo16"), A("psd0", 0, 8), A("DS", 17, 144, 18), mx),
            "state": lambda: vcopy(A("Y", 0, 128) if first else ind(A("Y", 0, made), v), nw),
            "scatter_l": lambda: vtt(ind(A("L"), A("lo16")), A("LE"), A("ODN"), add),
        }
        for j in range(6):
            for name, fn in (("link", link), ("lists", lists), ("b", list_b), ("h", list_h), ("c", list_c), ("in", own_in),
                             ("fetch", fetch), ("blend", blend), ("keep", keep), ("size", size), ("sum", sums), ("scan", scan),
                             ("rows", rows), ("srow", scan_rows), ("W", states)):
                steps[name + str(j)] = lambda fn=fn, j=j: fn(j)
        if not last:
            steps.update({
                "room_atoms": lambda: act(A("C", made, made + 128), a16),
                "room_f": lambda: k_numbers(FRn, 7 + t, 8 + t),
                "af": lambda: act(A("af"), a16),
                "al": lambda: vts(A("al"), A("mx", 8, 16), 511, band),
                "al2": lambda: vtt(A("mx", 0, 8), A("al"), IK, add),
                "next_room": lambda: first or act(A("PC", 0, 8), A("PC", 0, 8), bias=128.0),
                "wrap": wrap,
                "delta": delta,
                "um": lambda: vtt(A("um"), ind(A("M1"), P), A("dl"), mul),
                "scatter_c": lambda: vtt(A("C", 0, 128) if first else ind(A("C", 0, made), v), A("um"), A("C", made, made + 128), add),
                "pick_b": pick_b,
                "list_b": lambda: act(A("l16", 16, 24), A("psd1", 0, 8)),
                "h1_": lambda: act(A("hw", 0, 128), ind(A(FRc, 0, made), A("l16", 16, 24))),
                "turn_h": lambda: mms("psm", to_list(A("psm", 0, 8), FULL, "hw", 0, 128)),
                "list_h": lambda: act(A("l16", 24, 32), A("psm", 0, 8)),
                "h2_": lambda: act(A("hw", 128, 256), ind(A(FRc, 0, made), A("l16", 24, 32))),
                "hop": lambda: mms("psd1", [(A("psd1", 0, 8), A("I"), A("LH"))] + to_list(A("psd1", 0, 8), BLOCK, "hw", 128, 256)),
                "s2": lambda: vtt(A("s2"), A("vo16", 0, 8), A("psd1", 0, 8), sub),
                "v": lambda: vtt(vn, A("psd1", 0, 8), A("s2"), mn),
                "atoms": lambda: act(a16, ind(A("C", 0, made + 128), vn)),
            })
        else:
            steps.update({
                "out_base": lambda: dma("s", T.yo[:, 0:512], T.Y[:, 0:512], [("Y", 0, 512)], [], "out1"),
                "out_room": lambda: dma("s", T.yo[:, 896:1408], T.Y[:, 896:1408], [("Y", 896, 1408)], [], "out2"),
                "out_links": lambda: dma("s", T.lo[1:128:2, :], T.L[1:128:2, 0:1024], [("L", 0, 1024)], [], "out5"),
                "out_ghosts": lambda: dma("s", T.yo[:, 512:896], T.LAND[:, 384 * t:384 * t + 384], [("LAND", 384 * t, 384 * t + 384)],
                                          [], "out4"),
                "last_rooms": lambda: act(A("FO", 80, 88), LI, bias=1280.0),
                "out_f": out_f,
            })
        return steps

    rounds = [one_round(t, "FR%d" % (t % 2), "FR%d" % (1 - t % 2)) for t in range(RO)]
    for n, names in enumerate((START, FIRST, MIDDLE, MIDDLE, END)):
        for name in names:
            name, lane[0] = (name + "@a").split("@")[:2]
            steps = constants if name in constants else rounds[n - 1] if name in WRITES else rounds[n]
            if name in steps:
                HOOK.append(("step", n, name))
                steps[name]()
        HOOK.append(("step", -1, "end"))

    for sem in ("dv", "ac", "pe", "gp"):
        g.wait_ge(T.sem[sem], count[sem])
    for sem in sorted(total):
        g.wait_ge(T.sem[sem], total[sem])
